import numpy as np
import ml_dtypes


def mxq(x, axis, fmt="e4m3"):
    dtype, down = {"e4m3": (ml_dtypes.float8_e4m3fn, 7), "e5m2": (ml_dtypes.float8_e5m2, 14)}[fmt]
    v = np.moveaxis(np.asarray(x, np.float32).astype(ml_dtypes.bfloat16).astype(np.float64), axis, -1)
    blocks = v.reshape(v.shape[:-1] + (-1, 32))
    amax = np.abs(blocks).max(-1, keepdims=True)
    byte = np.maximum(np.where(amax > 0, np.frexp(amax)[1] - 1 + 127, 0) - down, 1)
    scale = np.exp2(byte - 127.0)
    codes = (blocks / scale).astype(np.float32).astype(dtype).astype(np.float64)
    return np.moveaxis((codes * scale).reshape(v.shape), -1, axis)


WIDE = False


def mx_kscale(k):
    if not WIDE:
        return np.ones(k)
    levels = np.array([10, -10, 5, -5, 0])
    if k % 512:
        return np.exp2(np.random.permutation(np.resize(levels, k // 32))).repeat(32)
    a = np.empty((k // 512, 16))
    for p in range(k // 512):
        a[p, :8] = np.random.permutation(np.resize(levels, 8))
        for g in range(8):
            far = levels[np.abs(levels - a[p, g]) >= 10]
            a[p, g + 8] = far[np.random.randint(len(far))]
    return np.exp2(a.ravel()).repeat(32)


def f64(x):
    return np.asarray(x).astype(np.float64)


def striped(idx):
    return np.tile(idx.reshape(-1, 16).T, (8, 1)).astype(np.uint16)


def unstriped(offs):
    return offs[:16].T.reshape(-1).astype(np.int64)


E2M1 = np.array([0.0, 0.5, 1.0, 1.5, 2.0, 3.0, 4.0, 6.0, -0.0, -0.5, -1.0, -1.5, -2.0, -3.0, -4.0, -6.0])


def pack_weight(w, fmt):
    k, n = w.shape
    w = f64(np.asarray(w, np.float32).astype(ml_dtypes.bfloat16)).reshape(k // 32, 32, n)
    amax = np.abs(w).max(1)
    if fmt == "e4m3":
        byte = np.frexp(amax)[1] - 1 + 127 - 7
    else:
        mant, ex = np.frexp(amax / 6.0)
        byte = np.where(mant > 0.5, ex, ex - 1) + 127
    byte = np.clip(np.where(amax > 0, byte, 1), 1, 254)
    scaled = (w * np.exp2(127.0 - byte)[:, None, :]).reshape(k, n).astype(np.float32)
    by_word = np.ascontiguousarray(scaled.reshape(k // 512, 128, 4, n).transpose(0, 1, 3, 2))
    if fmt == "e4m3":
        words = by_word.astype(ml_dtypes.float8_e4m3fn).view(np.uint8)
    else:
        c = by_word.astype(ml_dtypes.float4_e2m1fn).view(np.uint8) & 0xF
        words = (c[..., 0::2] | (c[..., 1::2] << 4)).reshape(k // 512, 128, 2 * n)
    return np.ascontiguousarray(words), np.ascontiguousarray(byte.astype(np.uint8).reshape(k // 512, 16, n))


def unpack_weight(words, scales, fmt):
    g, _, n = scales.shape
    words = np.ascontiguousarray(words).reshape(g, 128, n, -1)
    if fmt == "e4m3":
        vals = words.view(ml_dtypes.float8_e4m3fn).astype(np.float64)
    else:
        nib = np.empty((g, 128, n, 4), np.uint8)
        nib[..., 0::2] = words & 0xF
        nib[..., 1::2] = words >> 4
        vals = E2M1[nib]
    vals = vals * np.repeat(np.exp2(scales.astype(np.float64) - 127.0), 8, axis=1)[..., None]
    return vals.transpose(0, 1, 3, 2).reshape(g * 512, n)


def gelu(v):
    return 0.5 * v * (1.0 + np.tanh(np.sqrt(2.0 / np.pi) * (v + 0.044715 * v**3)))


def bf(x):
    return np.asarray(x, np.float32).astype(ml_dtypes.bfloat16)

def planes(Y):
    n, m = Y.shape
    b = f64(bf(Y)).reshape(n // 32, 32, m)
    amax = np.abs(b).max(1)
    byte = np.clip(np.where(amax > 0, np.frexp(amax)[1] - 1 + 127 - 7, 1), 1, 254)
    codes = (b * np.exp2(127.0 - byte)[:, None, :]).reshape(n, m).astype(np.float32).astype(ml_dtypes.float8_e4m3fn).view(np.uint8)
    words = codes.reshape(n // 512, 128, 4, m).transpose(0, 1, 3, 2)
    return np.ascontiguousarray(words), np.ascontiguousarray(byte.astype(np.uint8).reshape(n // 512, 16, m))


K, H, N, T, S = 1024, 512, 1024, 2048, 1024

def setup_inputs():
    n = np.random.standard_normal
    s = mx_kscale(K)[:, None]
    u = mx_kscale(H)[:, None]
    tab_words, tab_scales = pack_weight(n((K, T)) * s, "e4m3")
    offs = striped(np.random.permutation(T)[:S])
    common = 0.8 * n((K, H))
    wa = (common + 0.6 * n((K, H))) / np.sqrt(K) / s * u.T
    wb = (common + 0.6 * n((K, H))) / np.sqrt(K) / s * u.T
    wc = (common + 0.6 * n((K, H))) / np.sqrt(K) / s * u.T
    wb_words, wb_scales = pack_weight(wb, "e4m3")
    wc_words, wc_scales = pack_weight(wc, "e2m1")
    unit = np.exp(0.8 * n(N))
    we = n((H, N)) / np.sqrt(H) * unit[None, :] / u
    be = 0.4 * n(N) * unit
    return {"tab_words": tab_words, "tab_scales": tab_scales, "offs": offs,
            "wa": wa.astype(np.float32),
            "wb_words": wb_words, "wb_scales": wb_scales,
            "wc_words": wc_words, "wc_scales": wc_scales,
            "we": we.astype(np.float32), "be": be.astype(np.float32)}

def reference(tab_words, tab_scales, offs, wa, wb_words, wb_scales, wc_words, wc_scales, we, be):
    v = unpack_weight(tab_words, tab_scales, "e4m3")[:, unstriped(offs)]
    a = mxq(f64(wa), 0, "e4m3").T @ v
    b = unpack_weight(wb_words, wb_scales, "e4m3").T @ v
    c = unpack_weight(wc_words, wc_scales, "e2m1").T @ v
    h = np.maximum(np.minimum(a, b), np.minimum(np.maximum(a, b), c))
    y = (mxq(f64(we), 0, "e4m3").T @ mxq(h, 0, "e4m3")) + f64(be)[:, None]
    words, scales = planes(y)
    return y, words, scales

@@ -1,0 +1,256 @@
+from contextlib import ExitStack
+
+import concourse.mybir as mybir
+
+K, H, N, T, S = 1024, 512, 1024, 2048, 1024
+FLOPS = 2 * S * (3 * K * H + H * N)
+
+F32 = mybir.dt.float32
+BF16 = mybir.dt.bfloat16
+I32 = mybir.dt.int32
+U32 = mybir.dt.uint32
+U16 = mybir.dt.uint16
+U8 = mybir.dt.uint8
+FP8X4 = mybir.dt.float8_e4m3fn_x4
+FP4X4 = mybir.dt.float4_e2m1fn_x4
+MIN = mybir.AluOpType.min
+MAX = mybir.AluOpType.max
+MULT = mybir.AluOpType.mult
+IDENT = mybir.ActivationFunctionType.Identity
+
+P = 128
+CH = 128
+GROUPS = [256, 256, 256, 128, 128]
+FIRST = 256
+LEAD = 512
+
+
+def tile_list_triplex_median_vote_kernel(
+    tc, tab_words, tab_scales, offs, wa, wb_words, wb_scales, wc_words, wc_scales, we, be, out_0, out_1, out_2
+):
+    nc = tc.nc
+    with ExitStack() as ctx:
+        keep = ctx.enter_context(tc.tile_pool(name="keep", bufs=1))
+        ring = ctx.enter_context(tc.tile_pool(name="ring", bufs=2))
+        psum = ctx.enter_context(tc.psum_pool(name="psum", bufs=2))
+
+        offsets = keep.tile([P, S // 16], U16, name="offsets")
+        nc.sync.dma_start(offsets[:], offs)
+
+        tsc = keep.tile([P, T], U8, name="tsc", tag="tsc", align_bytes=64)
+        zero = keep.tile([P, 1], F32, name="zero")
+        nc.vector.memset(zero[:], 0.0)
+        warm = keep.tile([P, 1], F32, name="warm")
+        nc.scalar.activation(warm[:], zero[:], IDENT)
+        for q in range(4):
+            nc.vector.memset(tsc[32 * q : 32 * q + 24, :].bitcast(I32), 0)
+            nc.sync.dma_start(
+                tsc[32 * q + 24 : 32 * q + 32, :].bitcast(I32), tab_scales[:, 4 * q : 4 * q + 4, :].bitcast(I32)
+            )
+        wcs_raw = keep.tile([P, 2, H], U8, name="wcs_raw", tag="wcs_raw", align_bytes=64)
+        nc.gpsimd.memset(wcs_raw[:].bitcast(I32), 0)
+        wbs_raw = keep.tile([P, 2, H], U8, name="wbs_raw", tag="wbs_raw", align_bytes=64)
+        nc.vector.memset(wbs_raw[:].bitcast(I32), 0)
+        vscale = keep.tile([P, 2, S], U8, name="vscale", align_bytes=64)
+        nc.vector.memset(vscale[:].bitcast(I32), 0)
+
+        wb_raw = keep.tile([P, 2, H], I32, name="wb_raw", tag="wb_raw")
+        nc.sync.dma_start(wb_raw[:], wb_words.rearrange("a p e i -> p a (e i)").bitcast(I32))
+        wc_raw = keep.tile([P, 2, H // 2], I32, name="wc_raw", tag="wc_raw")
+        nc.sync.dma_start(wc_raw[:], wc_words.rearrange("a p b -> p a b").bitcast(I32))
+        tabw = []
+        for a in range(2):
+            tw = keep.tile([P, T], U32, name="tabw%d" % a, tag="tabw%d" % a, align_bytes=64)
+            nc.sync.dma_start(tw[:].bitcast(I32), tab_words[a].rearrange("p t i -> p (t i)").bitcast(I32))
+            tabw.append(tw)
+        for q in range(4):
+            nc.gpsimd.dma_start(
+                wcs_raw[32 * q : 32 * q + 4, :, :].bitcast(I32),
+                wc_scales[:, 4 * q : 4 * q + 4, :].rearrange("a r e -> r a e").bitcast(I32),
+            )
+            nc.scalar.dma_start(
+                wbs_raw[32 * q : 32 * q + 4, :, :].bitcast(I32),
+                wb_scales[:, 4 * q : 4 * q + 4, :].rearrange("a r e -> r a e").bitcast(I32),
+            )
+        bias = keep.tile([P, 2, 4], F32, name="bias")
+        nc.gpsimd.dma_start(bias[:], be.rearrange("(g p t) -> p g t", p=P, t=4))
+
+        vsc = keep.tile([P, S], U8, name="vsc", align_bytes=64)
+        nc.vector.tensor_copy(vsc[:], tsc[:].indirect(offsets[:]))
+        for a in range(2):
+            first = 24 + 4 * a
+            nc.scalar.dma_start(vscale[0 : P - first, a, :].bitcast(I32), vsc[first:P, :].bitcast(I32))
+
+        wb_p = keep.tile([P, 2, 4, P], I32, name="wb_p", tag="tsc", align_bytes=64)
+        nc.vector.tensor_copy(
+            wb_p[:].rearrange("p a t (q i) -> p a q t i", i=8), wb_raw[:].rearrange("p a (q t i) -> p a q t i", t=4, i=8)
+        )
+        wc_p = keep.tile([P, 2, 4, 2 * P], U8, name="wc_p", align_bytes=64)
+        nc.vector.tensor_copy(
+            wc_p[:].bitcast(I32).rearrange("p a t (q i) -> p a q t i", i=4),
+            wc_raw[:].rearrange("p a (q t i) -> p a q t i", t=4, i=4),
+        )
+        wa_raw = []
+        for a in range(2):
+            wr = keep.tile([P, 4, H], F32, name="wa_raw%d" % a, tag=("wb_raw", "wc_raw")[a])
+            nc.sync.dma_start(wr[:], wa[512 * a : 512 * (a + 1), :].rearrange("(p j) r -> p j r", j=4))
+            wa_raw.append(wr)
+
+        vw0 = keep.tile([P, S], U32, name="vw0", align_bytes=64)
+        nc.vector.tensor_copy(vw0[:], tabw[0][:].indirect(offsets[:]))
+        w_s = keep.tile([P, 2, 2, 4, P], U8, name="w_s", tag="tabw0", align_bytes=64)
+        wb_s, wc_s = w_s[:, 0], w_s[:, 1]
+        for dealt, raw in ((wb_s, wbs_raw), (wc_s, wcs_raw)):
+            nc.vector.tensor_copy(
+                dealt.bitcast(I32).rearrange("p a t (q i) -> p a q t i", i=2),
+                raw[:].bitcast(I32).rearrange("p a (q t i) -> p a q t i", t=4, i=2),
+            )
+        we_raw = keep.tile([P, 4, N], F32, name="we_raw", tag="wbs_raw", align_bytes=64)
+        we_rows = we.rearrange("(q s i) n -> s q i n", s=4, i=8)
+        for s in range(4):
+            nc.sync.dma_start(we_raw[:, s, :], we_rows[s])
+        vw1a = keep.tile([P, FIRST], U32, name="vw1a", align_bytes=64)
+        nc.vector.tensor_copy(vw1a[:], tabw[1][:].indirect(offsets[:, : FIRST // 16]))
+        vw1b = keep.tile([P, S - FIRST], U32, name="vw1b", align_bytes=64)
+        nc.vector.tensor_copy(vw1b[:], tabw[1][:].indirect(offsets[:, FIRST // 16 :]))
+
+        def picked(a, j):
+            if a == 0:
+                return vw0[:, j : j + CH]
+            return vw1a[:, j : j + CH] if j < FIRST else vw1b[:, j - FIRST : j - FIRST + CH]
+
+        wa_q = keep.tile([P, 2, 4, P], U32, name="wa_q", align_bytes=64)
+        wa_s = keep.tile([P, 2, 4, P], U8, name="wa_s", align_bytes=64)
+
+        def prepare_wa():
+            for a in range(2):
+                wa_bf = keep.tile([P, 4, P, 4], BF16, name="wa_bf%d" % a, align_bytes=64)
+                for t in range(4):
+                    nc.gpsimd.tensor_scalar(
+                        wa_bf[:, t, :, :].rearrange("p (q i) j -> p q i j", i=8),
+                        wa_raw[a][:].rearrange("p j (q t i) -> p t q i j", t=4, i=8)[:, t],
+                        1.0,
+                        1.0,
+                        MULT,
+                        MULT,
+                    )
+                nc.vector.quantize_mx(
+                    wa_q[:, a].rearrange("p t m -> p (t m)").bitcast(FP8X4),
+                    wa_s[:, a].rearrange("p t m -> p (t m)"),
+                    wa_bf[:].rearrange("p t m j -> p (t m j)"),
+                )
+
+        we_q = keep.tile([P, 2, 4, P], U32, name="we_q", align_bytes=64)
+        we_s = keep.tile([P, 2, 4, P], U8, name="we_s", align_bytes=64)
+
+        def prepare_we():
+            for g in range(2):
+                we_bf = keep.tile([P, 4, P, 4], BF16, name="we_bf%d" % g, align_bytes=64)
+                for m0 in range(0, P, 32):
+                    nc.scalar.copy(
+                        we_bf[:, :, m0 : m0 + 32, :].rearrange("p t m s -> p m s t"),
+                        we_raw[:, :, 512 * g + 4 * m0 : 512 * g + 4 * (m0 + 32)].rearrange("p s (m t) -> p m s t", t=4),
+                    )
+                nc.vector.quantize_mx(
+                    we_q[:, g].rearrange("p t m -> p (t m)").bitcast(FP8X4),
+                    we_s[:, g].rearrange("p t m -> p (t m)"),
+                    we_bf[:].rearrange("p t m j -> p (t m j)"),
+                )
+
+        def product(tag, codes, scales, j):
+            bank = psum.tile([P, 4, CH], F32, name=tag, tag=tag)
+            for t in range(4):
+                for a in range(2):
+                    nc.tensor.matmul_mx(
+                        bank[:, t, :],
+                        lhsT=codes(a, t),
+                        lhsT_scale=scales(a, t),
+                        rhs=picked(a, j).bitcast(FP8X4),
+                        rhs_scale=vscale[:, a, j : j + CH],
+                        start=(a == 0),
+                        stop=(a == 1),
+                    )
+            return bank[:].rearrange("p t j -> p j t")
+
+        y_s = keep.tile([P, 2, S], U8, name="y_s", align_bytes=64)
+        y_rows = out_0.rearrange("(g p t) j -> g p t j", p=P, t=4)
+        y_words = out_1.rearrange("g p m t -> p g (m t)").bitcast(I32)
+
+        lo = keep.tile([P, S, 4], F32, name="lo")
+        his = {}
+
+        def bounds(j):
+            b_ps = product("b", lambda a, t: wb_p[:, a, t, :].bitcast(FP8X4), lambda a, t: wb_s[:, a, t, :], j)
+            c_ps = product("c", lambda a, t: wc_p[:, a, t, :].bitcast(FP4X4), lambda a, t: wc_s[:, a, t, :], j)
+            b_sb = ring.tile([P, CH, 4], F32, name="b_sb", tag="b_sb", bufs=2)
+            nc.scalar.copy(b_sb[:], b_ps)
+            hi = ring.tile([P, CH, 4], F32, name="hi", tag="hi", bufs=5)
+            nc.vector.tensor_tensor(lo[:, j : j + CH, :], b_sb[:], c_ps, MIN)
+            nc.vector.tensor_tensor(hi[:], b_sb[:], c_ps, MAX)
+            his[j] = hi
+
+        def vote(j0, w):
+            mid = ring.tile([P, w, 4], F32, name="mid", tag="mid", bufs=2)
+            for c in range(0, w, CH):
+                a_ps = product("a", lambda a, t: wa_q[:, a, t, :].bitcast(FP8X4), lambda a, t: wa_s[:, a, t, :], j0 + c)
+                nc.vector.tensor_tensor(mid[:, c : c + CH, :], his[j0 + c][:], a_ps, MIN)
+            h_bf = ring.tile([P, w, 4], BF16, name="h_bf", tag="h_bf", align_bytes=64)
+            nc.vector.tensor_tensor(h_bf[:], lo[:, j0 : j0 + w, :], mid[:], MAX)
+            h_q = ring.tile([P, w], U32, name="h_q", tag="h_q", align_bytes=64)
+            h_s = ring.tile([P, w], U8, name="h_s", tag="h_s", align_bytes=64)
+            nc.vector.quantize_mx(h_q[:].bitcast(FP8X4), h_s[:], h_bf[:].rearrange("p j t -> p (j t)"))
+            return h_q, h_s
+
+        def estimate(j0, w, h_q, h_s):
+            y_q = ring.tile([P, 2, w], U32, name="y_q", tag="y_q", align_bytes=64, bufs=3)
+            for g in range(2):
+                y = ring.tile([P, 4, w], F32, name="y", tag="y", bufs=4)
+                per_bank = 512 // w
+                for t0 in range(0, 4, per_bank):
+                    bank = psum.tile([P, per_bank, w], F32, name="ybank", tag="ybank")
+                    for u in range(per_bank):
+                        nc.tensor.matmul_mx(
+                            bank[:, u, :],
+                            lhsT=we_q[:, g, t0 + u, :].bitcast(FP8X4),
+                            lhsT_scale=we_s[:, g, t0 + u, :],
+                            rhs=h_q[:].bitcast(FP8X4),
+                            rhs_scale=h_s[:],
+                            start=True,
+                            stop=True,
+                        )
+                    for u in range(per_bank):
+                        nc.scalar.activation(y[:, t0 + u, :], bank[:, u, :], IDENT, bias=bias[:, g, t0 + u : t0 + u + 1])
+                nc.sync.dma_start(y_rows[g][:, :, j0 : j0 + w], y[:])
+                y_bf = ring.tile([P, w, 4], BF16, name="y_bf", tag="y_bf", align_bytes=64, bufs=3)
+                dst = y_bf[:].rearrange("p (c i) t -> p c t i", i=4)
+                src = y[:].rearrange("p t (c i) -> p c t i", i=4)
+                if g == 0:
+                    nc.scalar.copy(dst, src)
+                elif j0 < 768:
+                    nc.gpsimd.tensor_scalar(y_bf[:], y[:].rearrange("p t j -> p j t"), 1.0, 1.0, MULT, MULT)
+                else:
+                    nc.vector.tensor_copy(dst, src)
+                nc.vector.quantize_mx(
+                    y_q[:, g, :].bitcast(FP8X4), y_s[:, g, j0 : j0 + w], y_bf[:].rearrange("p j t -> p (j t)")
+                )
+            nc.sync.dma_start(y_words[:, :, j0 : j0 + w], y_q[:].bitcast(I32))
+
+        starts = [sum(GROUPS[:i]) for i in range(len(GROUPS))]
+        for j in range(0, LEAD, CH):
+            bounds(j)
+        prepare_wa()
+        prepare_we()
+        voted = None
+        for i in range(len(GROUPS)):
+            ahead = vote(starts[i], GROUPS[i])
+            for j in range(LEAD + starts[i], min(S, LEAD + starts[i] + GROUPS[i]), CH):
+                bounds(j)
+            if voted is not None:
+                estimate(starts[i - 1], GROUPS[i - 1], *voted)
+            voted = ahead
+        estimate(starts[-1], GROUPS[-1], *voted)
+        for q in range(4):
+            nc.scalar.dma_start(
+                out_2[:, 4 * q : 4 * q + 4, :].rearrange("g r m -> r g m").bitcast(I32),
+                y_s[32 * q : 32 * q + 4, :, :].bitcast(I32),
+            )

@@ -15,6 +15,7 @@ FP8X4 = mybir.dt.float8_e4m3fn_x4
 FP4X4 = mybir.dt.float4_e2m1fn_x4
 MIN = mybir.AluOpType.min
 MAX = mybir.AluOpType.max
+ADD = mybir.AluOpType.add
 MULT = mybir.AluOpType.mult
 IDENT = mybir.ActivationFunctionType.Identity
 
@@ -37,51 +38,64 @@ def tile_list_triplex_median_vote_kernel(
         offsets = keep.tile([P, S // 16], U16, name="offsets")
         nc.sync.dma_start(offsets[:], offs)
 
-        tsc = keep.tile([P, T], U8, name="tsc", tag="tsc", align_bytes=64)
+        wbs_raw = keep.tile([P, 2, H], U8, name="wbs_raw", align_bytes=64)
+        nc.vector.memset(wbs_raw[:].bitcast(I32), 0)
+        wcs_raw = keep.tile([P, 2, H], U8, name="wcs_raw", align_bytes=64)
+        nc.gpsimd.memset(wcs_raw[:].bitcast(I32), 0)
         zero = keep.tile([P, 1], F32, name="zero")
         nc.vector.memset(zero[:], 0.0)
         warm = keep.tile([P, 1], F32, name="warm")
         nc.scalar.activation(warm[:], zero[:], IDENT)
+        tsc = keep.tile([P, T], U8, name="tsc", align_bytes=64)
         for q in range(4):
             nc.vector.memset(tsc[32 * q : 32 * q + 24, :].bitcast(I32), 0)
             nc.sync.dma_start(
                 tsc[32 * q + 24 : 32 * q + 32, :].bitcast(I32), tab_scales[:, 4 * q : 4 * q + 4, :].bitcast(I32)
             )
-        wcs_raw = keep.tile([P, 2, H], U8, name="wcs_raw", tag="wcs_raw", align_bytes=64)
-        nc.gpsimd.memset(wcs_raw[:].bitcast(I32), 0)
-        wbs_raw = keep.tile([P, 2, H], U8, name="wbs_raw", tag="wbs_raw", align_bytes=64)
-        nc.vector.memset(wbs_raw[:].bitcast(I32), 0)
         vscale = keep.tile([P, 2, S], U8, name="vscale", align_bytes=64)
         nc.vector.memset(vscale[:].bitcast(I32), 0)
 
-        wb_raw = keep.tile([P, 2, H], I32, name="wb_raw", tag="wb_raw")
+        tabw = [keep.tile([P, T], U32, name="tabw%d" % a, tag="tabw%d" % a, align_bytes=64) for a in range(2)]
+        tab_rows = tab_words.rearrange("a p t i -> a p (t i)").bitcast(I32)
+        nc.sync.dma_start(tabw[0][:].bitcast(I32), tab_rows[0])
+        wb_raw = keep.tile([P, 2, H], I32, name="wb_raw")
         nc.sync.dma_start(wb_raw[:], wb_words.rearrange("a p e i -> p a (e i)").bitcast(I32))
-        wc_raw = keep.tile([P, 2, H // 2], I32, name="wc_raw", tag="wc_raw")
+        wc_raw = keep.tile([P, 2, H // 2], I32, name="wc_raw")
         nc.sync.dma_start(wc_raw[:], wc_words.rearrange("a p b -> p a b").bitcast(I32))
-        tabw = []
-        for a in range(2):
-            tw = keep.tile([P, T], U32, name="tabw%d" % a, tag="tabw%d" % a, align_bytes=64)
-            nc.sync.dma_start(tw[:].bitcast(I32), tab_words[a].rearrange("p t i -> p (t i)").bitcast(I32))
-            tabw.append(tw)
         for q in range(4):
+            nc.sync.dma_start(
+                wbs_raw[32 * q : 32 * q + 4, :, :].bitcast(I32),
+                wb_scales[:, 4 * q : 4 * q + 4, :].rearrange("a r e -> r a e").bitcast(I32),
+            )
             nc.gpsimd.dma_start(
                 wcs_raw[32 * q : 32 * q + 4, :, :].bitcast(I32),
                 wc_scales[:, 4 * q : 4 * q + 4, :].rearrange("a r e -> r a e").bitcast(I32),
             )
-            nc.scalar.dma_start(
-                wbs_raw[32 * q : 32 * q + 4, :, :].bitcast(I32),
-                wb_scales[:, 4 * q : 4 * q + 4, :].rearrange("a r e -> r a e").bitcast(I32),
-            )
+        nc.sync.dma_start(tabw[1][:].bitcast(I32), tab_rows[1])
         bias = keep.tile([P, 2, 4], F32, name="bias")
         nc.gpsimd.dma_start(bias[:], be.rearrange("(g p t) -> p g t", p=P, t=4))
+        wa_raw = []
+        for a in range(2):
+            wr = keep.tile([P, 4, H], F32, name="wa_raw%d" % a)
+            nc.sync.dma_start(wr[:], wa[512 * a : 512 * (a + 1), :].rearrange("(p j) r -> p j r", j=4))
+            wa_raw.append(wr)
+        we_raw = []
+        we_rows = we.rearrange("(q s i) (g n) -> g s q i n", s=4, i=8, g=2)
+        for g in range(2):
+            wr = keep.tile([P, 4, 512], F32, name="we_raw%d" % g)
+            for s in range(4):
+                nc.sync.dma_start(wr[:, s, :], we_rows[g, s])
+            we_raw.append(wr)
 
         vsc = keep.tile([P, S], U8, name="vsc", align_bytes=64)
         nc.vector.tensor_copy(vsc[:], tsc[:].indirect(offsets[:]))
         for a in range(2):
             first = 24 + 4 * a
-            nc.scalar.dma_start(vscale[0 : P - first, a, :].bitcast(I32), vsc[first:P, :].bitcast(I32))
+            nc.gpsimd.dma_start(vscale[0 : P - first, a, :].bitcast(I32), vsc[first:P, :].bitcast(I32))
+        vw0 = keep.tile([P, S], U32, name="vw0", align_bytes=64)
+        nc.vector.tensor_copy(vw0[:], tabw[0][:].indirect(offsets[:]))
 
-        wb_p = keep.tile([P, 2, 4, P], I32, name="wb_p", tag="tsc", align_bytes=64)
+        wb_p = keep.tile([P, 2, 4, P], I32, name="wb_p", tag="tabw0", align_bytes=64)
         nc.vector.tensor_copy(
             wb_p[:].rearrange("p a t (q i) -> p a q t i", i=8), wb_raw[:].rearrange("p a (q t i) -> p a q t i", t=4, i=8)
         )
@@ -90,25 +104,13 @@ def tile_list_triplex_median_vote_kernel(
             wc_p[:].bitcast(I32).rearrange("p a t (q i) -> p a q t i", i=4),
             wc_raw[:].rearrange("p a (q t i) -> p a q t i", t=4, i=4),
         )
-        wa_raw = []
-        for a in range(2):
-            wr = keep.tile([P, 4, H], F32, name="wa_raw%d" % a, tag=("wb_raw", "wc_raw")[a])
-            nc.sync.dma_start(wr[:], wa[512 * a : 512 * (a + 1), :].rearrange("(p j) r -> p j r", j=4))
-            wa_raw.append(wr)
-
-        vw0 = keep.tile([P, S], U32, name="vw0", align_bytes=64)
-        nc.vector.tensor_copy(vw0[:], tabw[0][:].indirect(offsets[:]))
-        w_s = keep.tile([P, 2, 2, 4, P], U8, name="w_s", tag="tabw0", align_bytes=64)
-        wb_s, wc_s = w_s[:, 0], w_s[:, 1]
+        wb_s = keep.tile([P, 2, 4, P], U8, name="wb_s", align_bytes=64)
+        wc_s = keep.tile([P, 2, 4, P], U8, name="wc_s", align_bytes=64)
         for dealt, raw in ((wb_s, wbs_raw), (wc_s, wcs_raw)):
             nc.vector.tensor_copy(
-                dealt.bitcast(I32).rearrange("p a t (q i) -> p a q t i", i=2),
+                dealt[:].bitcast(I32).rearrange("p a t (q i) -> p a q t i", i=2),
                 raw[:].bitcast(I32).rearrange("p a (q t i) -> p a q t i", t=4, i=2),
             )
-        we_raw = keep.tile([P, 4, N], F32, name="we_raw", tag="wbs_raw", align_bytes=64)
-        we_rows = we.rearrange("(q s i) n -> s q i n", s=4, i=8)
-        for s in range(4):
-            nc.sync.dma_start(we_raw[:, s, :], we_rows[s])
         vw1a = keep.tile([P, FIRST], U32, name="vw1a", align_bytes=64)
         nc.vector.tensor_copy(vw1a[:], tabw[1][:].indirect(offsets[:, : FIRST // 16]))
         vw1b = keep.tile([P, S - FIRST], U32, name="vw1b", align_bytes=64)
@@ -126,14 +128,20 @@ def tile_list_triplex_median_vote_kernel(
             for a in range(2):
                 wa_bf = keep.tile([P, 4, P, 4], BF16, name="wa_bf%d" % a, align_bytes=64)
                 for t in range(4):
-                    nc.gpsimd.tensor_scalar(
-                        wa_bf[:, t, :, :].rearrange("p (q i) j -> p q i j", i=8),
-                        wa_raw[a][:].rearrange("p j (q t i) -> p t q i j", t=4, i=8)[:, t],
-                        1.0,
-                        1.0,
-                        MULT,
-                        MULT,
-                    )
+                    if a == 1 and t >= 3:
+                        nc.scalar.copy(
+                            wa_bf[:, t, :, :].rearrange("p (q i) j -> p q j i", i=8),
+                            wa_raw[a][:].rearrange("p j (q t i) -> p t q j i", t=4, i=8)[:, t],
+                        )
+                    else:
+                        nc.gpsimd.tensor_scalar(
+                            wa_bf[:, t, :, :].rearrange("p (q i) j -> p q i j", i=8),
+                            wa_raw[a][:].rearrange("p j (q t i) -> p t q i j", t=4, i=8)[:, t],
+                            1.0,
+                            1.0,
+                            MULT,
+                            MULT,
+                        )
                 nc.vector.quantize_mx(
                     wa_q[:, a].rearrange("p t m -> p (t m)").bitcast(FP8X4),
                     wa_s[:, a].rearrange("p t m -> p (t m)"),
@@ -143,19 +151,17 @@ def tile_list_triplex_median_vote_kernel(
         we_q = keep.tile([P, 2, 4, P], U32, name="we_q", align_bytes=64)
         we_s = keep.tile([P, 2, 4, P], U8, name="we_s", align_bytes=64)
 
-        def prepare_we():
-            for g in range(2):
-                we_bf = keep.tile([P, 4, P, 4], BF16, name="we_bf%d" % g, align_bytes=64)
-                for m0 in range(0, P, 32):
-                    nc.scalar.copy(
-                        we_bf[:, :, m0 : m0 + 32, :].rearrange("p t m s -> p m s t"),
-                        we_raw[:, :, 512 * g + 4 * m0 : 512 * g + 4 * (m0 + 32)].rearrange("p s (m t) -> p m s t", t=4),
-                    )
-                nc.vector.quantize_mx(
-                    we_q[:, g].rearrange("p t m -> p (t m)").bitcast(FP8X4),
-                    we_s[:, g].rearrange("p t m -> p (t m)"),
-                    we_bf[:].rearrange("p t m j -> p (t m j)"),
-                )
+        def prepare_we(g):
+            we_bf = keep.tile([P, 4, P, 4], BF16, name="we_bf%d" % g, tag="we_bf%d" % g, align_bytes=64)
+            for m0 in range(0, P, 32):
+                dst = we_bf[:, :, m0 : m0 + 32, :].rearrange("p t m s -> p m s t")
+                src = we_raw[g][:, :, 4 * m0 : 4 * (m0 + 32)].rearrange("p s (m t) -> p m s t", t=4)
+                nc.scalar.copy(dst, src)
+            nc.vector.quantize_mx(
+                we_q[:, g].rearrange("p t m -> p (t m)").bitcast(FP8X4),
+                we_s[:, g].rearrange("p t m -> p (t m)"),
+                we_bf[:].rearrange("p t m j -> p (t m j)"),
+            )
 
         def product(tag, codes, scales, j):
             bank = psum.tile([P, 4, CH], F32, name=tag, tag=tag)
@@ -176,7 +182,8 @@ def tile_list_triplex_median_vote_kernel(
         y_rows = out_0.rearrange("(g p t) j -> g p t j", p=P, t=4)
         y_words = out_1.rearrange("g p m t -> p g (m t)").bitcast(I32)
 
-        lo = keep.tile([P, S, 4], F32, name="lo")
+        starts = [sum(GROUPS[:i]) for i in range(len(GROUPS))]
+        los = {}
         his = {}
 
         def bounds(j):
@@ -184,18 +191,24 @@ def tile_list_triplex_median_vote_kernel(
             c_ps = product("c", lambda a, t: wc_p[:, a, t, :].bitcast(FP4X4), lambda a, t: wc_s[:, a, t, :], j)
             b_sb = ring.tile([P, CH, 4], F32, name="b_sb", tag="b_sb", bufs=2)
             nc.scalar.copy(b_sb[:], b_ps)
-            hi = ring.tile([P, CH, 4], F32, name="hi", tag="hi", bufs=5)
-            nc.vector.tensor_tensor(lo[:, j : j + CH, :], b_sb[:], c_ps, MIN)
+            hi = ring.tile([P, CH, 4], F32, name="hi", tag="hi", bufs=4)
+            if j in starts:
+                w = GROUPS[starts.index(j)]
+                lo = keep.tile([P, w, 4], F32, name="lo%d" % j, tag="we_bf1" if j == 512 else "lo%d" % j, align_bytes=64)
+                for c in range(0, w, CH):
+                    los[j + c] = (lo, c)
+            lo, c = los[j]
+            nc.vector.tensor_tensor(lo[:, c : c + CH, :], b_sb[:], c_ps, MIN)
             nc.vector.tensor_tensor(hi[:], b_sb[:], c_ps, MAX)
             his[j] = hi
 
         def vote(j0, w):
-            mid = ring.tile([P, w, 4], F32, name="mid", tag="mid", bufs=2)
+            mid = keep.tile([P, w, 4], F32, name="mid%d" % j0, tag="we_bf0" if j0 == 256 else "mid%d" % j0, align_bytes=64)
             for c in range(0, w, CH):
                 a_ps = product("a", lambda a, t: wa_q[:, a, t, :].bitcast(FP8X4), lambda a, t: wa_s[:, a, t, :], j0 + c)
                 nc.vector.tensor_tensor(mid[:, c : c + CH, :], his[j0 + c][:], a_ps, MIN)
             h_bf = ring.tile([P, w, 4], BF16, name="h_bf", tag="h_bf", align_bytes=64)
-            nc.vector.tensor_tensor(h_bf[:], lo[:, j0 : j0 + w, :], mid[:], MAX)
+            nc.vector.tensor_tensor(h_bf[:], los[j0][0][:], mid[:], MAX)
             h_q = ring.tile([P, w], U32, name="h_q", tag="h_q", align_bytes=64)
             h_s = ring.tile([P, w], U8, name="h_s", tag="h_s", align_bytes=64)
             nc.vector.quantize_mx(h_q[:].bitcast(FP8X4), h_s[:], h_bf[:].rearrange("p j t -> p (j t)"))
@@ -219,14 +232,18 @@ def tile_list_triplex_median_vote_kernel(
                             stop=True,
                         )
                     for u in range(per_bank):
-                        nc.scalar.activation(y[:, t0 + u, :], bank[:, u, :], IDENT, bias=bias[:, g, t0 + u : t0 + u + 1])
+                        column = bias[:, g, t0 + u : t0 + u + 1]
+                        if g == 1 and j0 + w == S:
+                            nc.vector.tensor_scalar(y[:, t0 + u, :], bank[:, u, :], column, None, ADD)
+                        else:
+                            nc.scalar.activation(y[:, t0 + u, :], bank[:, u, :], IDENT, bias=column)
                 nc.sync.dma_start(y_rows[g][:, :, j0 : j0 + w], y[:])
                 y_bf = ring.tile([P, w, 4], BF16, name="y_bf", tag="y_bf", align_bytes=64, bufs=3)
                 dst = y_bf[:].rearrange("p (c i) t -> p c t i", i=4)
                 src = y[:].rearrange("p t (c i) -> p c t i", i=4)
                 if g == 0:
                     nc.scalar.copy(dst, src)
-                elif j0 < 768:
+                elif j0 + w < S:
                     nc.gpsimd.tensor_scalar(y_bf[:], y[:].rearrange("p t j -> p j t"), 1.0, 1.0, MULT, MULT)
                 else:
                     nc.vector.tensor_copy(dst, src)
@@ -235,22 +252,19 @@ def tile_list_triplex_median_vote_kernel(
                 )
             nc.sync.dma_start(y_words[:, :, j0 : j0 + w], y_q[:].bitcast(I32))
 
-        starts = [sum(GROUPS[:i]) for i in range(len(GROUPS))]
         for j in range(0, LEAD, CH):
             bounds(j)
         prepare_wa()
-        prepare_we()
-        voted = None
         for i in range(len(GROUPS)):
-            ahead = vote(starts[i], GROUPS[i])
+            voted = vote(starts[i], GROUPS[i])
+            if i == 0:
+                prepare_we(0)
+                prepare_we(1)
+            estimate(starts[i], GROUPS[i], *voted)
             for j in range(LEAD + starts[i], min(S, LEAD + starts[i] + GROUPS[i]), CH):
                 bounds(j)
-            if voted is not None:
-                estimate(starts[i - 1], GROUPS[i - 1], *voted)
-            voted = ahead
-        estimate(starts[-1], GROUPS[-1], *voted)
         for q in range(4):
-            nc.scalar.dma_start(
+            (nc.scalar if q % 2 else nc.sync).dma_start(
                 out_2[:, 4 * q : 4 * q + 4, :].rearrange("g r m -> r g m").bitcast(I32),
                 y_s[32 * q : 32 * q + 4, :, :].bitcast(I32),
             )

@@ -38,60 +38,49 @@ def tile_list_triplex_median_vote_kernel(
         offsets = keep.tile([P, S // 16], U16, name="offsets")
         nc.sync.dma_start(offsets[:], offs)
 
-        wbs_raw = keep.tile([P, 2, H], U8, name="wbs_raw", align_bytes=64)
-        nc.vector.memset(wbs_raw[:].bitcast(I32), 0)
-        wcs_raw = keep.tile([P, 2, H], U8, name="wcs_raw", align_bytes=64)
-        nc.gpsimd.memset(wcs_raw[:].bitcast(I32), 0)
+        w_sraw = []
+        for name in ("wbs_raw", "wcs_raw"):
+            raw = keep.tile([P, 2, H], U8, name=name, tag=name, align_bytes=64)
+            (nc.vector if name == "wbs_raw" else nc.gpsimd).memset(raw[:].bitcast(I32), 0)
+            w_sraw.append(raw)
+        wbs_raw, wcs_raw = w_sraw
         zero = keep.tile([P, 1], F32, name="zero")
         nc.vector.memset(zero[:], 0.0)
         warm = keep.tile([P, 1], F32, name="warm")
         nc.scalar.activation(warm[:], zero[:], IDENT)
-        tsc = keep.tile([P, T], U8, name="tsc", align_bytes=64)
+        tsc = keep.tile([P, T], U8, name="tsc", tag="tsc", align_bytes=64)
         for q in range(4):
             nc.vector.memset(tsc[32 * q : 32 * q + 24, :].bitcast(I32), 0)
             nc.sync.dma_start(
                 tsc[32 * q + 24 : 32 * q + 32, :].bitcast(I32), tab_scales[:, 4 * q : 4 * q + 4, :].bitcast(I32)
             )
         vscale = keep.tile([P, 2, S], U8, name="vscale", align_bytes=64)
-        nc.vector.memset(vscale[:].bitcast(I32), 0)
+        nc.gpsimd.memset(vscale[:].bitcast(I32), 0)
+
+        def load_scale_rows(raw, scales, q):
+            nc.sync.dma_start(
+                raw[32 * q : 32 * q + 4, :, :].bitcast(I32),
+                scales[:, 4 * q : 4 * q + 4, :].rearrange("a r e -> r a e").bitcast(I32),
+            )
 
         tabw = [keep.tile([P, T], U32, name="tabw%d" % a, tag="tabw%d" % a, align_bytes=64) for a in range(2)]
         tab_rows = tab_words.rearrange("a p t i -> a p (t i)").bitcast(I32)
         nc.sync.dma_start(tabw[0][:].bitcast(I32), tab_rows[0])
-        wb_raw = keep.tile([P, 2, H], I32, name="wb_raw")
+        wb_raw = keep.tile([P, 2, H], I32, name="wb_raw", tag="wb_raw", align_bytes=64)
         nc.sync.dma_start(wb_raw[:], wb_words.rearrange("a p e i -> p a (e i)").bitcast(I32))
-        wc_raw = keep.tile([P, 2, H // 2], I32, name="wc_raw")
+        wc_raw = keep.tile([P, 2, H // 2], I32, name="wc_raw", tag="wc_raw", align_bytes=64)
         nc.sync.dma_start(wc_raw[:], wc_words.rearrange("a p b -> p a b").bitcast(I32))
         for q in range(4):
-            nc.sync.dma_start(
-                wbs_raw[32 * q : 32 * q + 4, :, :].bitcast(I32),
-                wb_scales[:, 4 * q : 4 * q + 4, :].rearrange("a r e -> r a e").bitcast(I32),
-            )
-            nc.gpsimd.dma_start(
-                wcs_raw[32 * q : 32 * q + 4, :, :].bitcast(I32),
-                wc_scales[:, 4 * q : 4 * q + 4, :].rearrange("a r e -> r a e").bitcast(I32),
-            )
+            load_scale_rows(wbs_raw, wb_scales, q)
         nc.sync.dma_start(tabw[1][:].bitcast(I32), tab_rows[1])
-        bias = keep.tile([P, 2, 4], F32, name="bias")
-        nc.gpsimd.dma_start(bias[:], be.rearrange("(g p t) -> p g t", p=P, t=4))
-        wa_raw = []
-        for a in range(2):
-            wr = keep.tile([P, 4, H], F32, name="wa_raw%d" % a)
-            nc.sync.dma_start(wr[:], wa[512 * a : 512 * (a + 1), :].rearrange("(p j) r -> p j r", j=4))
-            wa_raw.append(wr)
-        we_raw = []
-        we_rows = we.rearrange("(q s i) (g n) -> g s q i n", s=4, i=8, g=2)
-        for g in range(2):
-            wr = keep.tile([P, 4, 512], F32, name="we_raw%d" % g)
-            for s in range(4):
-                nc.sync.dma_start(wr[:, s, :], we_rows[g, s])
-            we_raw.append(wr)
+        for q in range(4):
+            load_scale_rows(wcs_raw, wc_scales, q)
 
-        vsc = keep.tile([P, S], U8, name="vsc", align_bytes=64)
+        vsc = keep.tile([P, S], U8, name="vsc", tag="vsc", align_bytes=64)
         nc.vector.tensor_copy(vsc[:], tsc[:].indirect(offsets[:]))
         for a in range(2):
             first = 24 + 4 * a
-            nc.gpsimd.dma_start(vscale[0 : P - first, a, :].bitcast(I32), vsc[first:P, :].bitcast(I32))
+            nc.sync.dma_start(vscale[0 : P - first, a, :].bitcast(I32), vsc[first:P, :].bitcast(I32))
         vw0 = keep.tile([P, S], U32, name="vw0", align_bytes=64)
         nc.vector.tensor_copy(vw0[:], tabw[0][:].indirect(offsets[:]))
 
@@ -99,22 +88,38 @@ def tile_list_triplex_median_vote_kernel(
         nc.vector.tensor_copy(
             wb_p[:].rearrange("p a t (q i) -> p a q t i", i=8), wb_raw[:].rearrange("p a (q t i) -> p a q t i", t=4, i=8)
         )
-        wc_p = keep.tile([P, 2, 4, 2 * P], U8, name="wc_p", align_bytes=64)
+        wc_p = keep.tile([P, 2, 4, 2 * P], U8, name="wc_p", tag="wb_raw", align_bytes=64)
         nc.vector.tensor_copy(
             wc_p[:].bitcast(I32).rearrange("p a t (q i) -> p a q t i", i=4),
             wc_raw[:].rearrange("p a (q t i) -> p a q t i", t=4, i=4),
         )
-        wb_s = keep.tile([P, 2, 4, P], U8, name="wb_s", align_bytes=64)
-        wc_s = keep.tile([P, 2, 4, P], U8, name="wc_s", align_bytes=64)
-        for dealt, raw in ((wb_s, wbs_raw), (wc_s, wcs_raw)):
+
+        def deal_scales(name, raw, tag):
+            dealt = keep.tile([P, 2, 4, P], U8, name=name, tag=tag, align_bytes=64)
             nc.vector.tensor_copy(
                 dealt[:].bitcast(I32).rearrange("p a t (q i) -> p a q t i", i=2),
                 raw[:].bitcast(I32).rearrange("p a (q t i) -> p a q t i", t=4, i=2),
             )
+            return dealt
+
+        wb_s = deal_scales("wb_s", wbs_raw, "wc_raw")
         vw1a = keep.tile([P, FIRST], U32, name="vw1a", align_bytes=64)
         nc.vector.tensor_copy(vw1a[:], tabw[1][:].indirect(offsets[:, : FIRST // 16]))
-        vw1b = keep.tile([P, S - FIRST], U32, name="vw1b", align_bytes=64)
+        wc_s = deal_scales("wc_s", wcs_raw, "wbs_raw")
+        vw1b = keep.tile([P, S - FIRST], U32, name="vw1b", tag="wcs_raw", align_bytes=64)
         nc.vector.tensor_copy(vw1b[:], tabw[1][:].indirect(offsets[:, FIRST // 16 :]))
+
+        stage = keep.tile([P, 4, 4, 512], F32, name="stage", tag="tsc", align_bytes=64)
+        wa_raw = [stage[:, a] for a in range(2)]
+        we_raw = [stage[:, 2 + g] for g in range(2)]
+        for a in range(2):
+            nc.sync.dma_start(wa_raw[a], wa[512 * a : 512 * (a + 1), :].rearrange("(p j) r -> p j r", j=4))
+        we_rows = we.rearrange("(q s i) (g n) -> g s q i n", s=4, i=8, g=2)
+        for g in range(2):
+            for s in range(4):
+                nc.sync.dma_start(we_raw[g][:, s, :], we_rows[g, s])
+        bias = keep.tile([P, 2, 4], F32, name="bias", tag="vsc", align_bytes=64)
+        nc.sync.dma_start(bias[:], be.rearrange("(g p t) -> p g t", p=P, t=4))
 
         def picked(a, j):
             if a == 0:
@@ -131,12 +136,12 @@ def tile_list_triplex_median_vote_kernel(
                     if a == 1 and t >= 3:
                         nc.scalar.copy(
                             wa_bf[:, t, :, :].rearrange("p (q i) j -> p q j i", i=8),
-                            wa_raw[a][:].rearrange("p j (q t i) -> p t q j i", t=4, i=8)[:, t],
+                            wa_raw[a].rearrange("p j (q t i) -> p t q j i", t=4, i=8)[:, t],
                         )
                     else:
                         nc.gpsimd.tensor_scalar(
                             wa_bf[:, t, :, :].rearrange("p (q i) j -> p q i j", i=8),
-                            wa_raw[a][:].rearrange("p j (q t i) -> p t q i j", t=4, i=8)[:, t],
+                            wa_raw[a].rearrange("p j (q t i) -> p t q i j", t=4, i=8)[:, t],
                             1.0,
                             1.0,
                             MULT,
@@ -152,7 +157,7 @@ def tile_list_triplex_median_vote_kernel(
         we_s = keep.tile([P, 2, 4, P], U8, name="we_s", align_bytes=64)
 
         def prepare_we(g):
-            we_bf = keep.tile([P, 4, P, 4], BF16, name="we_bf%d" % g, tag="we_bf%d" % g, align_bytes=64)
+            we_bf = keep.tile([P, 4, P, 4], BF16, name="we_bf%d" % g, align_bytes=64)
             for m0 in range(0, P, 32):
                 dst = we_bf[:, :, m0 : m0 + 32, :].rearrange("p t m s -> p m s t")
                 src = we_raw[g][:, :, 4 * m0 : 4 * (m0 + 32)].rearrange("p s (m t) -> p m s t", t=4)
@@ -183,39 +188,42 @@ def tile_list_triplex_median_vote_kernel(
         y_words = out_1.rearrange("g p m t -> p g (m t)").bitcast(I32)
 
         starts = [sum(GROUPS[:i]) for i in range(len(GROUPS))]
-        los = {}
+        lo = keep.tile([P, S, 4], F32, name="lo")
+        mid = keep.tile([P, S, 4], F32, name="mid")
+        pairs = {}
         his = {}
 
-        def bounds(j):
+        def lower(j):
             b_ps = product("b", lambda a, t: wb_p[:, a, t, :].bitcast(FP8X4), lambda a, t: wb_s[:, a, t, :], j)
             c_ps = product("c", lambda a, t: wc_p[:, a, t, :].bitcast(FP4X4), lambda a, t: wc_s[:, a, t, :], j)
             b_sb = ring.tile([P, CH, 4], F32, name="b_sb", tag="b_sb", bufs=2)
             nc.scalar.copy(b_sb[:], b_ps)
+            nc.vector.tensor_tensor(lo[:, j : j + CH, :], b_sb[:], c_ps, MIN)
+            pairs[j] = (b_sb, c_ps)
+
+        def upper(j):
+            b_sb, c_ps = pairs[j]
             hi = ring.tile([P, CH, 4], F32, name="hi", tag="hi", bufs=4)
-            if j in starts:
-                w = GROUPS[starts.index(j)]
-                lo = keep.tile([P, w, 4], F32, name="lo%d" % j, tag="we_bf1" if j == 512 else "lo%d" % j, align_bytes=64)
-                for c in range(0, w, CH):
-                    los[j + c] = (lo, c)
-            lo, c = los[j]
-            nc.vector.tensor_tensor(lo[:, c : c + CH, :], b_sb[:], c_ps, MIN)
             nc.vector.tensor_tensor(hi[:], b_sb[:], c_ps, MAX)
             his[j] = hi
 
-        def vote(j0, w):
-            mid = keep.tile([P, w, 4], F32, name="mid%d" % j0, tag="we_bf0" if j0 == 256 else "mid%d" % j0, align_bytes=64)
-            for c in range(0, w, CH):
-                a_ps = product("a", lambda a, t: wa_q[:, a, t, :].bitcast(FP8X4), lambda a, t: wa_s[:, a, t, :], j0 + c)
-                nc.vector.tensor_tensor(mid[:, c : c + CH, :], his[j0 + c][:], a_ps, MIN)
+        def clip(j):
+            a_ps = product("a", lambda a, t: wa_q[:, a, t, :].bitcast(FP8X4), lambda a, t: wa_s[:, a, t, :], j)
+            nc.vector.tensor_tensor(mid[:, j : j + CH, :], his[j][:], a_ps, MIN)
+
+        def median(j0, w):
             h_bf = ring.tile([P, w, 4], BF16, name="h_bf", tag="h_bf", align_bytes=64)
-            nc.vector.tensor_tensor(h_bf[:], los[j0][0][:], mid[:], MAX)
-            h_q = ring.tile([P, w], U32, name="h_q", tag="h_q", align_bytes=64)
-            h_s = ring.tile([P, w], U8, name="h_s", tag="h_s", align_bytes=64)
+            nc.vector.tensor_tensor(h_bf[:], lo[:, j0 : j0 + w, :], mid[:, j0 : j0 + w, :], MAX)
+            return h_bf
+
+        def quantise_h(h_bf, w):
+            h_q = ring.tile([P, w], U32, name="h_q", tag="h_q", align_bytes=64, bufs=3)
+            h_s = ring.tile([P, w], U8, name="h_s", tag="h_s", align_bytes=64, bufs=3)
             nc.vector.quantize_mx(h_q[:].bitcast(FP8X4), h_s[:], h_bf[:].rearrange("p j t -> p (j t)"))
             return h_q, h_s
 
         def estimate(j0, w, h_q, h_s):
-            y_q = ring.tile([P, 2, w], U32, name="y_q", tag="y_q", align_bytes=64, bufs=3)
+            rounded = []
             for g in range(2):
                 y = ring.tile([P, 4, w], F32, name="y", tag="y", bufs=4)
                 per_bank = 512 // w
@@ -238,7 +246,7 @@ def tile_list_triplex_median_vote_kernel(
                         else:
                             nc.scalar.activation(y[:, t0 + u, :], bank[:, u, :], IDENT, bias=column)
                 nc.sync.dma_start(y_rows[g][:, :, j0 : j0 + w], y[:])
-                y_bf = ring.tile([P, w, 4], BF16, name="y_bf", tag="y_bf", align_bytes=64, bufs=3)
+                y_bf = ring.tile([P, w, 4], BF16, name="y_bf", tag="y_bf", align_bytes=64, bufs=4)
                 dst = y_bf[:].rearrange("p (c i) t -> p c t i", i=4)
                 src = y[:].rearrange("p t (c i) -> p c t i", i=4)
                 if g == 0:
@@ -247,22 +255,40 @@ def tile_list_triplex_median_vote_kernel(
                     nc.gpsimd.tensor_scalar(y_bf[:], y[:].rearrange("p t j -> p j t"), 1.0, 1.0, MULT, MULT)
                 else:
                     nc.vector.tensor_copy(dst, src)
+                rounded.append(y_bf)
+            return rounded
+
+        def planes(j0, w, rounded):
+            y_q = ring.tile([P, 2, w], U32, name="y_q", tag="y_q", align_bytes=64, bufs=3)
+            for g in range(2):
                 nc.vector.quantize_mx(
-                    y_q[:, g, :].bitcast(FP8X4), y_s[:, g, j0 : j0 + w], y_bf[:].rearrange("p j t -> p (j t)")
+                    y_q[:, g, :].bitcast(FP8X4), y_s[:, g, j0 : j0 + w], rounded[g][:].rearrange("p j t -> p (j t)")
                 )
             nc.sync.dma_start(y_words[:, :, j0 : j0 + w], y_q[:].bitcast(I32))
 
         for j in range(0, LEAD, CH):
-            bounds(j)
+            lower(j)
+            upper(j)
         prepare_wa()
-        for i in range(len(GROUPS)):
-            voted = vote(starts[i], GROUPS[i])
+        behind = None
+        for i, (j0, w) in enumerate(zip(starts, GROUPS)):
+            ahead = LEAD + CH * i
+            for j in range(j0, j0 + w, CH):
+                clip(j)
+            if ahead < S:
+                lower(ahead)
             if i == 0:
                 prepare_we(0)
+            h_bf = median(j0, w)
+            if ahead < S:
+                upper(ahead)
+            if i == 0:
                 prepare_we(1)
-            estimate(starts[i], GROUPS[i], *voted)
-            for j in range(LEAD + starts[i], min(S, LEAD + starts[i] + GROUPS[i]), CH):
-                bounds(j)
+            h_mx = quantise_h(h_bf, w)
+            if behind is not None:
+                planes(*behind)
+            behind = (j0, w, estimate(j0, w, *h_mx))
+        planes(*behind)
         for q in range(4):
             (nc.scalar if q % 2 else nc.sync).dma_start(
                 out_2[:, 4 * q : 4 * q + 4, :].rearrange("g r m -> r g m").bitcast(I32),

@@ -16,7 +16,6 @@ FP4X4 = mybir.dt.float4_e2m1fn_x4
 MIN = mybir.AluOpType.min
 MAX = mybir.AluOpType.max
 ADD = mybir.AluOpType.add
-MULT = mybir.AluOpType.mult
 IDENT = mybir.ActivationFunctionType.Identity
 
 P = 128
@@ -133,20 +132,12 @@ def tile_list_triplex_median_vote_kernel(
             for a in range(2):
                 wa_bf = keep.tile([P, 4, P, 4], BF16, name="wa_bf%d" % a, align_bytes=64)
                 for t in range(4):
-                    if a == 1 and t >= 3:
-                        nc.scalar.copy(
-                            wa_bf[:, t, :, :].rearrange("p (q i) j -> p q j i", i=8),
-                            wa_raw[a].rearrange("p j (q t i) -> p t q j i", t=4, i=8)[:, t],
-                        )
+                    dst = wa_bf[:, t, :, :].rearrange("p (q i) j -> p q i j", i=8)
+                    src = wa_raw[a].rearrange("p j (q t i) -> p t q i j", t=4, i=8)[:, t]
+                    if a == 1 and t == 3:
+                        nc.vector.tensor_copy(dst, src)
                     else:
-                        nc.gpsimd.tensor_scalar(
-                            wa_bf[:, t, :, :].rearrange("p (q i) j -> p q i j", i=8),
-                            wa_raw[a].rearrange("p j (q t i) -> p t q i j", t=4, i=8)[:, t],
-                            1.0,
-                            1.0,
-                            MULT,
-                            MULT,
-                        )
+                        nc.scalar.copy(dst, src)
                 nc.vector.quantize_mx(
                     wa_q[:, a].rearrange("p t m -> p (t m)").bitcast(FP8X4),
                     wa_s[:, a].rearrange("p t m -> p (t m)"),
@@ -159,8 +150,8 @@ def tile_list_triplex_median_vote_kernel(
         def prepare_we(g):
             we_bf = keep.tile([P, 4, P, 4], BF16, name="we_bf%d" % g, align_bytes=64)
             for m0 in range(0, P, 32):
-                dst = we_bf[:, :, m0 : m0 + 32, :].rearrange("p t m s -> p m s t")
-                src = we_raw[g][:, :, 4 * m0 : 4 * (m0 + 32)].rearrange("p s (m t) -> p m s t", t=4)
+                dst = we_bf[:, :, m0 : m0 + 32, :].rearrange("p t m s -> p m t s")
+                src = we_raw[g][:, :, 4 * m0 : 4 * (m0 + 32)].rearrange("p s (m t) -> p m t s", t=4)
                 nc.scalar.copy(dst, src)
             nc.vector.quantize_mx(
                 we_q[:, g].rearrange("p t m -> p (t m)").bitcast(FP8X4),
@@ -247,22 +238,18 @@ def tile_list_triplex_median_vote_kernel(
                             nc.scalar.activation(y[:, t0 + u, :], bank[:, u, :], IDENT, bias=column)
                 nc.sync.dma_start(y_rows[g][:, :, j0 : j0 + w], y[:])
                 y_bf = ring.tile([P, w, 4], BF16, name="y_bf", tag="y_bf", align_bytes=64, bufs=4)
-                dst = y_bf[:].rearrange("p (c i) t -> p c t i", i=4)
-                src = y[:].rearrange("p t (c i) -> p c t i", i=4)
                 if g == 0:
-                    nc.scalar.copy(dst, src)
-                elif j0 + w < S:
-                    nc.gpsimd.tensor_scalar(y_bf[:], y[:].rearrange("p t j -> p j t"), 1.0, 1.0, MULT, MULT)
-                else:
-                    nc.vector.tensor_copy(dst, src)
-                rounded.append(y_bf)
+                    nc.scalar.copy(y_bf[:], y[:].rearrange("p t j -> p j t"))
+                rounded.append((y, y_bf))
             return rounded
 
         def planes(j0, w, rounded):
             y_q = ring.tile([P, 2, w], U32, name="y_q", tag="y_q", align_bytes=64, bufs=3)
+            y, y_bf = rounded[1]
+            nc.vector.tensor_copy(y_bf[:], y[:].rearrange("p t j -> p j t"))
             for g in range(2):
                 nc.vector.quantize_mx(
-                    y_q[:, g, :].bitcast(FP8X4), y_s[:, g, j0 : j0 + w], rounded[g][:].rearrange("p j t -> p (j t)")
+                    y_q[:, g, :].bitcast(FP8X4), y_s[:, g, j0 : j0 + w], rounded[g][1][:].rearrange("p j t -> p (j t)")
                 )
             nc.sync.dma_start(y_words[:, :, j0 : j0 + w], y_q[:].bitcast(I32))
 

@@ -15,6 +15,7 @@ FP8X4 = mybir.dt.float8_e4m3fn_x4
 FP4X4 = mybir.dt.float4_e2m1fn_x4
 MIN = mybir.AluOpType.min
 MAX = mybir.AluOpType.max
+MULT = mybir.AluOpType.mult
 ADD = mybir.AluOpType.add
 IDENT = mybir.ActivationFunctionType.Identity
 
@@ -43,10 +44,6 @@ def tile_list_triplex_median_vote_kernel(
             (nc.vector if name == "wbs_raw" else nc.gpsimd).memset(raw[:].bitcast(I32), 0)
             w_sraw.append(raw)
         wbs_raw, wcs_raw = w_sraw
-        zero = keep.tile([P, 1], F32, name="zero")
-        nc.vector.memset(zero[:], 0.0)
-        warm = keep.tile([P, 1], F32, name="warm")
-        nc.scalar.activation(warm[:], zero[:], IDENT)
         tsc = keep.tile([P, T], U8, name="tsc", tag="tsc", align_bytes=64)
         for q in range(4):
             nc.vector.memset(tsc[32 * q : 32 * q + 24, :].bitcast(I32), 0)
@@ -134,7 +131,12 @@ def tile_list_triplex_median_vote_kernel(
                 for t in range(4):
                     dst = wa_bf[:, t, :, :].rearrange("p (q i) j -> p q i j", i=8)
                     src = wa_raw[a].rearrange("p j (q t i) -> p t q i j", t=4, i=8)[:, t]
-                    if a == 1 and t == 3:
+                    if a == 0:
+                        nc.gpsimd.tensor_scalar(dst, src, 1.0, 1.0, MULT, MULT)
+                        continue
+                    dst = dst.rearrange("p q (u e) j -> p q u j e", e=2)
+                    src = src.rearrange("p q (u e) j -> p q u j e", e=2)
+                    if t == 3:
                         nc.vector.tensor_copy(dst, src)
                     else:
                         nc.scalar.copy(dst, src)
@@ -172,39 +174,40 @@ def tile_list_triplex_median_vote_kernel(
                         start=(a == 0),
                         stop=(a == 1),
                     )
-            return bank[:].rearrange("p t j -> p j t")
+            return bank[:].rearrange("p t (u e) -> p u t e", e=2)
 
         y_s = keep.tile([P, 2, S], U8, name="y_s", align_bytes=64)
         y_rows = out_0.rearrange("(g p t) j -> g p t j", p=P, t=4)
         y_words = out_1.rearrange("g p m t -> p g (m t)").bitcast(I32)
 
         starts = [sum(GROUPS[:i]) for i in range(len(GROUPS))]
-        lo = keep.tile([P, S, 4], F32, name="lo")
-        mid = keep.tile([P, S, 4], F32, name="mid")
+        lo = keep.tile([P, S // 2, 4, 2], F32, name="lo")
+        mid = keep.tile([P, S // 2, 4, 2], F32, name="mid")
         pairs = {}
         his = {}
 
         def lower(j):
             b_ps = product("b", lambda a, t: wb_p[:, a, t, :].bitcast(FP8X4), lambda a, t: wb_s[:, a, t, :], j)
             c_ps = product("c", lambda a, t: wc_p[:, a, t, :].bitcast(FP4X4), lambda a, t: wc_s[:, a, t, :], j)
-            b_sb = ring.tile([P, CH, 4], F32, name="b_sb", tag="b_sb", bufs=2)
-            nc.scalar.copy(b_sb[:], b_ps)
-            nc.vector.tensor_tensor(lo[:, j : j + CH, :], b_sb[:], c_ps, MIN)
+            b_sb = ring.tile([P, CH // 2, 4, 2], F32, name="b_sb", tag="b_sb", bufs=2)
+            nc.scalar.activation(b_sb[:], b_ps, IDENT)
+            nc.vector.tensor_tensor(lo[:, j // 2 : (j + CH) // 2], b_sb[:], c_ps, MIN)
             pairs[j] = (b_sb, c_ps)
 
         def upper(j):
             b_sb, c_ps = pairs[j]
-            hi = ring.tile([P, CH, 4], F32, name="hi", tag="hi", bufs=4)
+            hi = ring.tile([P, CH // 2, 4, 2], F32, name="hi", tag="hi", bufs=4)
             nc.vector.tensor_tensor(hi[:], b_sb[:], c_ps, MAX)
             his[j] = hi
 
         def clip(j):
             a_ps = product("a", lambda a, t: wa_q[:, a, t, :].bitcast(FP8X4), lambda a, t: wa_s[:, a, t, :], j)
-            nc.vector.tensor_tensor(mid[:, j : j + CH, :], his[j][:], a_ps, MIN)
+            nc.vector.tensor_tensor(mid[:, j // 2 : (j + CH) // 2], his[j][:], a_ps, MIN)
 
         def median(j0, w):
             h_bf = ring.tile([P, w, 4], BF16, name="h_bf", tag="h_bf", align_bytes=64)
-            nc.vector.tensor_tensor(h_bf[:], lo[:, j0 : j0 + w, :], mid[:, j0 : j0 + w, :], MAX)
+            span = slice(j0 // 2, (j0 + w) // 2)
+            nc.vector.tensor_tensor(h_bf[:].rearrange("p (u e) t -> p u t e", e=2), lo[:, span], mid[:, span], MAX)
             return h_bf
 
         def quantise_h(h_bf, w):
@@ -216,7 +219,7 @@ def tile_list_triplex_median_vote_kernel(
         def estimate(j0, w, h_q, h_s):
             rounded = []
             for g in range(2):
-                y = ring.tile([P, 4, w], F32, name="y", tag="y", bufs=4)
+                y = ring.tile([P, 4, w], F32, name="y", tag="y", bufs=6)
                 per_bank = 512 // w
                 for t0 in range(0, 4, per_bank):
                     bank = psum.tile([P, per_bank, w], F32, name="ybank", tag="ybank")
@@ -237,16 +240,16 @@ def tile_list_triplex_median_vote_kernel(
                         else:
                             nc.scalar.activation(y[:, t0 + u, :], bank[:, u, :], IDENT, bias=column)
                 nc.sync.dma_start(y_rows[g][:, :, j0 : j0 + w], y[:])
-                y_bf = ring.tile([P, w, 4], BF16, name="y_bf", tag="y_bf", align_bytes=64, bufs=4)
+                y_bf = ring.tile([P, w, 4], BF16, name="y_bf", tag="y_bf", align_bytes=64, bufs=6)
                 if g == 0:
-                    nc.scalar.copy(y_bf[:], y[:].rearrange("p t j -> p j t"))
+                    nc.scalar.copy(y_bf[:].rearrange("p (u e) t -> p u t e", e=2), y[:].rearrange("p t (u e) -> p u t e", e=2))
                 rounded.append((y, y_bf))
             return rounded
 
         def planes(j0, w, rounded):
             y_q = ring.tile([P, 2, w], U32, name="y_q", tag="y_q", align_bytes=64, bufs=3)
             y, y_bf = rounded[1]
-            nc.vector.tensor_copy(y_bf[:], y[:].rearrange("p t j -> p j t"))
+            nc.vector.tensor_copy(y_bf[:].rearrange("p (u e) t -> p u t e", e=2), y[:].rearrange("p t (u e) -> p u t e", e=2))
             for g in range(2):
                 nc.vector.quantize_mx(
                     y_q[:, g, :].bitcast(FP8X4), y_s[:, g, j0 : j0 + w], rounded[g][1][:].rearrange("p j t -> p (j t)")

@@ -16,14 +16,18 @@ FP4X4 = mybir.dt.float4_e2m1fn_x4
 MIN = mybir.AluOpType.min
 MAX = mybir.AluOpType.max
 MULT = mybir.AluOpType.mult
-ADD = mybir.AluOpType.add
 IDENT = mybir.ActivationFunctionType.Identity
 
 P = 128
-CH = 128
-GROUPS = [256, 256, 256, 128, 128]
-FIRST = 256
-LEAD = 512
+HALF = 512
+BATCHES = [256, 256, 256, 128, 128]
+SCALAR_ROUNDS = [(0, 0), (0, 1), (1, 0), (1, 1), (2, 0)]
+B_BANKS = [0, 1, 5, 6, 7, 0, 1, 7]
+C_BANKS = [2, 3, 4]
+A_BANKS = [6, 5]
+Y_BANKS = [[0, 1, 7], [0, 1, 7, 2, 3, 4]]
+RAW = 4 * 512 * 4
+LAG = 2
 
 
 def tile_list_triplex_median_vote_kernel(
@@ -32,253 +36,299 @@ def tile_list_triplex_median_vote_kernel(
     nc = tc.nc
     with ExitStack() as ctx:
         keep = ctx.enter_context(tc.tile_pool(name="keep", bufs=1))
+        late = ctx.enter_context(tc.tile_pool(name="late", bufs=1))
         ring = ctx.enter_context(tc.tile_pool(name="ring", bufs=2))
-        psum = ctx.enter_context(tc.psum_pool(name="psum", bufs=2))
+        psum = ctx.enter_context(tc.psum_pool(name="psum", bufs=1))
 
         offsets = keep.tile([P, S // 16], U16, name="offsets")
         nc.sync.dma_start(offsets[:], offs)
 
-        w_sraw = []
-        for name in ("wbs_raw", "wcs_raw"):
-            raw = keep.tile([P, 2, H], U8, name=name, tag=name, align_bytes=64)
-            (nc.vector if name == "wbs_raw" else nc.gpsimd).memset(raw[:].bitcast(I32), 0)
-            w_sraw.append(raw)
-        wbs_raw, wcs_raw = w_sraw
-        tsc = keep.tile([P, T], U8, name="tsc", tag="tsc", align_bytes=64)
-        for q in range(4):
-            nc.vector.memset(tsc[32 * q : 32 * q + 24, :].bitcast(I32), 0)
-            nc.sync.dma_start(
-                tsc[32 * q + 24 : 32 * q + 32, :].bitcast(I32), tab_scales[:, 4 * q : 4 * q + 4, :].bitcast(I32)
-            )
-        vscale = keep.tile([P, 2, S], U8, name="vscale", align_bytes=64)
-        nc.gpsimd.memset(vscale[:].bitcast(I32), 0)
-
-        def load_scale_rows(raw, scales, q):
-            nc.sync.dma_start(
-                raw[32 * q : 32 * q + 4, :, :].bitcast(I32),
-                scales[:, 4 * q : 4 * q + 4, :].rearrange("a r e -> r a e").bitcast(I32),
-            )
+        tsc = keep.tile([P, T], U8, name="tsc", align_bytes=64)
+        nc.sync.dma_start(tsc[0:32, :].bitcast(I32), tab_scales.rearrange("a i t -> i a t").bitcast(I32))
+        nc.vector.memset(tsc[32:64, :].bitcast(I32), 0)
+        nc.vector.memset(tsc[64:128, :].bitcast(I32), 0)
+        wsr = []
+        for name, scales in (("wbs_raw", wb_scales), ("wcs_raw", wc_scales)):
+            raw = keep.tile([32, H], U8, name=name, align_bytes=64)
+            nc.sync.dma_start(raw[:].bitcast(I32), scales.rearrange("a i e -> i a e").bitcast(I32))
+            wsr.append(raw)
+        planes = keep.tile([P, 2, S + 2 * H], U8, name="planes", align_bytes=64)
+        nc.gpsimd.memset(planes[:].bitcast(I32), 0)
 
         tabw = [keep.tile([P, T], U32, name="tabw%d" % a, tag="tabw%d" % a, align_bytes=64) for a in range(2)]
         tab_rows = tab_words.rearrange("a p t i -> a p (t i)").bitcast(I32)
         nc.sync.dma_start(tabw[0][:].bitcast(I32), tab_rows[0])
         wb_raw = keep.tile([P, 2, H], I32, name="wb_raw", tag="wb_raw", align_bytes=64)
         nc.sync.dma_start(wb_raw[:], wb_words.rearrange("a p e i -> p a (e i)").bitcast(I32))
+        nc.sync.dma_start(tabw[1][:].bitcast(I32), tab_rows[1])
         wc_raw = keep.tile([P, 2, H // 2], I32, name="wc_raw", tag="wc_raw", align_bytes=64)
         nc.sync.dma_start(wc_raw[:], wc_words.rearrange("a p b -> p a b").bitcast(I32))
-        for q in range(4):
-            load_scale_rows(wbs_raw, wb_scales, q)
-        nc.sync.dma_start(tabw[1][:].bitcast(I32), tab_rows[1])
-        for q in range(4):
-            load_scale_rows(wcs_raw, wc_scales, q)
 
-        vsc = keep.tile([P, S], U8, name="vsc", tag="vsc", align_bytes=64)
-        nc.vector.tensor_copy(vsc[:], tsc[:].indirect(offsets[:]))
-        for a in range(2):
-            first = 24 + 4 * a
-            nc.sync.dma_start(vscale[0 : P - first, a, :].bitcast(I32), vsc[first:P, :].bitcast(I32))
-        vw0 = keep.tile([P, S], U32, name="vw0", align_bytes=64)
-        nc.vector.tensor_copy(vw0[:], tabw[0][:].indirect(offsets[:]))
-
-        wb_p = keep.tile([P, 2, 4, P], I32, name="wb_p", tag="tabw0", align_bytes=64)
-        nc.vector.tensor_copy(
-            wb_p[:].rearrange("p a t (q i) -> p a q t i", i=8), wb_raw[:].rearrange("p a (q t i) -> p a q t i", t=4, i=8)
-        )
-        wc_p = keep.tile([P, 2, 4, 2 * P], U8, name="wc_p", tag="wb_raw", align_bytes=64)
-        nc.vector.tensor_copy(
-            wc_p[:].bitcast(I32).rearrange("p a t (q i) -> p a q t i", i=4),
-            wc_raw[:].rearrange("p a (q t i) -> p a q t i", t=4, i=4),
-        )
-
-        def deal_scales(name, raw, tag):
-            dealt = keep.tile([P, 2, 4, P], U8, name=name, tag=tag, align_bytes=64)
-            nc.vector.tensor_copy(
-                dealt[:].bitcast(I32).rearrange("p a t (q i) -> p a q t i", i=2),
-                raw[:].bitcast(I32).rearrange("p a (q t i) -> p a q t i", t=4, i=2),
+        vsc = late.tile([P, 4 * RAW + 64], U8, name="vsc", offset=0, align_bytes=64)
+        nc.vector.tensor_copy(vsc[:, 0:S], tsc[:].indirect(offsets[:]))
+        staged = keep.tile([P, S + 2 * H], U8, name="staged", align_bytes=64)
+        for n, raw in enumerate(wsr):
+            nc.gpsimd.tensor_copy(
+                staged[0:32, S + n * H : S + (n + 1) * H].bitcast(I32).rearrange("p (t q i) -> p q t i", t=4, i=2),
+                raw[:].bitcast(I32).rearrange("p (q t i) -> p q t i", t=4, i=2),
             )
-            return dealt
+        nc.vector.tensor_copy(staged[:, 0:S].bitcast(I32), vsc[:, 0:S].bitcast(I32))
+        for q in range(4):
+            nc.sync.dma_start(planes[32 * q : 32 * q + 4, :, :].bitcast(I32), staged[8 * q : 8 * q + 8, :].bitcast(I32))
 
-        wb_s = deal_scales("wb_s", wbs_raw, "wc_raw")
-        vw1a = keep.tile([P, FIRST], U32, name="vw1a", align_bytes=64)
-        nc.vector.tensor_copy(vw1a[:], tabw[1][:].indirect(offsets[:, : FIRST // 16]))
-        wc_s = deal_scales("wc_s", wcs_raw, "wbs_raw")
-        vw1b = keep.tile([P, S - FIRST], U32, name="vw1b", tag="wcs_raw", align_bytes=64)
-        nc.vector.tensor_copy(vw1b[:], tabw[1][:].indirect(offsets[:, FIRST // 16 :]))
-
-        stage = keep.tile([P, 4, 4, 512], F32, name="stage", tag="tsc", align_bytes=64)
-        wa_raw = [stage[:, a] for a in range(2)]
-        we_raw = [stage[:, 2 + g] for g in range(2)]
+        wa_raw = [late.tile([P, 4, 512], F32, name="wa_raw%d" % a, offset=a * RAW, align_bytes=64) for a in range(2)]
+        we_raw = [late.tile([P, 4, 512], F32, name="we_raw%d" % g, offset=(2 + g) * RAW, align_bytes=64) for g in range(2)]
         for a in range(2):
-            nc.sync.dma_start(wa_raw[a], wa[512 * a : 512 * (a + 1), :].rearrange("(p j) r -> p j r", j=4))
+            nc.sync.dma_start(wa_raw[a][:], wa[512 * a : 512 * (a + 1), :].rearrange("(p j) r -> p j r", j=4))
         we_rows = we.rearrange("(q s i) (g n) -> g s q i n", s=4, i=8, g=2)
         for g in range(2):
             for s in range(4):
                 nc.sync.dma_start(we_raw[g][:, s, :], we_rows[g, s])
-        bias = keep.tile([P, 2, 4], F32, name="bias", tag="vsc", align_bytes=64)
+        bias = late.tile([P, 2, 4], F32, name="bias", offset=4 * RAW, align_bytes=64)
         nc.sync.dma_start(bias[:], be.rearrange("(g p t) -> p g t", p=P, t=4))
 
-        def picked(a, j):
-            if a == 0:
-                return vw0[:, j : j + CH]
-            return vw1a[:, j : j + CH] if j < FIRST else vw1b[:, j - FIRST : j - FIRST + CH]
+        wb_p = keep.tile([P, 2, 4, P], I32, name="wb_p", align_bytes=64)
+        nc.gpsimd.tensor_copy(
+            wb_p[:].rearrange("p a t (q i) -> p a q t i", i=8), wb_raw[:].rearrange("p a (q t i) -> p a q t i", t=4, i=8)
+        )
+        wc_p = keep.tile([P, 2, 4, 2 * P], U8, name="wc_p", align_bytes=64)
+        nc.gpsimd.tensor_copy(
+            wc_p[:].bitcast(I32).rearrange("p a t (q i) -> p a q t i", i=4),
+            wc_raw[:].rearrange("p a (q t i) -> p a q t i", t=4, i=4),
+        )
+        vw = {}
+        for a in range(2):
+            for h in range(2):
+                vw[a, h] = keep.tile([P, HALF], U32, name="vw%d_%d" % (a, h), align_bytes=64)
+                nc.vector.tensor_copy(vw[a, h][:], tabw[a][:].indirect(offsets[:, h * HALF // 16 : (h + 1) * HALF // 16]))
+
+        def picked(a, j, w):
+            h, c0 = divmod(j, HALF)
+            return vw[a, h][:, c0 : c0 + w]
+
+        def bank_tile(n):
+            return psum.tile([P, 512], F32, name="bank%d" % n, tag="bank%d" % n)
+
+        def product(out, codes, scales, j, w):
+            for a in range(2):
+                nc.tensor.matmul_mx(
+                    out,
+                    lhsT=codes(a),
+                    lhsT_scale=scales(a),
+                    rhs=picked(a, j, w).bitcast(FP8X4),
+                    rhs_scale=planes[:, a, j : j + w],
+                    start=(a == 0),
+                    stop=(a == 1),
+                )
+
+        idle = bank_tile(7)
+        for n in range(4):
+            nc.tensor.matmul_mx(
+                idle[:],
+                lhsT=vw[0, 0][:, 0:P].bitcast(FP8X4),
+                lhsT_scale=staged[:, 0:P],
+                rhs=vw[0, 0][:].bitcast(FP8X4),
+                rhs_scale=staged[:, 0:HALF],
+                start=True,
+                stop=True,
+            )
+
+        b_sb = {}
+        c_ps = {}
+        lo = [keep.tile([P, 4, HALF], F32, name="lo%d" % h) for h in range(2)]
+        hi = [keep.tile([P, 4, HALF], F32, name="hi%d" % h) for h in range(2)]
+
+        def channel_b(n):
+            h, t = divmod(n, 4)
+            bank = bank_tile(B_BANKS[n])
+            product(
+                bank[:],
+                lambda a: wb_p[:, a, t, :].bitcast(FP8X4),
+                lambda a: planes[:, a, S + P * t : S + P * (t + 1)],
+                h * HALF,
+                HALF,
+            )
+            b_sb[n] = keep.tile([P, HALF], F32, name="b_sb%d" % n)
+            nc.scalar.activation(b_sb[n][:], bank[:], IDENT)
+
+        def channel_c(n):
+            h, t = divmod(n, 4)
+            c_ps[n] = bank_tile(C_BANKS[n % len(C_BANKS)])
+            product(
+                c_ps[n][:],
+                lambda a: wc_p[:, a, t, :].bitcast(FP4X4),
+                lambda a: planes[:, a, S + H + P * t : S + H + P * (t + 1)],
+                h * HALF,
+                HALF,
+            )
+
+        def bound(n, dst, op):
+            h, t = divmod(n, 4)
+            nc.vector.tensor_tensor(dst[h][:, t, :], b_sb[n][:], c_ps[n][:], op)
 
         wa_q = keep.tile([P, 2, 4, P], U32, name="wa_q", align_bytes=64)
         wa_s = keep.tile([P, 2, 4, P], U8, name="wa_s", align_bytes=64)
+        wa_bf = {}
 
-        def prepare_wa():
-            for a in range(2):
-                wa_bf = keep.tile([P, 4, P, 4], BF16, name="wa_bf%d" % a, align_bytes=64)
-                for t in range(4):
-                    dst = wa_bf[:, t, :, :].rearrange("p (q i) j -> p q i j", i=8)
-                    src = wa_raw[a].rearrange("p j (q t i) -> p t q i j", t=4, i=8)[:, t]
-                    if a == 0:
-                        nc.gpsimd.tensor_scalar(dst, src, 1.0, 1.0, MULT, MULT)
-                        continue
-                    dst = dst.rearrange("p q (u e) j -> p q u j e", e=2)
-                    src = src.rearrange("p q (u e) j -> p q u j e", e=2)
-                    if t == 3:
-                        nc.vector.tensor_copy(dst, src)
-                    else:
-                        nc.scalar.copy(dst, src)
-                nc.vector.quantize_mx(
-                    wa_q[:, a].rearrange("p t m -> p (t m)").bitcast(FP8X4),
-                    wa_s[:, a].rearrange("p t m -> p (t m)"),
-                    wa_bf[:].rearrange("p t m j -> p (t m j)"),
-                )
+        def round_wa(a):
+            wa_bf[a] = keep.tile([P, 4, P, 4], BF16, name="wa_bf%d" % a, align_bytes=64)
+            for t in range(4):
+                dst = wa_bf[a][:, t, :, :].rearrange("p (q i) j -> p q i j", i=8)
+                src = wa_raw[a][:].rearrange("p j (q t i) -> p t q i j", t=4, i=8)[:, t]
+                if t >= 2:
+                    nc.gpsimd.tensor_scalar(dst, src, 1.0, 1.0, MULT, MULT)
+                else:
+                    nc.scalar.copy(
+                        dst.rearrange("p q (u e) j -> p q u j e", e=2), src.rearrange("p q (u e) j -> p q u j e", e=2)
+                    )
+
+        def quantise_wa(a):
+            nc.vector.quantize_mx(
+                wa_q[:, a].rearrange("p t m -> p (t m)").bitcast(FP8X4),
+                wa_s[:, a].rearrange("p t m -> p (t m)"),
+                wa_bf[a][:].rearrange("p t m j -> p (t m j)"),
+            )
 
         we_q = keep.tile([P, 2, 4, P], U32, name="we_q", align_bytes=64)
         we_s = keep.tile([P, 2, 4, P], U8, name="we_s", align_bytes=64)
 
-        def prepare_we(g):
-            we_bf = keep.tile([P, 4, P, 4], BF16, name="we_bf%d" % g, align_bytes=64)
-            for m0 in range(0, P, 32):
-                dst = we_bf[:, :, m0 : m0 + 32, :].rearrange("p t m s -> p m t s")
-                src = we_raw[g][:, :, 4 * m0 : 4 * (m0 + 32)].rearrange("p s (m t) -> p m t s", t=4)
-                nc.scalar.copy(dst, src)
+        def round_we():
+            we_bf = late.tile([P, 2, 4, P, 4], BF16, name="we_bf", offset=RAW, align_bytes=64)
+            for g in range(2):
+                for m0 in range(0, P, 32):
+                    dst = we_bf[:, g, :, m0 : m0 + 32, :].rearrange("p t m s -> p m t s")
+                    src = we_raw[g][:, :, 4 * m0 : 4 * (m0 + 32)].rearrange("p s (m t) -> p m t s", t=4)
+                    if g == 0 or m0 >= 96:
+                        nc.scalar.copy(dst, src)
+                    else:
+                        nc.gpsimd.tensor_scalar(dst, src, 1.0, 1.0, MULT, MULT)
+            return we_bf
+
+        def quantise_we(we_bf, g):
             nc.vector.quantize_mx(
                 we_q[:, g].rearrange("p t m -> p (t m)").bitcast(FP8X4),
                 we_s[:, g].rearrange("p t m -> p (t m)"),
-                we_bf[:].rearrange("p t m j -> p (t m j)"),
+                we_bf[:, g].rearrange("p t m j -> p (t m j)"),
             )
 
-        def product(tag, codes, scales, j):
-            bank = psum.tile([P, 4, CH], F32, name=tag, tag=tag)
-            for t in range(4):
-                for a in range(2):
-                    nc.tensor.matmul_mx(
-                        bank[:, t, :],
-                        lhsT=codes(a, t),
-                        lhsT_scale=scales(a, t),
-                        rhs=picked(a, j).bitcast(FP8X4),
-                        rhs_scale=vscale[:, a, j : j + CH],
-                        start=(a == 0),
-                        stop=(a == 1),
-                    )
-            return bank[:].rearrange("p t (u e) -> p u t e", e=2)
+        starts = [sum(BATCHES[:i]) for i in range(len(BATCHES))]
+        used = {"a": 0, "y": 0}
 
-        y_s = keep.tile([P, 2, S], U8, name="y_s", align_bytes=64)
-        y_rows = out_0.rearrange("(g p t) j -> g p t j", p=P, t=4)
-        y_words = out_1.rearrange("g p m t -> p g (m t)").bitcast(I32)
+        def next_bank(kind, banks):
+            used[kind] = used[kind] + 1
+            return bank_tile(banks[(used[kind] - 1) % len(banks)])
 
-        starts = [sum(GROUPS[:i]) for i in range(len(GROUPS))]
-        lo = keep.tile([P, S // 2, 4, 2], F32, name="lo")
-        mid = keep.tile([P, S // 2, 4, 2], F32, name="mid")
-        pairs = {}
-        his = {}
+        def clip(i):
+            j0, w = starts[i], BATCHES[i]
+            h, c0 = divmod(j0, HALF)
+            per_bank = 512 // w
+            mid = ring.tile([P, 4, w], F32, name="mid", tag="mid")
+            for t0 in range(0, 4, per_bank):
+                bank = next_bank("a", A_BANKS)[:].rearrange("p (u j) -> p u j", u=per_bank)
+                for u in range(per_bank):
+                    t = t0 + u
+                    product(bank[:, u, :], lambda a: wa_q[:, a, t, :].bitcast(FP8X4), lambda a: wa_s[:, a, t, :], j0, w)
+                nc.vector.tensor_tensor(mid[:, t0 : t0 + per_bank, :], hi[h][:, t0 : t0 + per_bank, c0 : c0 + w], bank, MIN)
+            return mid
 
-        def lower(j):
-            b_ps = product("b", lambda a, t: wb_p[:, a, t, :].bitcast(FP8X4), lambda a, t: wb_s[:, a, t, :], j)
-            c_ps = product("c", lambda a, t: wc_p[:, a, t, :].bitcast(FP4X4), lambda a, t: wc_s[:, a, t, :], j)
-            b_sb = ring.tile([P, CH // 2, 4, 2], F32, name="b_sb", tag="b_sb", bufs=2)
-            nc.scalar.activation(b_sb[:], b_ps, IDENT)
-            nc.vector.tensor_tensor(lo[:, j // 2 : (j + CH) // 2], b_sb[:], c_ps, MIN)
-            pairs[j] = (b_sb, c_ps)
-
-        def upper(j):
-            b_sb, c_ps = pairs[j]
-            hi = ring.tile([P, CH // 2, 4, 2], F32, name="hi", tag="hi", bufs=4)
-            nc.vector.tensor_tensor(hi[:], b_sb[:], c_ps, MAX)
-            his[j] = hi
-
-        def clip(j):
-            a_ps = product("a", lambda a, t: wa_q[:, a, t, :].bitcast(FP8X4), lambda a, t: wa_s[:, a, t, :], j)
-            nc.vector.tensor_tensor(mid[:, j // 2 : (j + CH) // 2], his[j][:], a_ps, MIN)
-
-        def median(j0, w):
+        def median(i, mid):
+            j0, w = starts[i], BATCHES[i]
+            h, c0 = divmod(j0, HALF)
             h_bf = ring.tile([P, w, 4], BF16, name="h_bf", tag="h_bf", align_bytes=64)
-            span = slice(j0 // 2, (j0 + w) // 2)
-            nc.vector.tensor_tensor(h_bf[:].rearrange("p (u e) t -> p u t e", e=2), lo[:, span], mid[:, span], MAX)
-            return h_bf
-
-        def quantise_h(h_bf, w):
+            nc.vector.tensor_tensor(
+                h_bf[:].rearrange("p (u e) t -> p u t e", e=2),
+                lo[h][:, :, c0 : c0 + w].rearrange("p t (u e) -> p u t e", e=2),
+                mid[:].rearrange("p t (u e) -> p u t e", e=2),
+                MAX,
+            )
             h_q = ring.tile([P, w], U32, name="h_q", tag="h_q", align_bytes=64, bufs=3)
             h_s = ring.tile([P, w], U8, name="h_s", tag="h_s", align_bytes=64, bufs=3)
             nc.vector.quantize_mx(h_q[:].bitcast(FP8X4), h_s[:], h_bf[:].rearrange("p j t -> p (j t)"))
             return h_q, h_s
 
-        def estimate(j0, w, h_q, h_s):
-            rounded = []
-            for g in range(2):
-                y = ring.tile([P, 4, w], F32, name="y", tag="y", bufs=6)
-                per_bank = 512 // w
-                for t0 in range(0, 4, per_bank):
-                    bank = psum.tile([P, per_bank, w], F32, name="ybank", tag="ybank")
-                    for u in range(per_bank):
-                        nc.tensor.matmul_mx(
-                            bank[:, u, :],
-                            lhsT=we_q[:, g, t0 + u, :].bitcast(FP8X4),
-                            lhsT_scale=we_s[:, g, t0 + u, :],
-                            rhs=h_q[:].bitcast(FP8X4),
-                            rhs_scale=h_s[:],
-                            start=True,
-                            stop=True,
-                        )
-                    for u in range(per_bank):
-                        column = bias[:, g, t0 + u : t0 + u + 1]
-                        if g == 1 and j0 + w == S:
-                            nc.vector.tensor_scalar(y[:, t0 + u, :], bank[:, u, :], column, None, ADD)
-                        else:
-                            nc.scalar.activation(y[:, t0 + u, :], bank[:, u, :], IDENT, bias=column)
-                nc.sync.dma_start(y_rows[g][:, :, j0 : j0 + w], y[:])
-                y_bf = ring.tile([P, w, 4], BF16, name="y_bf", tag="y_bf", align_bytes=64, bufs=6)
-                if g == 0:
-                    nc.scalar.copy(y_bf[:].rearrange("p (u e) t -> p u t e", e=2), y[:].rearrange("p t (u e) -> p u t e", e=2))
-                rounded.append((y, y_bf))
-            return rounded
+        y_s = keep.tile([P, 2, S], U8, name="y_s", align_bytes=64)
+        y_rows = out_0.rearrange("(g p t) j -> g p t j", p=P, t=4)
+        y_words = out_1.rearrange("g p m t -> p g (m t)").bitcast(I32)
+        ys = {}
+        y_bf = {}
 
-        def planes(j0, w, rounded):
-            y_q = ring.tile([P, 2, w], U32, name="y_q", tag="y_q", align_bytes=64, bufs=3)
-            y, y_bf = rounded[1]
-            nc.vector.tensor_copy(y_bf[:].rearrange("p (u e) t -> p u t e", e=2), y[:].rearrange("p t (u e) -> p u t e", e=2))
+        def round_y(copy, i, g):
+            w = BATCHES[i]
+            y_bf[i, g] = keep.tile([P, w, 4], BF16, name="y_bf%d_%d" % (i, g), align_bytes=64)
+            copy(
+                y_bf[i, g][:].rearrange("p (u e) t -> p u t e", e=2), ys[i, g][:].rearrange("p t (u e) -> p u t e", e=2)
+            )
+
+        def estimate(i, g, h_q, h_s):
+            j0, w = starts[i], BATCHES[i]
+            per_bank = 512 // w
+            y = keep.tile([P, 4, w], F32, name="y%d_%d" % (i, g))
+            for t0 in range(0, 4, per_bank):
+                bank = next_bank("y", Y_BANKS[j0 // HALF])[:].rearrange("p (u j) -> p u j", u=per_bank)
+                for u in range(per_bank):
+                    nc.tensor.matmul_mx(
+                        bank[:, u, :],
+                        lhsT=we_q[:, g, t0 + u, :].bitcast(FP8X4),
+                        lhsT_scale=we_s[:, g, t0 + u, :],
+                        rhs=h_q[:].bitcast(FP8X4),
+                        rhs_scale=h_s[:],
+                        start=True,
+                        stop=True,
+                    )
+                for u in range(per_bank):
+                    nc.scalar.activation(y[:, t0 + u, :], bank[:, u, :], IDENT, bias=bias[:, g, t0 + u : t0 + u + 1])
+            nc.sync.dma_start(y_rows[g][:, :, j0 : j0 + w], y[:])
+            ys[i, g] = y
+
+        def y_planes(i):
+            j0, w = starts[i], BATCHES[i]
+            y_q = keep.tile([P, 2, w], U32, name="y_q%d" % i, align_bytes=64)
+            for g in range(2):
+                if (i, g) not in SCALAR_ROUNDS:
+                    round_y(nc.vector.tensor_copy, i, g)
             for g in range(2):
                 nc.vector.quantize_mx(
-                    y_q[:, g, :].bitcast(FP8X4), y_s[:, g, j0 : j0 + w], rounded[g][1][:].rearrange("p j t -> p (j t)")
+                    y_q[:, g, :].bitcast(FP8X4), y_s[:, g, j0 : j0 + w], y_bf[i, g][:].rearrange("p j t -> p (j t)")
                 )
             nc.sync.dma_start(y_words[:, :, j0 : j0 + w], y_q[:].bitcast(I32))
 
-        for j in range(0, LEAD, CH):
-            lower(j)
-            upper(j)
-        prepare_wa()
-        behind = None
-        for i, (j0, w) in enumerate(zip(starts, GROUPS)):
-            ahead = LEAD + CH * i
-            for j in range(j0, j0 + w, CH):
-                clip(j)
-            if ahead < S:
-                lower(ahead)
+        for n in range(4):
+            channel_b(n)
+            channel_c(n)
+            if n < 3:
+                bound(n, lo, MIN)
+                bound(n, hi, MAX)
+        for a in range(2):
+            round_wa(a)
+        quantise_wa(0)
+        bound(3, lo, MIN)
+        quantise_wa(1)
+        bound(3, hi, MAX)
+        we_bf = round_we()
+        for n in range(4, 8):
+            channel_b(n)
+        mids = {0: clip(0)}
+        quantise_we(we_bf, 0)
+        for i, j0 in enumerate(starts):
+            h_mx = median(i, mids[i])
+            estimate(i, 0, *h_mx)
+            if i + 1 < len(BATCHES):
+                if starts[i + 1] == HALF:
+                    for n in range(4, 8):
+                        channel_c(n)
+                        bound(n, lo, MIN)
+                        bound(n, hi, MAX)
+                mids[i + 1] = clip(i + 1)
             if i == 0:
-                prepare_we(0)
-            h_bf = median(j0, w)
-            if ahead < S:
-                upper(ahead)
-            if i == 0:
-                prepare_we(1)
-            h_mx = quantise_h(h_bf, w)
-            if behind is not None:
-                planes(*behind)
-            behind = (j0, w, estimate(j0, w, *h_mx))
-        planes(*behind)
+                quantise_we(we_bf, 1)
+            estimate(i, 1, *h_mx)
+            for g in range(2):
+                if (i, g) in SCALAR_ROUNDS:
+                    round_y(nc.scalar.copy, i, g)
+            if i >= LAG - 1 and i + 1 < len(BATCHES):
+                y_planes(i - LAG + 1)
+        for i in range(len(BATCHES) - LAG, len(BATCHES)):
+            y_planes(i)
         for q in range(4):
             (nc.scalar if q % 2 else nc.sync).dma_start(
                 out_2[:, 4 * q : 4 * q + 4, :].rearrange("g r m -> r g m").bitcast(I32),

@@ -20,14 +20,14 @@ IDENT = mybir.ActivationFunctionType.Identity
 
 P = 128
 HALF = 512
-BATCHES = [256, 256, 256, 128, 128]
-SCALAR_ROUNDS = [(0, 0), (0, 1), (1, 0), (1, 1), (2, 0)]
-B_BANKS = [0, 1, 5, 6, 7, 0, 1, 7]
+BATCHES = [128, 128, 256, 256, 128, 128]
+SCALAR_ROUNDS = [(i, g) for i in range(4) for g in range(2)]
+B_BANKS = [0, 1, 5, 6, 7, 0, 1, 3]
 C_BANKS = [2, 3, 4]
-A_BANKS = [6, 5]
-Y_BANKS = [[0, 1, 7], [0, 1, 7, 2, 3, 4]]
+A_BANKS = [5, 6, 2]
+Y_BANKS = [4, 7, 0, 1, 3]
 RAW = 4 * 512 * 4
-LAG = 2
+LAG = 4
 
 
 def tile_list_triplex_median_vote_kernel(
@@ -109,6 +109,12 @@ def tile_list_triplex_median_vote_kernel(
         def bank_tile(n):
             return psum.tile([P, 512], F32, name="bank%d" % n, tag="bank%d" % n)
 
+        used = {"a": 0, "y": 0}
+
+        def next_bank(kind, banks):
+            used[kind] = used[kind] + 1
+            return bank_tile(banks[(used[kind] - 1) % len(banks)])
+
         def product(out, codes, scales, j, w):
             for a in range(2):
                 nc.tensor.matmul_mx(
@@ -135,8 +141,9 @@ def tile_list_triplex_median_vote_kernel(
 
         b_sb = {}
         c_ps = {}
-        lo = [keep.tile([P, 4, HALF], F32, name="lo%d" % h) for h in range(2)]
-        hi = [keep.tile([P, 4, HALF], F32, name="hi%d" % h) for h in range(2)]
+        lo = {0: keep.tile([P, 4, HALF], F32, name="lo_first")}
+        hi = {0: keep.tile([P, 4, HALF], F32, name="hi_first")}
+        b_second = keep.tile([P, 4, HALF], F32, name="b_second")
 
         def channel_b(n):
             h, t = divmod(n, 4)
@@ -148,8 +155,8 @@ def tile_list_triplex_median_vote_kernel(
                 h * HALF,
                 HALF,
             )
-            b_sb[n] = keep.tile([P, HALF], F32, name="b_sb%d" % n)
-            nc.scalar.activation(b_sb[n][:], bank[:], IDENT)
+            b_sb[n] = keep.tile([P, HALF], F32, name="b_sb%d" % n)[:] if h == 0 else b_second[:, t, :]
+            nc.scalar.activation(b_sb[n], bank[:], IDENT)
 
         def channel_c(n):
             h, t = divmod(n, 4)
@@ -164,7 +171,7 @@ def tile_list_triplex_median_vote_kernel(
 
         def bound(n, dst, op):
             h, t = divmod(n, 4)
-            nc.vector.tensor_tensor(dst[h][:, t, :], b_sb[n][:], c_ps[n][:], op)
+            nc.vector.tensor_tensor(dst[h][:, t, :], b_sb[n], c_ps[n][:], op)
 
         wa_q = keep.tile([P, 2, 4, P], U32, name="wa_q", align_bytes=64)
         wa_s = keep.tile([P, 2, 4, P], U8, name="wa_s", align_bytes=64)
@@ -193,12 +200,14 @@ def tile_list_triplex_median_vote_kernel(
         we_s = keep.tile([P, 2, 4, P], U8, name="we_s", align_bytes=64)
 
         def round_we():
-            we_bf = late.tile([P, 2, 4, P, 4], BF16, name="we_bf", offset=RAW, align_bytes=64)
+            we_bf = [
+                late.tile([P, 4, P, 4], BF16, name="we_bf%d" % g, offset=RAW + g * RAW // 2, align_bytes=64) for g in range(2)
+            ]
             for g in range(2):
                 for m0 in range(0, P, 32):
-                    dst = we_bf[:, g, :, m0 : m0 + 32, :].rearrange("p t m s -> p m t s")
+                    dst = we_bf[g][:, :, m0 : m0 + 32, :].rearrange("p t m s -> p m t s")
                     src = we_raw[g][:, :, 4 * m0 : 4 * (m0 + 32)].rearrange("p s (m t) -> p m t s", t=4)
-                    if g == 0 or m0 >= 96:
+                    if g == 0:
                         nc.scalar.copy(dst, src)
                     else:
                         nc.gpsimd.tensor_scalar(dst, src, 1.0, 1.0, MULT, MULT)
@@ -208,19 +217,35 @@ def tile_list_triplex_median_vote_kernel(
             nc.vector.quantize_mx(
                 we_q[:, g].rearrange("p t m -> p (t m)").bitcast(FP8X4),
                 we_s[:, g].rearrange("p t m -> p (t m)"),
-                we_bf[:, g].rearrange("p t m j -> p (t m j)"),
+                we_bf[g][:].rearrange("p t m j -> p (t m j)"),
             )
 
         starts = [sum(BATCHES[:i]) for i in range(len(BATCHES))]
-        used = {"a": 0, "y": 0}
+        def span(tiles, i):
+            if starts[i] < HALF:
+                return tiles[0][:, :, starts[i] : starts[i] + BATCHES[i]]
+            return tiles[i][:]
 
-        def next_bank(kind, banks):
-            used[kind] = used[kind] + 1
-            return bank_tile(banks[(used[kind] - 1) % len(banks)])
+        def late_bounds(i):
+            j0, w = starts[i], BATCHES[i]
+            lo[i] = keep.tile([P, 4, w], F32, name="lo%d" % i)
+            hi[i] = keep.tile([P, 4, w], F32, name="hi%d" % i)
+            for c0 in range(0, w, P):
+                bank = next_bank("a", A_BANKS)[:].rearrange("p (t j) -> p t j", t=4)
+                for t in range(4):
+                    product(
+                        bank[:, t, :],
+                        lambda a: wc_p[:, a, t, :].bitcast(FP4X4),
+                        lambda a: planes[:, a, S + H + P * t : S + H + P * (t + 1)],
+                        j0 + c0,
+                        P,
+                    )
+                b = b_second[:, :, j0 - HALF + c0 : j0 - HALF + c0 + P]
+                nc.vector.tensor_tensor(hi[i][:, :, c0 : c0 + P], b, bank, MAX)
+                nc.vector.tensor_tensor(lo[i][:, :, c0 : c0 + P], b, bank, MIN)
 
         def clip(i):
             j0, w = starts[i], BATCHES[i]
-            h, c0 = divmod(j0, HALF)
             per_bank = 512 // w
             mid = ring.tile([P, 4, w], F32, name="mid", tag="mid")
             for t0 in range(0, 4, per_bank):
@@ -228,16 +253,15 @@ def tile_list_triplex_median_vote_kernel(
                 for u in range(per_bank):
                     t = t0 + u
                     product(bank[:, u, :], lambda a: wa_q[:, a, t, :].bitcast(FP8X4), lambda a: wa_s[:, a, t, :], j0, w)
-                nc.vector.tensor_tensor(mid[:, t0 : t0 + per_bank, :], hi[h][:, t0 : t0 + per_bank, c0 : c0 + w], bank, MIN)
+                nc.vector.tensor_tensor(mid[:, t0 : t0 + per_bank, :], span(hi, i)[:, t0 : t0 + per_bank, :], bank, MIN)
             return mid
 
         def median(i, mid):
-            j0, w = starts[i], BATCHES[i]
-            h, c0 = divmod(j0, HALF)
+            w = BATCHES[i]
             h_bf = ring.tile([P, w, 4], BF16, name="h_bf", tag="h_bf", align_bytes=64)
             nc.vector.tensor_tensor(
                 h_bf[:].rearrange("p (u e) t -> p u t e", e=2),
-                lo[h][:, :, c0 : c0 + w].rearrange("p t (u e) -> p u t e", e=2),
+                span(lo, i).rearrange("p t (u e) -> p u t e", e=2),
                 mid[:].rearrange("p t (u e) -> p u t e", e=2),
                 MAX,
             )
@@ -264,7 +288,7 @@ def tile_list_triplex_median_vote_kernel(
             per_bank = 512 // w
             y = keep.tile([P, 4, w], F32, name="y%d_%d" % (i, g))
             for t0 in range(0, 4, per_bank):
-                bank = next_bank("y", Y_BANKS[j0 // HALF])[:].rearrange("p (u j) -> p u j", u=per_bank)
+                bank = next_bank("y", Y_BANKS)[:].rearrange("p (u j) -> p u j", u=per_bank)
                 for u in range(per_bank):
                     nc.tensor.matmul_mx(
                         bank[:, u, :],
@@ -313,11 +337,8 @@ def tile_list_triplex_median_vote_kernel(
             h_mx = median(i, mids[i])
             estimate(i, 0, *h_mx)
             if i + 1 < len(BATCHES):
-                if starts[i + 1] == HALF:
-                    for n in range(4, 8):
-                        channel_c(n)
-                        bound(n, lo, MIN)
-                        bound(n, hi, MAX)
+                if starts[i + 1] >= HALF:
+                    late_bounds(i + 1)
                 mids[i + 1] = clip(i + 1)
             if i == 0:
                 quantise_we(we_bf, 1)

@@ -199,19 +199,19 @@ def tile_list_triplex_median_vote_kernel(
         we_q = keep.tile([P, 2, 4, P], U32, name="we_q", align_bytes=64)
         we_s = keep.tile([P, 2, 4, P], U8, name="we_s", align_bytes=64)
 
-        def round_we():
-            we_bf = [
-                late.tile([P, 4, P, 4], BF16, name="we_bf%d" % g, offset=RAW + g * RAW // 2, align_bytes=64) for g in range(2)
-            ]
-            for g in range(2):
-                for m0 in range(0, P, 32):
+        we_bf = [
+            late.tile([P, 4, P, 4], BF16, name="we_bf%d" % g, offset=RAW + g * RAW // 2, align_bytes=64) for g in range(2)
+        ]
+
+        def round_we(pieces):
+            for g, first, last in pieces:
+                for m0 in range(first, last, 32):
                     dst = we_bf[g][:, :, m0 : m0 + 32, :].rearrange("p t m s -> p m t s")
                     src = we_raw[g][:, :, 4 * m0 : 4 * (m0 + 32)].rearrange("p s (m t) -> p m t s", t=4)
-                    if g == 0:
+                    if g == 0 or m0 >= 64:
                         nc.scalar.copy(dst, src)
                     else:
-                        nc.gpsimd.tensor_scalar(dst, src, 1.0, 1.0, MULT, MULT)
-            return we_bf
+                        nc.vector.tensor_copy(dst, src)
 
         def quantise_we(we_bf, g):
             nc.vector.quantize_mx(
@@ -328,7 +328,7 @@ def tile_list_triplex_median_vote_kernel(
         bound(3, lo, MIN)
         quantise_wa(1)
         bound(3, hi, MAX)
-        we_bf = round_we()
+        round_we([(0, 0, P), (1, 64, P)])
         for n in range(4, 8):
             channel_b(n)
         mids = {0: clip(0)}
@@ -341,6 +341,7 @@ def tile_list_triplex_median_vote_kernel(
                     late_bounds(i + 1)
                 mids[i + 1] = clip(i + 1)
             if i == 0:
+                round_we([(1, 0, 64)])
                 quantise_we(we_bf, 1)
             estimate(i, 1, *h_mx)
             for g in range(2):

@@ -66,13 +66,13 @@ def tile_list_triplex_median_vote_kernel(
 
         vsc = late.tile([P, 4 * RAW + 64], U8, name="vsc", offset=0, align_bytes=64)
         nc.vector.tensor_copy(vsc[:, 0:S], tsc[:].indirect(offsets[:]))
-        staged = keep.tile([P, S + 2 * H], U8, name="staged", align_bytes=64)
+        staged = keep.tile([32, S + 2 * H], U8, name="staged", align_bytes=64)
         for n, raw in enumerate(wsr):
             nc.gpsimd.tensor_copy(
-                staged[0:32, S + n * H : S + (n + 1) * H].bitcast(I32).rearrange("p (t q i) -> p q t i", t=4, i=2),
+                staged[:, S + n * H : S + (n + 1) * H].bitcast(I32).rearrange("p (t q i) -> p q t i", t=4, i=2),
                 raw[:].bitcast(I32).rearrange("p (q t i) -> p q t i", t=4, i=2),
             )
-        nc.vector.tensor_copy(staged[:, 0:S].bitcast(I32), vsc[:, 0:S].bitcast(I32))
+        nc.vector.tensor_copy(staged[:, 0:S].bitcast(I32), vsc[0:32, 0:S].bitcast(I32))
         for q in range(4):
             nc.sync.dma_start(planes[32 * q : 32 * q + 4, :, :].bitcast(I32), staged[8 * q : 8 * q + 8, :].bitcast(I32))
 
@@ -126,18 +126,6 @@ def tile_list_triplex_median_vote_kernel(
                     start=(a == 0),
                     stop=(a == 1),
                 )
-
-        idle = bank_tile(7)
-        for n in range(4):
-            nc.tensor.matmul_mx(
-                idle[:],
-                lhsT=vw[0, 0][:, 0:P].bitcast(FP8X4),
-                lhsT_scale=staged[:, 0:P],
-                rhs=vw[0, 0][:].bitcast(FP8X4),
-                rhs_scale=staged[:, 0:HALF],
-                start=True,
-                stop=True,
-            )
 
         b_sb = {}
         c_ps = {}

@@ -21,13 +21,15 @@ IDENT = mybir.ActivationFunctionType.Identity
 P = 128
 HALF = 512
 BATCHES = [128, 128, 256, 256, 128, 128]
-SCALAR_ROUNDS = [(i, g) for i in range(4) for g in range(2)]
-B_BANKS = [0, 1, 5, 6, 7, 0, 1, 3]
+B_BANKS = [0, 1, 5, 6, 7, 3, 4, 2]
 C_BANKS = [2, 3, 4]
-A_BANKS = [5, 6, 2]
-Y_BANKS = [4, 7, 0, 1, 3]
+A_BANKS = [5, 6, 0, 1]
+Y_BANKS = [7, 3, 4, 2]
 RAW = 4 * 512 * 4
-LAG = 4
+KB = 1024
+WA_BF_AT = 4 * RAW + 64
+BOUND_AT = {3: (0, 4 * KB), 4: (4 * KB, 6 * KB), 5: (5 * KB, 7 * KB)}
+H_AT = [0, 1 * KB, 3 * KB, 6 * KB, 8 * KB, 10 * KB]
 
 
 def tile_list_triplex_median_vote_kernel(
@@ -38,6 +40,8 @@ def tile_list_triplex_median_vote_kernel(
         keep = ctx.enter_context(tc.tile_pool(name="keep", bufs=1))
         late = ctx.enter_context(tc.tile_pool(name="late", bufs=1))
         ring = ctx.enter_context(tc.tile_pool(name="ring", bufs=2))
+        bnd = ctx.enter_context(tc.tile_pool(name="bnd", bufs=1))
+        rnd = ctx.enter_context(tc.tile_pool(name="rnd", bufs=1))
         psum = ctx.enter_context(tc.psum_pool(name="psum", bufs=1))
 
         offsets = keep.tile([P, S // 16], U16, name="offsets")
@@ -129,7 +133,7 @@ def tile_list_triplex_median_vote_kernel(
 
         b_sb = {}
         c_ps = {}
-        lo = {0: keep.tile([P, 4, HALF], F32, name="lo_first")}
+        lo = {0: bnd.tile([P, 4, HALF], F32, name="lo_first", offset=0)}
         hi = {0: keep.tile([P, 4, HALF], F32, name="hi_first")}
         b_second = keep.tile([P, 4, HALF], F32, name="b_second")
 
@@ -166,7 +170,7 @@ def tile_list_triplex_median_vote_kernel(
         wa_bf = {}
 
         def round_wa(a):
-            wa_bf[a] = keep.tile([P, 4, P, 4], BF16, name="wa_bf%d" % a, align_bytes=64)
+            wa_bf[a] = late.tile([P, 4, P, 4], BF16, name="wa_bf%d" % a, offset=WA_BF_AT + a * RAW // 2, align_bytes=64)
             for t in range(4):
                 dst = wa_bf[a][:, t, :, :].rearrange("p (q i) j -> p q i j", i=8)
                 src = wa_raw[a][:].rearrange("p j (q t i) -> p t q i j", t=4, i=8)[:, t]
@@ -187,25 +191,18 @@ def tile_list_triplex_median_vote_kernel(
         we_q = keep.tile([P, 2, 4, P], U32, name="we_q", align_bytes=64)
         we_s = keep.tile([P, 2, 4, P], U8, name="we_s", align_bytes=64)
 
-        we_bf = [
-            late.tile([P, 4, P, 4], BF16, name="we_bf%d" % g, offset=RAW + g * RAW // 2, align_bytes=64) for g in range(2)
-        ]
+        we_bf = {}
 
-        def round_we(pieces):
-            for g, first, last in pieces:
-                for m0 in range(first, last, 32):
-                    dst = we_bf[g][:, :, m0 : m0 + 32, :].rearrange("p t m s -> p m t s")
-                    src = we_raw[g][:, :, 4 * m0 : 4 * (m0 + 32)].rearrange("p s (m t) -> p m t s", t=4)
-                    if g == 0 or m0 >= 64:
-                        nc.scalar.copy(dst, src)
-                    else:
-                        nc.vector.tensor_copy(dst, src)
+        def round_we(copy, g, half, at):
+            we_bf[g, half] = late.tile([P, 2, P, 4], BF16, name="we_bf%d_%d" % (g, half), offset=at, align_bytes=64)
+            src = we_raw[g][:].rearrange("p s (m t) -> p m s t", t=4)[:, :, :, 2 * half : 2 * half + 2]
+            copy(we_bf[g, half][:].rearrange("p t m s -> p m s t"), src)
 
-        def quantise_we(we_bf, g):
+        def quantise_we(g, half):
             nc.vector.quantize_mx(
-                we_q[:, g].rearrange("p t m -> p (t m)").bitcast(FP8X4),
-                we_s[:, g].rearrange("p t m -> p (t m)"),
-                we_bf[g][:].rearrange("p t m j -> p (t m j)"),
+                we_q[:, g, 2 * half : 2 * half + 2].rearrange("p t m -> p (t m)").bitcast(FP8X4),
+                we_s[:, g, 2 * half : 2 * half + 2].rearrange("p t m -> p (t m)"),
+                we_bf[g, half][:].rearrange("p t m j -> p (t m j)"),
             )
 
         starts = [sum(BATCHES[:i]) for i in range(len(BATCHES))]
@@ -216,8 +213,8 @@ def tile_list_triplex_median_vote_kernel(
 
         def late_bounds(i):
             j0, w = starts[i], BATCHES[i]
-            lo[i] = keep.tile([P, 4, w], F32, name="lo%d" % i)
-            hi[i] = keep.tile([P, 4, w], F32, name="hi%d" % i)
+            hi[i] = bnd.tile([P, 4, w], F32, name="hi%d" % i, offset=BOUND_AT[i][0])
+            lo[i] = bnd.tile([P, 4, w], F32, name="lo%d" % i, offset=BOUND_AT[i][1])
             for c0 in range(0, w, P):
                 bank = next_bank("a", A_BANKS)[:].rearrange("p (t j) -> p t j", t=4)
                 for t in range(4):
@@ -235,24 +232,36 @@ def tile_list_triplex_median_vote_kernel(
         def clip(i):
             j0, w = starts[i], BATCHES[i]
             per_bank = 512 // w
-            mid = ring.tile([P, 4, w], F32, name="mid", tag="mid")
+            mid = ring.tile([P, 4, w], F32, name="mid", tag="mid", bufs=3)
             for t0 in range(0, 4, per_bank):
                 bank = next_bank("a", A_BANKS)[:].rearrange("p (u j) -> p u j", u=per_bank)
-                for u in range(per_bank):
-                    t = t0 + u
-                    product(bank[:, u, :], lambda a: wa_q[:, a, t, :].bitcast(FP8X4), lambda a: wa_s[:, a, t, :], j0, w)
+                for a in range(2):
+                    for u in range(per_bank):
+                        nc.tensor.matmul_mx(
+                            bank[:, u, :],
+                            lhsT=wa_q[:, a, t0 + u, :].bitcast(FP8X4),
+                            lhsT_scale=wa_s[:, a, t0 + u, :],
+                            rhs=picked(a, j0, w).bitcast(FP8X4),
+                            rhs_scale=planes[:, a, j0 : j0 + w],
+                            start=(a == 0 and u == 0),
+                            stop=(a == 1 and u == per_bank - 1),
+                        )
                 nc.vector.tensor_tensor(mid[:, t0 : t0 + per_bank, :], span(hi, i)[:, t0 : t0 + per_bank, :], bank, MIN)
             return mid
 
         def median(i, mid):
             w = BATCHES[i]
-            h_bf = ring.tile([P, w, 4], BF16, name="h_bf", tag="h_bf", align_bytes=64)
+            h_bf = rnd.tile([P, w, 4], BF16, name="h_bf%d" % i, offset=H_AT[i], align_bytes=64)
             nc.vector.tensor_tensor(
                 h_bf[:].rearrange("p (u e) t -> p u t e", e=2),
                 span(lo, i).rearrange("p t (u e) -> p u t e", e=2),
                 mid[:].rearrange("p t (u e) -> p u t e", e=2),
                 MAX,
             )
+            return h_bf
+
+        def quantise_h(i, h_bf):
+            w = BATCHES[i]
             h_q = ring.tile([P, w], U32, name="h_q", tag="h_q", align_bytes=64, bufs=3)
             h_s = ring.tile([P, w], U8, name="h_s", tag="h_s", align_bytes=64, bufs=3)
             nc.vector.quantize_mx(h_q[:].bitcast(FP8X4), h_s[:], h_bf[:].rearrange("p j t -> p (j t)"))
@@ -261,20 +270,35 @@ def tile_list_triplex_median_vote_kernel(
         y_s = keep.tile([P, 2, S], U8, name="y_s", align_bytes=64)
         y_rows = out_0.rearrange("(g p t) j -> g p t j", p=P, t=4)
         y_words = out_1.rearrange("g p m t -> p g (m t)").bitcast(I32)
+        joint = [keep.tile([P, 2, 4, w], F32, name="y%d" % i) for i, w in enumerate(BATCHES[:2])]
         ys = {}
+        for i, w in enumerate(BATCHES):
+            for g in range(2):
+                ys[i, g] = joint[i][:, g] if i < 2 else keep.tile([P, 4, w], F32, name="y%d_%d" % (i, g))[:]
+        y_q = [keep.tile([P, 2, w], U32, name="y_q%d" % i, align_bytes=64) for i, w in enumerate(BATCHES)]
         y_bf = {}
 
         def round_y(copy, i, g):
             w = BATCHES[i]
-            y_bf[i, g] = keep.tile([P, w, 4], BF16, name="y_bf%d_%d" % (i, g), align_bytes=64)
+            y_bf[i, g] = keep.tile([P, w, 4], BF16, name="y_bf%d_%d" % (i, g), align_bytes=64)[:]
             copy(
-                y_bf[i, g][:].rearrange("p (u e) t -> p u t e", e=2), ys[i, g][:].rearrange("p t (u e) -> p u t e", e=2)
+                y_bf[i, g].rearrange("p (u e) t -> p u t e", e=2), ys[i, g].rearrange("p t (u e) -> p u t e", e=2)
             )
+
+        def round_y_gpsimd(i, groups, at):
+            w = BATCHES[i]
+            dst = rnd.tile([P, len(groups), w, 4], BF16, name="y_bfg%d" % i, offset=at, align_bytes=64)
+            if len(groups) == 2:
+                nc.gpsimd.tensor_scalar(dst[:], joint[i][:].rearrange("p g t j -> p g j t"), 1.0, 1.0, MULT, MULT)
+            else:
+                nc.gpsimd.tensor_scalar(dst[:, 0], ys[i, groups[0]].rearrange("p t j -> p j t"), 1.0, 1.0, MULT, MULT)
+            for n, g in enumerate(groups):
+                y_bf[i, g] = dst[:, n]
 
         def estimate(i, g, h_q, h_s):
             j0, w = starts[i], BATCHES[i]
             per_bank = 512 // w
-            y = keep.tile([P, 4, w], F32, name="y%d_%d" % (i, g))
+            y = ys[i, g]
             for t0 in range(0, 4, per_bank):
                 bank = next_bank("y", Y_BANKS)[:].rearrange("p (u j) -> p u j", u=per_bank)
                 for u in range(per_bank):
@@ -289,20 +313,15 @@ def tile_list_triplex_median_vote_kernel(
                     )
                 for u in range(per_bank):
                     nc.scalar.activation(y[:, t0 + u, :], bank[:, u, :], IDENT, bias=bias[:, g, t0 + u : t0 + u + 1])
-            nc.sync.dma_start(y_rows[g][:, :, j0 : j0 + w], y[:])
-            ys[i, g] = y
+            nc.sync.dma_start(y_rows[g][:, :, j0 : j0 + w], y)
 
-        def y_planes(i):
+        def quantise_y(i, g):
             j0, w = starts[i], BATCHES[i]
-            y_q = keep.tile([P, 2, w], U32, name="y_q%d" % i, align_bytes=64)
-            for g in range(2):
-                if (i, g) not in SCALAR_ROUNDS:
-                    round_y(nc.vector.tensor_copy, i, g)
-            for g in range(2):
-                nc.vector.quantize_mx(
-                    y_q[:, g, :].bitcast(FP8X4), y_s[:, g, j0 : j0 + w], y_bf[i, g][:].rearrange("p j t -> p (j t)")
-                )
-            nc.sync.dma_start(y_words[:, :, j0 : j0 + w], y_q[:].bitcast(I32))
+            nc.vector.quantize_mx(
+                y_q[i][:, g, :].bitcast(FP8X4), y_s[:, g, j0 : j0 + w], y_bf[i, g].rearrange("p j t -> p (j t)")
+            )
+            if g == 1:
+                nc.sync.dma_start(y_words[:, :, j0 : j0 + w], y_q[i][:].bitcast(I32))
 
         for n in range(4):
             channel_b(n)
@@ -310,35 +329,59 @@ def tile_list_triplex_median_vote_kernel(
             if n < 3:
                 bound(n, lo, MIN)
                 bound(n, hi, MAX)
-        for a in range(2):
-            round_wa(a)
+            if n in (0, 2):
+                round_wa(n // 2)
         quantise_wa(0)
         bound(3, lo, MIN)
         quantise_wa(1)
         bound(3, hi, MAX)
-        round_we([(0, 0, P), (1, 64, P)])
+        round_we(nc.scalar.copy, 0, 0, RAW)
+        round_we(nc.vector.tensor_copy, 0, 1, WA_BF_AT + RAW // 2)
+        mids = {0: clip(0), 1: clip(1)}
+        round_we(nc.scalar.copy, 1, 0, RAW + 2 * KB)
+        round_we(nc.scalar.copy, 1, 1, RAW + 4 * KB)
         for n in range(4, 8):
             channel_b(n)
-        mids = {0: clip(0)}
-        quantise_we(we_bf, 0)
-        for i, j0 in enumerate(starts):
-            h_mx = median(i, mids[i])
+        h_bf = median(0, mids[0])
+        quantise_we(0, 0)
+        quantise_we(0, 1)
+        h_first = quantise_h(0, h_bf)
+        estimate(0, 0, *h_first)
+        mids[2] = clip(2)
+        planes_after = {3: [(0, 0), (0, 1), (1, 0), (1, 1)], 4: [(2, 0)], 5: [(2, 1), (3, 0)]}
+        for i in range(1, len(BATCHES)):
+            h_bf = median(i, mids[i])
+            if i == 1:
+                quantise_we(1, 0)
+                quantise_we(1, 1)
+            for piece in planes_after.get(i, []):
+                quantise_y(*piece)
+            h_mx = quantise_h(i, h_bf)
+            if i == 1:
+                estimate(0, 1, *h_first)
+            if i == 2:
+                round_y_gpsimd(0, [0, 1], 2 * KB)
+                round_y_gpsimd(1, [0, 1], 4 * KB)
+            if i == 3:
+                round_y_gpsimd(2, [0], 6 * KB)
+            if i == 4:
+                round_y_gpsimd(3, [0], 8 * KB)
             estimate(i, 0, *h_mx)
-            if i + 1 < len(BATCHES):
-                if starts[i + 1] >= HALF:
-                    late_bounds(i + 1)
+            if 2 <= i < len(BATCHES) - 1:
+                late_bounds(i + 1)
                 mids[i + 1] = clip(i + 1)
-            if i == 0:
-                round_we([(1, 0, 64)])
-                quantise_we(we_bf, 1)
             estimate(i, 1, *h_mx)
-            for g in range(2):
-                if (i, g) in SCALAR_ROUNDS:
-                    round_y(nc.scalar.copy, i, g)
-            if i >= LAG - 1 and i + 1 < len(BATCHES):
-                y_planes(i - LAG + 1)
-        for i in range(len(BATCHES) - LAG, len(BATCHES)):
-            y_planes(i)
+            if i in (2, 3):
+                round_y(nc.scalar.copy, i, 1)
+            if i == 4:
+                round_y(nc.scalar.copy, i, 0)
+                round_y(nc.scalar.copy, i, 1)
+        for piece in [(3, 1), (4, 0), (4, 1)]:
+            quantise_y(*piece)
+        for g in range(2):
+            round_y(nc.vector.tensor_copy, 5, g)
+        for g in range(2):
+            quantise_y(5, g)
         for q in range(4):
             (nc.scalar if q % 2 else nc.sync).dma_start(
                 out_2[:, 4 * q : 4 * q + 4, :].rearrange("g r m -> r g m").bitcast(I32),

@@ -100,11 +100,12 @@ def tile_list_triplex_median_vote_kernel(
             wc_p[:].bitcast(I32).rearrange("p a t (q i) -> p a q t i", i=4),
             wc_raw[:].rearrange("p a (q t i) -> p a q t i", t=4, i=4),
         )
-        vw = {}
-        for a in range(2):
-            for h in range(2):
-                vw[a, h] = keep.tile([P, HALF], U32, name="vw%d_%d" % (a, h), align_bytes=64)
-                nc.vector.tensor_copy(vw[a, h][:], tabw[a][:].indirect(offsets[:, h * HALF // 16 : (h + 1) * HALF // 16]))
+        vw_first = keep.tile([P, S], U32, name="vw_first", align_bytes=64)
+        nc.vector.tensor_copy(vw_first[:], tabw[0][:].indirect(offsets[:]))
+        vw = {(0, h): vw_first[:, h * HALF : (h + 1) * HALF] for h in range(2)}
+        for h in range(2):
+            vw[1, h] = keep.tile([P, HALF], U32, name="vw1_%d" % h, align_bytes=64)[:]
+            nc.vector.tensor_copy(vw[1, h], tabw[1][:].indirect(offsets[:, h * HALF // 16 : (h + 1) * HALF // 16]))
 
         def picked(a, j, w):
             h, c0 = divmod(j, HALF)
@@ -191,18 +192,21 @@ def tile_list_triplex_median_vote_kernel(
         we_q = keep.tile([P, 2, 4, P], U32, name="we_q", align_bytes=64)
         we_s = keep.tile([P, 2, 4, P], U8, name="we_s", align_bytes=64)
 
-        we_bf = {}
+        we_bf = [
+            late.tile([P, 4, P, 4], BF16, name="we_bf%d" % g, offset=RAW + g * RAW // 2, align_bytes=64) for g in range(2)
+        ]
 
-        def round_we(copy, g, half, at):
-            we_bf[g, half] = late.tile([P, 2, P, 4], BF16, name="we_bf%d_%d" % (g, half), offset=at, align_bytes=64)
-            src = we_raw[g][:].rearrange("p s (m t) -> p m s t", t=4)[:, :, :, 2 * half : 2 * half + 2]
-            copy(we_bf[g, half][:].rearrange("p t m s -> p m s t"), src)
+        def round_we(g):
+            for m0 in range(0, P, 64):
+                dst = we_bf[g][:, :, m0 : m0 + 64, :].rearrange("p t m s -> p m s t")
+                src = we_raw[g][:, :, 4 * m0 : 4 * (m0 + 64)].rearrange("p s (m t) -> p m s t", t=4)
+                nc.scalar.copy(dst, src)
 
-        def quantise_we(g, half):
+        def quantise_we(g):
             nc.vector.quantize_mx(
-                we_q[:, g, 2 * half : 2 * half + 2].rearrange("p t m -> p (t m)").bitcast(FP8X4),
-                we_s[:, g, 2 * half : 2 * half + 2].rearrange("p t m -> p (t m)"),
-                we_bf[g, half][:].rearrange("p t m j -> p (t m j)"),
+                we_q[:, g].rearrange("p t m -> p (t m)").bitcast(FP8X4),
+                we_s[:, g].rearrange("p t m -> p (t m)"),
+                we_bf[g][:].rearrange("p t m j -> p (t m j)"),
             )
 
         starts = [sum(BATCHES[:i]) for i in range(len(BATCHES))]
@@ -275,7 +279,6 @@ def tile_list_triplex_median_vote_kernel(
         for i, w in enumerate(BATCHES):
             for g in range(2):
                 ys[i, g] = joint[i][:, g] if i < 2 else keep.tile([P, 4, w], F32, name="y%d_%d" % (i, g))[:]
-        y_q = [keep.tile([P, 2, w], U32, name="y_q%d" % i, align_bytes=64) for i, w in enumerate(BATCHES)]
         y_bf = {}
 
         def round_y(copy, i, g):
@@ -285,15 +288,18 @@ def tile_list_triplex_median_vote_kernel(
                 y_bf[i, g].rearrange("p (u e) t -> p u t e", e=2), ys[i, g].rearrange("p t (u e) -> p u t e", e=2)
             )
 
-        def round_y_gpsimd(i, groups, at):
-            w = BATCHES[i]
-            dst = rnd.tile([P, len(groups), w, 4], BF16, name="y_bfg%d" % i, offset=at, align_bytes=64)
-            if len(groups) == 2:
-                nc.gpsimd.tensor_scalar(dst[:], joint[i][:].rearrange("p g t j -> p g j t"), 1.0, 1.0, MULT, MULT)
-            else:
-                nc.gpsimd.tensor_scalar(dst[:, 0], ys[i, groups[0]].rearrange("p t j -> p j t"), 1.0, 1.0, MULT, MULT)
-            for n, g in enumerate(groups):
-                y_bf[i, g] = dst[:, n]
+        def round_first_two(at):
+            dst = rnd.tile([P, 2, 2 * P, 4], BF16, name="y_bf_first", offset=at, align_bytes=64)
+            for i in range(2):
+                nc.gpsimd.tensor_scalar(
+                    dst[:, :, i * P : (i + 1) * P, :], joint[i][:].rearrange("p g t j -> p g j t"), 1.0, 1.0, MULT, MULT
+                )
+            for g in range(2):
+                y_bf[1, g] = dst[:, g]
+
+        def round_y_gpsimd(i, g, at):
+            y_bf[i, g] = rnd.tile([P, BATCHES[i], 4], BF16, name="y_bfg%d" % i, offset=at, align_bytes=64)[:]
+            nc.gpsimd.tensor_scalar(y_bf[i, g], ys[i, g].rearrange("p t j -> p j t"), 1.0, 1.0, MULT, MULT)
 
         def estimate(i, g, h_q, h_s):
             j0, w = starts[i], BATCHES[i]
@@ -315,12 +321,17 @@ def tile_list_triplex_median_vote_kernel(
                     nc.scalar.activation(y[:, t0 + u, :], bank[:, u, :], IDENT, bias=bias[:, g, t0 + u : t0 + u + 1])
             nc.sync.dma_start(y_rows[g][:, :, j0 : j0 + w], y)
 
+        y_q = {}
+
         def quantise_y(i, g):
-            j0, w = starts[i], BATCHES[i]
+            j0, w = (0, 2 * P) if i == 1 else (starts[i], BATCHES[i])
+            last = i in y_q
+            if not last:
+                y_q[i] = keep.tile([P, 2, w], U32, name="y_q%d" % i, align_bytes=64)
             nc.vector.quantize_mx(
                 y_q[i][:, g, :].bitcast(FP8X4), y_s[:, g, j0 : j0 + w], y_bf[i, g].rearrange("p j t -> p (j t)")
             )
-            if g == 1:
+            if last:
                 nc.sync.dma_start(y_words[:, :, j0 : j0 + w], y_q[i][:].bitcast(I32))
 
         for n in range(4):
@@ -335,37 +346,35 @@ def tile_list_triplex_median_vote_kernel(
         bound(3, lo, MIN)
         quantise_wa(1)
         bound(3, hi, MAX)
-        round_we(nc.scalar.copy, 0, 0, RAW)
-        round_we(nc.vector.tensor_copy, 0, 1, WA_BF_AT + RAW // 2)
+        round_we(0)
         mids = {0: clip(0), 1: clip(1)}
-        round_we(nc.scalar.copy, 1, 0, RAW + 2 * KB)
-        round_we(nc.scalar.copy, 1, 1, RAW + 4 * KB)
+        round_we(1)
         for n in range(4, 8):
             channel_b(n)
         h_bf = median(0, mids[0])
-        quantise_we(0, 0)
-        quantise_we(0, 1)
+        quantise_we(0)
         h_first = quantise_h(0, h_bf)
         estimate(0, 0, *h_first)
         mids[2] = clip(2)
-        planes_after = {3: [(0, 0), (0, 1), (1, 0), (1, 1)], 4: [(2, 0)], 5: [(2, 1), (3, 0)]}
+        planes_before = {3: (1, 0), 4: (2, 1), 5: (3, 1)}
+        planes_after = {3: (1, 1), 4: (2, 0), 5: (3, 0)}
         for i in range(1, len(BATCHES)):
+            if i in planes_before:
+                quantise_y(*planes_before[i])
             h_bf = median(i, mids[i])
             if i == 1:
-                quantise_we(1, 0)
-                quantise_we(1, 1)
-            for piece in planes_after.get(i, []):
-                quantise_y(*piece)
+                quantise_we(1)
+            if i in planes_after:
+                quantise_y(*planes_after[i])
             h_mx = quantise_h(i, h_bf)
             if i == 1:
                 estimate(0, 1, *h_first)
             if i == 2:
-                round_y_gpsimd(0, [0, 1], 2 * KB)
-                round_y_gpsimd(1, [0, 1], 4 * KB)
+                round_first_two(2 * KB)
             if i == 3:
-                round_y_gpsimd(2, [0], 6 * KB)
+                round_y_gpsimd(2, 0, 6 * KB)
             if i == 4:
-                round_y_gpsimd(3, [0], 8 * KB)
+                round_y_gpsimd(3, 0, 8 * KB)
             estimate(i, 0, *h_mx)
             if 2 <= i < len(BATCHES) - 1:
                 late_bounds(i + 1)
@@ -376,8 +385,8 @@ def tile_list_triplex_median_vote_kernel(
             if i == 4:
                 round_y(nc.scalar.copy, i, 0)
                 round_y(nc.scalar.copy, i, 1)
-        for piece in [(3, 1), (4, 0), (4, 1)]:
-            quantise_y(*piece)
+        for g in range(2):
+            quantise_y(4, g)
         for g in range(2):
             round_y(nc.vector.tensor_copy, 5, g)
         for g in range(2):

@@ -21,13 +21,13 @@ IDENT = mybir.ActivationFunctionType.Identity
 P = 128
 HALF = 512
 BATCHES = [128, 128, 256, 256, 128, 128]
-B_BANKS = [0, 1, 5, 6, 7, 3, 4, 2]
-C_BANKS = [2, 3, 4]
-A_BANKS = [5, 6, 0, 1]
-Y_BANKS = [7, 3, 4, 2]
+B_BANKS = [0, 1, 1, 2, 3, 4, 2, 5]
+C_BANKS = [2, 3, 4, 5]
+A_BANKS = [0, 6, 7, 1]
+Y_BANKS = [3, 4, 2, 5]
 RAW = 4 * 512 * 4
 KB = 1024
-WA_BF_AT = 4 * RAW + 64
+WA_BF_AT = 4 * RAW + 64 + 4 * KB
 BOUND_AT = {3: (0, 4 * KB), 4: (4 * KB, 6 * KB), 5: (5 * KB, 7 * KB)}
 H_AT = [0, 1 * KB, 3 * KB, 6 * KB, 8 * KB, 10 * KB]
 
@@ -62,13 +62,11 @@ def tile_list_triplex_median_vote_kernel(
         tabw = [keep.tile([P, T], U32, name="tabw%d" % a, tag="tabw%d" % a, align_bytes=64) for a in range(2)]
         tab_rows = tab_words.rearrange("a p t i -> a p (t i)").bitcast(I32)
         nc.sync.dma_start(tabw[0][:].bitcast(I32), tab_rows[0])
-        wb_raw = keep.tile([P, 2, H], I32, name="wb_raw", tag="wb_raw", align_bytes=64)
-        nc.sync.dma_start(wb_raw[:], wb_words.rearrange("a p e i -> p a (e i)").bitcast(I32))
-        nc.sync.dma_start(tabw[1][:].bitcast(I32), tab_rows[1])
         wc_raw = keep.tile([P, 2, H // 2], I32, name="wc_raw", tag="wc_raw", align_bytes=64)
         nc.sync.dma_start(wc_raw[:], wc_words.rearrange("a p b -> p a b").bitcast(I32))
+        nc.sync.dma_start(tabw[1][:].bitcast(I32), tab_rows[1])
 
-        vsc = late.tile([P, 4 * RAW + 64], U8, name="vsc", offset=0, align_bytes=64)
+        vsc = late.tile([P, 4 * RAW + 128], U8, name="vsc", offset=0, align_bytes=64)
         nc.vector.tensor_copy(vsc[:, 0:S], tsc[:].indirect(offsets[:]))
         staged = keep.tile([32, S + 2 * H], U8, name="staged", align_bytes=64)
         for n, raw in enumerate(wsr):
@@ -80,6 +78,8 @@ def tile_list_triplex_median_vote_kernel(
         for q in range(4):
             nc.sync.dma_start(planes[32 * q : 32 * q + 4, :, :].bitcast(I32), staged[8 * q : 8 * q + 8, :].bitcast(I32))
 
+        wb_raw = late.tile([P, 2, H], I32, name="wb_raw", offset=4 * RAW + 64, align_bytes=64)
+        nc.sync.dma_start(wb_raw[:], wb_words.rearrange("a p e i -> p a (e i)").bitcast(I32))
         wa_raw = [late.tile([P, 4, 512], F32, name="wa_raw%d" % a, offset=a * RAW, align_bytes=64) for a in range(2)]
         we_raw = [late.tile([P, 4, 512], F32, name="we_raw%d" % g, offset=(2 + g) * RAW, align_bytes=64) for g in range(2)]
         for a in range(2):
@@ -91,10 +91,6 @@ def tile_list_triplex_median_vote_kernel(
         bias = late.tile([P, 2, 4], F32, name="bias", offset=4 * RAW, align_bytes=64)
         nc.sync.dma_start(bias[:], be.rearrange("(g p t) -> p g t", p=P, t=4))
 
-        wb_p = keep.tile([P, 2, 4, P], I32, name="wb_p", align_bytes=64)
-        nc.gpsimd.tensor_copy(
-            wb_p[:].rearrange("p a t (q i) -> p a q t i", i=8), wb_raw[:].rearrange("p a (q t i) -> p a q t i", t=4, i=8)
-        )
         wc_p = keep.tile([P, 2, 4, 2 * P], U8, name="wc_p", align_bytes=64)
         nc.gpsimd.tensor_copy(
             wc_p[:].bitcast(I32).rearrange("p a t (q i) -> p a q t i", i=4),
@@ -106,6 +102,11 @@ def tile_list_triplex_median_vote_kernel(
         for h in range(2):
             vw[1, h] = keep.tile([P, HALF], U32, name="vw1_%d" % h, align_bytes=64)[:]
             nc.vector.tensor_copy(vw[1, h], tabw[1][:].indirect(offsets[:, h * HALF // 16 : (h + 1) * HALF // 16]))
+        wb_p = [keep.tile([P, 4, P], I32, name="wb_p%d" % a, align_bytes=64) for a in range(2)]
+        for a in range(2):
+            nc.vector.tensor_copy(
+                wb_p[a][:].rearrange("p t (q i) -> p q t i", i=8), wb_raw[:, a].rearrange("p (q t i) -> p q t i", t=4, i=8)
+            )
 
         def picked(a, j, w):
             h, c0 = divmod(j, HALF)
@@ -120,8 +121,8 @@ def tile_list_triplex_median_vote_kernel(
             used[kind] = used[kind] + 1
             return bank_tile(banks[(used[kind] - 1) % len(banks)])
 
-        def product(out, codes, scales, j, w):
-            for a in range(2):
+        def product(out, codes, scales, j, w, passes=(0, 1)):
+            for a in passes:
                 nc.tensor.matmul_mx(
                     out,
                     lhsT=codes(a),
@@ -138,16 +139,25 @@ def tile_list_triplex_median_vote_kernel(
         hi = {0: keep.tile([P, 4, HALF], F32, name="hi_first")}
         b_second = keep.tile([P, 4, HALF], F32, name="b_second")
 
-        def channel_b(n):
+        copied_ps = {}
+
+        def product_copied(n, passes):
             h, t = divmod(n, 4)
-            bank = bank_tile(B_BANKS[n])
+            if n not in copied_ps:
+                copied_ps[n] = bank_tile(B_BANKS[n])
             product(
-                bank[:],
-                lambda a: wb_p[:, a, t, :].bitcast(FP8X4),
-                lambda a: planes[:, a, S + P * t : S + P * (t + 1)],
+                copied_ps[n][:],
+                lambda a: wc_p[:, a, t, :].bitcast(FP4X4),
+                lambda a: planes[:, a, S + H + P * t : S + H + P * (t + 1)],
                 h * HALF,
                 HALF,
+                passes,
             )
+
+        def channel_b(n):
+            h, t = divmod(n, 4)
+            product_copied(n, (1,) if n < 2 else (0, 1))
+            bank = copied_ps[n]
             b_sb[n] = keep.tile([P, HALF], F32, name="b_sb%d" % n)[:] if h == 0 else b_second[:, t, :]
             nc.scalar.activation(b_sb[n], bank[:], IDENT)
 
@@ -156,8 +166,8 @@ def tile_list_triplex_median_vote_kernel(
             c_ps[n] = bank_tile(C_BANKS[n % len(C_BANKS)])
             product(
                 c_ps[n][:],
-                lambda a: wc_p[:, a, t, :].bitcast(FP4X4),
-                lambda a: planes[:, a, S + H + P * t : S + H + P * (t + 1)],
+                lambda a: wb_p[a][:, t, :].bitcast(FP8X4),
+                lambda a: planes[:, a, S + P * t : S + P * (t + 1)],
                 h * HALF,
                 HALF,
             )
@@ -192,21 +202,18 @@ def tile_list_triplex_median_vote_kernel(
         we_q = keep.tile([P, 2, 4, P], U32, name="we_q", align_bytes=64)
         we_s = keep.tile([P, 2, 4, P], U8, name="we_s", align_bytes=64)
 
-        we_bf = [
-            late.tile([P, 4, P, 4], BF16, name="we_bf%d" % g, offset=RAW + g * RAW // 2, align_bytes=64) for g in range(2)
-        ]
+        we_bf = {}
 
-        def round_we(g):
-            for m0 in range(0, P, 64):
-                dst = we_bf[g][:, :, m0 : m0 + 64, :].rearrange("p t m s -> p m s t")
-                src = we_raw[g][:, :, 4 * m0 : 4 * (m0 + 64)].rearrange("p s (m t) -> p m s t", t=4)
-                nc.scalar.copy(dst, src)
+        def round_we(copy, g, half, at):
+            we_bf[g, half] = late.tile([P, 2, P, 4], BF16, name="we_bf%d_%d" % (g, half), offset=at, align_bytes=64)
+            src = we_raw[g][:].rearrange("p s (m t) -> p m s t", t=4)[:, :, :, 2 * half : 2 * half + 2]
+            copy(we_bf[g, half][:].rearrange("p t m s -> p m s t"), src)
 
-        def quantise_we(g):
+        def quantise_we(g, half):
             nc.vector.quantize_mx(
-                we_q[:, g].rearrange("p t m -> p (t m)").bitcast(FP8X4),
-                we_s[:, g].rearrange("p t m -> p (t m)"),
-                we_bf[g][:].rearrange("p t m j -> p (t m j)"),
+                we_q[:, g, 2 * half : 2 * half + 2].rearrange("p t m -> p (t m)").bitcast(FP8X4),
+                we_s[:, g, 2 * half : 2 * half + 2].rearrange("p t m -> p (t m)"),
+                we_bf[g, half][:].rearrange("p t m j -> p (t m j)"),
             )
 
         starts = [sum(BATCHES[:i]) for i in range(len(BATCHES))]
@@ -224,8 +231,8 @@ def tile_list_triplex_median_vote_kernel(
                 for t in range(4):
                     product(
                         bank[:, t, :],
-                        lambda a: wc_p[:, a, t, :].bitcast(FP4X4),
-                        lambda a: planes[:, a, S + H + P * t : S + H + P * (t + 1)],
+                        lambda a: wb_p[a][:, t, :].bitcast(FP8X4),
+                        lambda a: planes[:, a, S + P * t : S + P * (t + 1)],
                         j0 + c0,
                         P,
                     )
@@ -281,25 +288,26 @@ def tile_list_triplex_median_vote_kernel(
                 ys[i, g] = joint[i][:, g] if i < 2 else keep.tile([P, 4, w], F32, name="y%d_%d" % (i, g))[:]
         y_bf = {}
 
+        def interleave(copy, dst, src):
+            copy(dst.rearrange("p (u e) t -> p u t e", e=2), src.rearrange("p t (u e) -> p u t e", e=2))
+
         def round_y(copy, i, g):
             w = BATCHES[i]
             y_bf[i, g] = keep.tile([P, w, 4], BF16, name="y_bf%d_%d" % (i, g), align_bytes=64)[:]
-            copy(
-                y_bf[i, g].rearrange("p (u e) t -> p u t e", e=2), ys[i, g].rearrange("p t (u e) -> p u t e", e=2)
-            )
+            interleave(copy, y_bf[i, g], ys[i, g])
 
         def round_first_two(at):
             dst = rnd.tile([P, 2, 2 * P, 4], BF16, name="y_bf_first", offset=at, align_bytes=64)
-            for i in range(2):
-                nc.gpsimd.tensor_scalar(
-                    dst[:, :, i * P : (i + 1) * P, :], joint[i][:].rearrange("p g t j -> p g j t"), 1.0, 1.0, MULT, MULT
-                )
+            nc.gpsimd.tensor_scalar(dst[:, :, 0:P, :], joint[0][:].rearrange("p g t j -> p g j t"), 1.0, 1.0, MULT, MULT)
             for g in range(2):
                 y_bf[1, g] = dst[:, g]
+                interleave(nc.scalar.copy, dst[:, g, P : 2 * P, :], ys[1, g])
 
         def round_y_gpsimd(i, g, at):
             y_bf[i, g] = rnd.tile([P, BATCHES[i], 4], BF16, name="y_bfg%d" % i, offset=at, align_bytes=64)[:]
-            nc.gpsimd.tensor_scalar(y_bf[i, g], ys[i, g].rearrange("p t j -> p j t"), 1.0, 1.0, MULT, MULT)
+            nc.gpsimd.tensor_scalar(
+                y_bf[i, g][:, 0:P, :], ys[i, g][:, :, 0:P].rearrange("p t j -> p j t"), 1.0, 1.0, MULT, MULT
+            )
 
         def estimate(i, g, h_q, h_s):
             j0, w = starts[i], BATCHES[i]
@@ -334,6 +342,8 @@ def tile_list_triplex_median_vote_kernel(
             if last:
                 nc.sync.dma_start(y_words[:, :, j0 : j0 + w], y_q[i][:].bitcast(I32))
 
+        for n in range(2):
+            product_copied(n, (0,))
         for n in range(4):
             channel_b(n)
             channel_c(n)
@@ -346,13 +356,16 @@ def tile_list_triplex_median_vote_kernel(
         bound(3, lo, MIN)
         quantise_wa(1)
         bound(3, hi, MAX)
-        round_we(0)
+        round_we(nc.scalar.copy, 0, 0, RAW)
+        round_we(nc.vector.tensor_copy, 0, 1, WA_BF_AT + RAW // 2)
         mids = {0: clip(0), 1: clip(1)}
-        round_we(1)
+        round_we(nc.scalar.copy, 1, 0, RAW + 2 * KB)
+        round_we(nc.scalar.copy, 1, 1, RAW + 4 * KB)
         for n in range(4, 8):
             channel_b(n)
         h_bf = median(0, mids[0])
-        quantise_we(0)
+        quantise_we(0, 0)
+        quantise_we(0, 1)
         h_first = quantise_h(0, h_bf)
         estimate(0, 0, *h_first)
         mids[2] = clip(2)
@@ -363,7 +376,8 @@ def tile_list_triplex_median_vote_kernel(
                 quantise_y(*planes_before[i])
             h_bf = median(i, mids[i])
             if i == 1:
-                quantise_we(1)
+                quantise_we(1, 0)
+                quantise_we(1, 1)
             if i in planes_after:
                 quantise_y(*planes_after[i])
             h_mx = quantise_h(i, h_bf)
@@ -382,6 +396,8 @@ def tile_list_triplex_median_vote_kernel(
             estimate(i, 1, *h_mx)
             if i in (2, 3):
                 round_y(nc.scalar.copy, i, 1)
+            if i in (3, 4):
+                interleave(nc.scalar.copy, y_bf[i - 1, 0][:, P : 2 * P, :], ys[i - 1, 0][:, :, P : 2 * P])
             if i == 4:
                 round_y(nc.scalar.copy, i, 0)
                 round_y(nc.scalar.copy, i, 1)

@@ -16,6 +16,7 @@ FP4X4 = mybir.dt.float4_e2m1fn_x4
 MIN = mybir.AluOpType.min
 MAX = mybir.AluOpType.max
 MULT = mybir.AluOpType.mult
+ADD = mybir.AluOpType.add
 IDENT = mybir.ActivationFunctionType.Identity
 
 P = 128
@@ -28,7 +29,7 @@ Y_BANKS = [3, 4, 2, 5]
 RAW = 4 * 512 * 4
 KB = 1024
 WA_BF_AT = 4 * RAW + 64 + 4 * KB
-BOUND_AT = {3: (0, 4 * KB), 4: (4 * KB, 6 * KB), 5: (5 * KB, 7 * KB)}
+BOUND_AT = {3: (10 * KB, 4 * KB), 4: (4 * KB, 6 * KB), 5: (5 * KB, 7 * KB)}
 H_AT = [0, 1 * KB, 3 * KB, 6 * KB, 8 * KB, 10 * KB]
 
 
@@ -99,14 +100,15 @@ def tile_list_triplex_median_vote_kernel(
         vw_first = keep.tile([P, S], U32, name="vw_first", align_bytes=64)
         nc.vector.tensor_copy(vw_first[:], tabw[0][:].indirect(offsets[:]))
         vw = {(0, h): vw_first[:, h * HALF : (h + 1) * HALF] for h in range(2)}
-        for h in range(2):
-            vw[1, h] = keep.tile([P, HALF], U32, name="vw1_%d" % h, align_bytes=64)[:]
-            nc.vector.tensor_copy(vw[1, h], tabw[1][:].indirect(offsets[:, h * HALF // 16 : (h + 1) * HALF // 16]))
+        vw[1, 0] = keep.tile([P, HALF], U32, name="vw1_0", align_bytes=64)[:]
+        nc.vector.tensor_copy(vw[1, 0], tabw[1][:].indirect(offsets[:, 0 : HALF // 16]))
         wb_p = [keep.tile([P, 4, P], I32, name="wb_p%d" % a, align_bytes=64) for a in range(2)]
         for a in range(2):
             nc.vector.tensor_copy(
                 wb_p[a][:].rearrange("p t (q i) -> p q t i", i=8), wb_raw[:, a].rearrange("p (q t i) -> p q t i", t=4, i=8)
             )
+        vw[1, 1] = late.tile([P, HALF], U32, name="vw1_1", offset=4 * RAW + 64, align_bytes=64)[:]
+        nc.vector.tensor_copy(vw[1, 1], tabw[1][:].indirect(offsets[:, HALF // 16 : S // 16]))
 
         def picked(a, j, w):
             h, c0 = divmod(j, HALF)
@@ -136,7 +138,7 @@ def tile_list_triplex_median_vote_kernel(
         b_sb = {}
         c_ps = {}
         lo = {0: bnd.tile([P, 4, HALF], F32, name="lo_first", offset=0)}
-        hi = {0: keep.tile([P, 4, HALF], F32, name="hi_first")}
+        hi = {0: bnd.tile([P, 4, HALF], F32, name="hi_first", offset=10 * KB)}
         b_second = keep.tile([P, 4, HALF], F32, name="b_second")
 
         copied_ps = {}
@@ -325,6 +327,9 @@ def tile_list_triplex_median_vote_kernel(
                         start=True,
                         stop=True,
                     )
+                if (i, g) == (5, 1):
+                    nc.vector.tensor_tensor(y, bank, bias[:, g, :].unsqueeze(2).broadcast_to([P, 4, w]), ADD)
+                    continue
                 for u in range(per_bank):
                     nc.scalar.activation(y[:, t0 + u, :], bank[:, u, :], IDENT, bias=bias[:, g, t0 + u : t0 + u + 1])
             nc.sync.dma_start(y_rows[g][:, :, j0 : j0 + w], y)
@@ -393,6 +398,9 @@ def tile_list_triplex_median_vote_kernel(
             if 2 <= i < len(BATCHES) - 1:
                 late_bounds(i + 1)
                 mids[i + 1] = clip(i + 1)
+            if i == 5:
+                for g in range(2):
+                    quantise_y(4, g)
             estimate(i, 1, *h_mx)
             if i in (2, 3):
                 round_y(nc.scalar.copy, i, 1)
@@ -401,8 +409,6 @@ def tile_list_triplex_median_vote_kernel(
             if i == 4:
                 round_y(nc.scalar.copy, i, 0)
                 round_y(nc.scalar.copy, i, 1)
-        for g in range(2):
-            quantise_y(4, g)
         for g in range(2):
             round_y(nc.vector.tensor_copy, 5, g)
         for g in range(2):

@@ -248,17 +248,19 @@ def tile_list_triplex_median_vote_kernel(
             mid = ring.tile([P, 4, w], F32, name="mid", tag="mid", bufs=3)
             for t0 in range(0, 4, per_bank):
                 bank = next_bank("a", A_BANKS)[:].rearrange("p (u j) -> p u j", u=per_bank)
-                for a in range(2):
-                    for u in range(per_bank):
-                        nc.tensor.matmul_mx(
-                            bank[:, u, :],
-                            lhsT=wa_q[:, a, t0 + u, :].bitcast(FP8X4),
-                            lhsT_scale=wa_s[:, a, t0 + u, :],
-                            rhs=picked(a, j0, w).bitcast(FP8X4),
-                            rhs_scale=planes[:, a, j0 : j0 + w],
-                            start=(a == 0 and u == 0),
-                            stop=(a == 1 and u == per_bank - 1),
-                        )
+                order = [(a, u) for a in range(2) for u in range(per_bank)]
+                if i >= 2:
+                    order = [(a, u) for u in range(per_bank) for a in range(2)]
+                for n, (a, u) in enumerate(order):
+                    nc.tensor.matmul_mx(
+                        bank[:, u, :],
+                        lhsT=wa_q[:, a, t0 + u, :].bitcast(FP8X4),
+                        lhsT_scale=wa_s[:, a, t0 + u, :],
+                        rhs=picked(a, j0, w).bitcast(FP8X4),
+                        rhs_scale=planes[:, a, j0 : j0 + w],
+                        start=(n == 0),
+                        stop=(n == len(order) - 1),
+                    )
                 nc.vector.tensor_tensor(mid[:, t0 : t0 + per_bank, :], span(hi, i)[:, t0 : t0 + per_bank, :], bank, MIN)
             return mid
 
@@ -352,15 +354,12 @@ def tile_list_triplex_median_vote_kernel(
         for n in range(4):
             channel_b(n)
             channel_c(n)
-            if n < 3:
-                bound(n, lo, MIN)
-                bound(n, hi, MAX)
+            bound(n, lo, MIN)
+            bound(n, hi, MAX)
             if n in (0, 2):
                 round_wa(n // 2)
         quantise_wa(0)
-        bound(3, lo, MIN)
         quantise_wa(1)
-        bound(3, hi, MAX)
         round_we(nc.scalar.copy, 0, 0, RAW)
         round_we(nc.vector.tensor_copy, 0, 1, WA_BF_AT + RAW // 2)
         mids = {0: clip(0), 1: clip(1)}

@@ -21,16 +21,19 @@ IDENT = mybir.ActivationFunctionType.Identity
 
 P = 128
 HALF = 512
+FIRST_BANK = 6
 BATCHES = [128, 128, 256, 256, 128, 128]
-B_BANKS = [0, 1, 1, 2, 3, 4, 2, 5]
-C_BANKS = [2, 3, 4, 5]
-A_BANKS = [0, 6, 7, 1]
-Y_BANKS = [3, 4, 2, 5]
+B_BANKS = [0, 1, 1, 2]
+LATE_BANKS = [2, 3, 2, 3]
+C_BANKS = [2, 3, 6, 3]
+A_BANKS = [1, 0, 6, 7, 0, 6, 7, 0, 1, 6, 7, 0]
+Y_BANKS = [4, 5, 2, 3]
 RAW = 4 * 512 * 4
 KB = 1024
 WA_BF_AT = 4 * RAW + 64 + 4 * KB
-BOUND_AT = {3: (10 * KB, 4 * KB), 4: (4 * KB, 6 * KB), 5: (5 * KB, 7 * KB)}
-H_AT = [0, 1 * KB, 3 * KB, 6 * KB, 8 * KB, 10 * KB]
+HI_AT = [18 * KB, 10 * KB, 20 * KB, 5 * KB]
+LO_AT = {3: 20 * KB, 4: 6 * KB, 5: 7 * KB}
+H_AT = [12 * KB, 1 * KB, 3 * KB, 6 * KB, 8 * KB, 10 * KB]
 
 
 def tile_list_triplex_median_vote_kernel(
@@ -102,16 +105,21 @@ def tile_list_triplex_median_vote_kernel(
         vw = {(0, h): vw_first[:, h * HALF : (h + 1) * HALF] for h in range(2)}
         vw[1, 0] = keep.tile([P, HALF], U32, name="vw1_0", align_bytes=64)[:]
         nc.vector.tensor_copy(vw[1, 0], tabw[1][:].indirect(offsets[:, 0 : HALF // 16]))
+        third = keep.tile([P, HALF // 2], U32, name="vw1_2", align_bytes=64)
+        nc.vector.tensor_copy(third[:], tabw[1][:].indirect(offsets[:, HALF // 16 : 3 * HALF // 32]))
         wb_p = [keep.tile([P, 4, P], I32, name="wb_p%d" % a, align_bytes=64) for a in range(2)]
         for a in range(2):
             nc.vector.tensor_copy(
                 wb_p[a][:].rearrange("p t (q i) -> p q t i", i=8), wb_raw[:, a].rearrange("p (q t i) -> p q t i", t=4, i=8)
             )
-        vw[1, 1] = late.tile([P, HALF], U32, name="vw1_1", offset=4 * RAW + 64, align_bytes=64)[:]
-        nc.vector.tensor_copy(vw[1, 1], tabw[1][:].indirect(offsets[:, HALF // 16 : S // 16]))
+        fourth = late.tile([P, HALF // 2], U32, name="vw1_3", offset=4 * RAW + 64, align_bytes=64)
+        nc.vector.tensor_copy(fourth[:], tabw[1][:].indirect(offsets[:, 3 * HALF // 32 : S // 16]))
 
         def picked(a, j, w):
             h, c0 = divmod(j, HALF)
+            if (a, h) == (1, 1):
+                quarter, c0 = divmod(c0, HALF // 2)
+                return (third, fourth)[quarter][:, c0 : c0 + w]
             return vw[a, h][:, c0 : c0 + w]
 
         def bank_tile(n):
@@ -139,7 +147,7 @@ def tile_list_triplex_median_vote_kernel(
         c_ps = {}
         lo = {0: bnd.tile([P, 4, HALF], F32, name="lo_first", offset=0)}
         hi = {0: bnd.tile([P, 4, HALF], F32, name="hi_first", offset=10 * KB)}
-        b_second = keep.tile([P, 4, HALF], F32, name="b_second")
+        c_late = {}
 
         copied_ps = {}
 
@@ -160,8 +168,21 @@ def tile_list_triplex_median_vote_kernel(
             h, t = divmod(n, 4)
             product_copied(n, (1,) if n < 2 else (0, 1))
             bank = copied_ps[n]
-            b_sb[n] = keep.tile([P, HALF], F32, name="b_sb%d" % n)[:] if h == 0 else b_second[:, t, :]
+            b_sb[n] = keep.tile([P, HALF], F32, name="b_sb%d" % n)[:]
             nc.scalar.activation(b_sb[n], bank[:], IDENT)
+
+        def copy_c_late(u, at):
+            bank = bank_tile(LATE_BANKS[u])
+            for t in range(4):
+                product(
+                    bank[:, t * P : (t + 1) * P],
+                    lambda a: wc_p[:, a, t, :].bitcast(FP4X4),
+                    lambda a: planes[:, a, S + H + P * t : S + H + P * (t + 1)],
+                    HALF + u * P,
+                    P,
+                )
+            c_late[u] = late.tile([P, 4, P], F32, name="c_late%d" % u, offset=at, align_bytes=64)
+            nc.scalar.activation(c_late[u][:].rearrange("p t j -> p (t j)"), bank[:], IDENT)
 
         def channel_c(n):
             h, t = divmod(n, 4)
@@ -178,6 +199,17 @@ def tile_list_triplex_median_vote_kernel(
             h, t = divmod(n, 4)
             nc.vector.tensor_tensor(dst[h][:, t, :], b_sb[n], c_ps[n][:], op)
 
+        def first_pair():
+            w = HALF // 2
+            for part, n in enumerate((C_BANKS[0], FIRST_BANK)):
+                bank = bank_tile(n)[:, 0:w]
+                product(
+                    bank, lambda a: wb_p[a][:, 0, :].bitcast(FP8X4), lambda a: planes[:, a, S : S + P], part * w, w
+                )
+                cols = slice(part * w, (part + 1) * w)
+                for dst, op in ((lo, MIN), (hi, MAX)):
+                    nc.vector.tensor_tensor(dst[0][:, 0, cols], b_sb[0][:, cols], bank, op)
+
         wa_q = keep.tile([P, 2, 4, P], U32, name="wa_q", align_bytes=64)
         wa_s = keep.tile([P, 2, 4, P], U8, name="wa_s", align_bytes=64)
         wa_bf = {}
@@ -188,7 +220,7 @@ def tile_list_triplex_median_vote_kernel(
                 dst = wa_bf[a][:, t, :, :].rearrange("p (q i) j -> p q i j", i=8)
                 src = wa_raw[a][:].rearrange("p j (q t i) -> p t q i j", t=4, i=8)[:, t]
                 if t >= 2:
-                    nc.gpsimd.tensor_scalar(dst, src, 1.0, 1.0, MULT, MULT)
+                    nc.gpsimd.tensor_scalar(dst.rearrange("p q i j -> p q j i"), src.rearrange("p q i j -> p q j i"), 1.0, 1.0, MULT, MULT)
                 else:
                     nc.scalar.copy(
                         dst.rearrange("p q (u e) j -> p q u j e", e=2), src.rearrange("p q (u e) j -> p q u j e", e=2)
@@ -211,6 +243,12 @@ def tile_list_triplex_median_vote_kernel(
             src = we_raw[g][:].rearrange("p s (m t) -> p m s t", t=4)[:, :, :, 2 * half : 2 * half + 2]
             copy(we_bf[g, half][:].rearrange("p t m s -> p m s t"), src)
 
+        def round_we_gpsimd(g, pool, at):
+            we_bf[g, 1] = pool.tile([P, 2, P, 4], BF16, name="we_bf%d_1" % g, offset=at, align_bytes=64)
+            dst = we_bf[g, 1][:].rearrange("p t m s -> p m s t")
+            src = we_raw[g][:].rearrange("p s (m t) -> p m s t", t=4)[:, :, :, 2:4]
+            nc.gpsimd.tensor_scalar(dst, src, 1.0, 1.0, MULT, MULT)
+
         def quantise_we(g, half):
             nc.vector.quantize_mx(
                 we_q[:, g, 2 * half : 2 * half + 2].rearrange("p t m -> p (t m)").bitcast(FP8X4),
@@ -224,23 +262,39 @@ def tile_list_triplex_median_vote_kernel(
                 return tiles[0][:, :, starts[i] : starts[i] + BATCHES[i]]
             return tiles[i][:]
 
-        def late_bounds(i):
-            j0, w = starts[i], BATCHES[i]
-            hi[i] = bnd.tile([P, 4, w], F32, name="hi%d" % i, offset=BOUND_AT[i][0])
-            lo[i] = bnd.tile([P, 4, w], F32, name="lo%d" % i, offset=BOUND_AT[i][1])
-            for c0 in range(0, w, P):
-                bank = next_bank("a", A_BANKS)[:].rearrange("p (t j) -> p t j", t=4)
-                for t in range(4):
-                    product(
-                        bank[:, t, :],
-                        lambda a: wb_p[a][:, t, :].bitcast(FP8X4),
-                        lambda a: planes[:, a, S + P * t : S + P * (t + 1)],
-                        j0 + c0,
-                        P,
-                    )
-                b = b_second[:, :, j0 - HALF + c0 : j0 - HALF + c0 + P]
-                nc.vector.tensor_tensor(hi[i][:, :, c0 : c0 + P], b, bank, MAX)
-                nc.vector.tensor_tensor(lo[i][:, :, c0 : c0 + P], b, bank, MIN)
+        b_ps = {}
+        hi_late = {}
+
+        def upper(u):
+            b_ps[u] = next_bank("a", A_BANKS)[:].rearrange("p (t j) -> p t j", t=4)
+            for t in range(4):
+                product(
+                    b_ps[u][:, t, :],
+                    lambda a: wb_p[a][:, t, :].bitcast(FP8X4),
+                    lambda a: planes[:, a, S + P * t : S + P * (t + 1)],
+                    HALF + u * P,
+                    P,
+                )
+            hi_late[u] = bnd.tile([P, 4, P], F32, name="hi_late%d" % u, offset=HI_AT[u])
+            nc.vector.tensor_tensor(hi_late[u][:], c_late[u][:], b_ps[u], MAX)
+
+        def lower(i, u):
+            c0 = HALF + u * P - starts[i]
+            if c0 == 0:
+                lo[i] = bnd.tile([P, 4, BATCHES[i]], F32, name="lo%d" % i, offset=LO_AT[i])
+            nc.vector.tensor_tensor(lo[i][:, :, c0 : c0 + P], c_late[u][:], b_ps[u], MIN)
+
+        def channel_a(bank, order, t0, j0, w):
+            for n, (a, u) in enumerate(order):
+                nc.tensor.matmul_mx(
+                    bank[:, u, :],
+                    lhsT=wa_q[:, a, t0 + u, :].bitcast(FP8X4),
+                    lhsT_scale=wa_s[:, a, t0 + u, :],
+                    rhs=picked(a, j0, w).bitcast(FP8X4),
+                    rhs_scale=planes[:, a, j0 : j0 + w],
+                    start=(n == 0),
+                    stop=(n == len(order) - 1),
+                )
 
         def clip(i):
             j0, w = starts[i], BATCHES[i]
@@ -251,17 +305,25 @@ def tile_list_triplex_median_vote_kernel(
                 order = [(a, u) for a in range(2) for u in range(per_bank)]
                 if i >= 2:
                     order = [(a, u) for u in range(per_bank) for a in range(2)]
-                for n, (a, u) in enumerate(order):
-                    nc.tensor.matmul_mx(
-                        bank[:, u, :],
-                        lhsT=wa_q[:, a, t0 + u, :].bitcast(FP8X4),
-                        lhsT_scale=wa_s[:, a, t0 + u, :],
-                        rhs=picked(a, j0, w).bitcast(FP8X4),
-                        rhs_scale=planes[:, a, j0 : j0 + w],
-                        start=(n == 0),
-                        stop=(n == len(order) - 1),
-                    )
+                channel_a(bank, order, t0, j0, w)
                 nc.vector.tensor_tensor(mid[:, t0 : t0 + per_bank, :], span(hi, i)[:, t0 : t0 + per_bank, :], bank, MIN)
+            return mid
+
+        def late_batch(i):
+            j0, w = starts[i], BATCHES[i]
+            units = range((j0 - HALF) // P, (j0 - HALF + w) // P)
+            for u in units:
+                if u not in b_ps:
+                    upper(u)
+            for u in units:
+                if u > 0:
+                    lower(i, u)
+            mid = ring.tile([P, 4, w], F32, name="mid", tag="mid", bufs=3)
+            for u in units:
+                bank = next_bank("a", A_BANKS)[:].rearrange("p (t j) -> p t j", t=4)
+                channel_a(bank, [(a, t) for t in range(4) for a in range(2)], 0, HALF + u * P, P)
+                c0 = HALF + u * P - j0
+                nc.vector.tensor_tensor(mid[:, :, c0 : c0 + P], hi_late[u][:], bank, MIN)
             return mid
 
         def median(i, mid):
@@ -285,15 +347,24 @@ def tile_list_triplex_median_vote_kernel(
         y_s = keep.tile([P, 2, S], U8, name="y_s", align_bytes=64)
         y_rows = out_0.rearrange("(g p t) j -> g p t j", p=P, t=4)
         y_words = out_1.rearrange("g p m t -> p g (m t)").bitcast(I32)
-        joint = [keep.tile([P, 2, 4, w], F32, name="y%d" % i) for i, w in enumerate(BATCHES[:2])]
+        joint = [keep.tile([P, 4, 2 * P], F32, name="y_first%d" % g) for g in range(2)]
         ys = {}
         for i, w in enumerate(BATCHES):
             for g in range(2):
-                ys[i, g] = joint[i][:, g] if i < 2 else keep.tile([P, 4, w], F32, name="y%d_%d" % (i, g))[:]
+                ys[i, g] = joint[g][:, :, i * P : (i + 1) * P] if i < 2 else keep.tile([P, 4, w], F32, name="y%d_%d" % (i, g))[:]
         y_bf = {}
 
         def interleave(copy, dst, src):
             copy(dst.rearrange("p (u e) t -> p u t e", e=2), src.rearrange("p t (u e) -> p u t e", e=2))
+
+        def pairs_out(ap):
+            return ap.rearrange("p (u e) t -> p u t e", e=2)
+
+        def pairs_in(ap):
+            return ap.rearrange("p t (u e) -> p u t e", e=2)
+
+        def gpsimd_round(dst, src):
+            nc.gpsimd.tensor_scalar(pairs_out(dst), pairs_in(src), 1.0, 1.0, MULT, MULT)
 
         def round_y(copy, i, g):
             w = BATCHES[i]
@@ -301,17 +372,12 @@ def tile_list_triplex_median_vote_kernel(
             interleave(copy, y_bf[i, g], ys[i, g])
 
         def round_first_two(at):
-            dst = rnd.tile([P, 2, 2 * P, 4], BF16, name="y_bf_first", offset=at, align_bytes=64)
-            nc.gpsimd.tensor_scalar(dst[:, :, 0:P, :], joint[0][:].rearrange("p g t j -> p g j t"), 1.0, 1.0, MULT, MULT)
-            for g in range(2):
-                y_bf[1, g] = dst[:, g]
-                interleave(nc.scalar.copy, dst[:, g, P : 2 * P, :], ys[1, g])
+            y_bf[1, 0] = rnd.tile([P, 2 * P, 4], BF16, name="y_bf_first", offset=at, align_bytes=64)[:]
+            gpsimd_round(y_bf[1, 0], joint[0][:])
 
         def round_y_gpsimd(i, g, at):
             y_bf[i, g] = rnd.tile([P, BATCHES[i], 4], BF16, name="y_bfg%d" % i, offset=at, align_bytes=64)[:]
-            nc.gpsimd.tensor_scalar(
-                y_bf[i, g][:, 0:P, :], ys[i, g][:, :, 0:P].rearrange("p t j -> p j t"), 1.0, 1.0, MULT, MULT
-            )
+            gpsimd_round(y_bf[i, g], ys[i, g])
 
         def estimate(i, g, h_q, h_s):
             j0, w = starts[i], BATCHES[i]
@@ -338,43 +404,53 @@ def tile_list_triplex_median_vote_kernel(
 
         y_q = {}
 
-        def quantise_y(i, g):
+        left = {}
+
+        def quantise_y(i, g, part=slice(None)):
             j0, w = (0, 2 * P) if i == 1 else (starts[i], BATCHES[i])
-            last = i in y_q
-            if not last:
+            if i not in y_q:
                 y_q[i] = keep.tile([P, 2, w], U32, name="y_q%d" % i, align_bytes=64)
+                left[i] = 2 * w
+            codes = y_q[i][:, g, part]
             nc.vector.quantize_mx(
-                y_q[i][:, g, :].bitcast(FP8X4), y_s[:, g, j0 : j0 + w], y_bf[i, g].rearrange("p j t -> p (j t)")
+                codes.bitcast(FP8X4), y_s[:, g, j0 : j0 + w][:, part], y_bf[i, g][:, part, :].rearrange("p j t -> p (j t)")
             )
-            if last:
+            left[i] = left[i] - codes.shape[1]
+            if left[i] == 0:
                 nc.sync.dma_start(y_words[:, :, j0 : j0 + w], y_q[i][:].bitcast(I32))
 
         for n in range(2):
             product_copied(n, (0,))
         for n in range(4):
             channel_b(n)
-            channel_c(n)
-            bound(n, lo, MIN)
-            bound(n, hi, MAX)
+            if n == 0:
+                first_pair()
+            else:
+                channel_c(n)
+                bound(n, lo, MIN)
+                bound(n, hi, MAX)
             if n in (0, 2):
                 round_wa(n // 2)
         quantise_wa(0)
         quantise_wa(1)
+        copy_c_late(0, 0)
+        upper(0)
         round_we(nc.scalar.copy, 0, 0, RAW)
-        round_we(nc.vector.tensor_copy, 0, 1, WA_BF_AT + RAW // 2)
+        round_we_gpsimd(0, late, WA_BF_AT + RAW // 2)
         mids = {0: clip(0), 1: clip(1)}
         round_we(nc.scalar.copy, 1, 0, RAW + 2 * KB)
-        round_we(nc.scalar.copy, 1, 1, RAW + 4 * KB)
-        for n in range(4, 8):
-            channel_b(n)
+        for u in range(1, 4):
+            copy_c_late(u, 2 * KB * u)
         h_bf = median(0, mids[0])
         quantise_we(0, 0)
         quantise_we(0, 1)
         h_first = quantise_h(0, h_bf)
+        round_we_gpsimd(1, rnd, H_AT[0])
         estimate(0, 0, *h_first)
         mids[2] = clip(2)
-        planes_before = {3: (1, 0), 4: (2, 1), 5: (3, 1)}
-        planes_after = {3: (1, 1), 4: (2, 0), 5: (3, 0)}
+        lower(3, 0)
+        planes_before = {3: (1, 0), 4: (2, 1), 5: (3, 0, slice(0, P))}
+        planes_after = {3: (1, 1), 4: (2, 0), 5: (3, 0, slice(P, 2 * P))}
         for i in range(1, len(BATCHES)):
             if i in planes_before:
                 quantise_y(*planes_before[i])
@@ -395,19 +471,22 @@ def tile_list_triplex_median_vote_kernel(
                 round_y_gpsimd(3, 0, 8 * KB)
             estimate(i, 0, *h_mx)
             if 2 <= i < len(BATCHES) - 1:
-                late_bounds(i + 1)
-                mids[i + 1] = clip(i + 1)
+                mids[i + 1] = late_batch(i + 1)
+            if i == 4:
+                spare = bank_tile(A_BANKS[-1])
+                product(spare[:], lambda a: wb_p[a][:, 0, :].bitcast(FP8X4), lambda a: planes[:, a, S : S + P], 0, HALF)
             if i == 5:
                 for g in range(2):
+                    round_y(nc.vector.tensor_copy, 4, g)
+                for g in range(2):
                     quantise_y(4, g)
+                quantise_y(3, 1)
             estimate(i, 1, *h_mx)
-            if i in (2, 3):
-                round_y(nc.scalar.copy, i, 1)
-            if i in (3, 4):
-                interleave(nc.scalar.copy, y_bf[i - 1, 0][:, P : 2 * P, :], ys[i - 1, 0][:, :, P : 2 * P])
-            if i == 4:
-                round_y(nc.scalar.copy, i, 0)
-                round_y(nc.scalar.copy, i, 1)
+            if i == 2:
+                y_bf[1, 1] = keep.tile([P, 2 * P, 4], BF16, name="y_bf_second", align_bytes=64)[:]
+                interleave(nc.scalar.copy, y_bf[1, 1], joint[1][:])
+            if i in (2, 4):
+                round_y(nc.scalar.copy, i - i // 4, 1)
         for g in range(2):
             round_y(nc.vector.tensor_copy, 5, g)
         for g in range(2):

@@ -79,7 +79,7 @@ def tile_list_triplex_median_vote_kernel(
                 raw[:].bitcast(I32).rearrange("p (q t i) -> p q t i", t=4, i=2),
             )
         nc.vector.tensor_copy(staged[:, 0:S].bitcast(I32), vsc[0:32, 0:S].bitcast(I32))
-        for q in range(4):
+        for q in (0, 2, 1, 3):
             nc.sync.dma_start(planes[32 * q : 32 * q + 4, :, :].bitcast(I32), staged[8 * q : 8 * q + 8, :].bitcast(I32))
 
         wb_raw = late.tile([P, 2, H], I32, name="wb_raw", offset=4 * RAW + 64, align_bytes=64)
@@ -492,7 +492,7 @@ def tile_list_triplex_median_vote_kernel(
         for g in range(2):
             quantise_y(5, g)
         for q in range(4):
-            (nc.scalar if q % 2 else nc.sync).dma_start(
+            (nc.scalar if q // 2 else nc.sync).dma_start(
                 out_2[:, 4 * q : 4 * q + 4, :].rearrange("g r m -> r g m").bitcast(I32),
                 y_s[32 * q : 32 * q + 4, :, :].bitcast(I32),
             )

@@ -449,12 +449,17 @@ def tile_list_triplex_median_vote_kernel(
         estimate(0, 0, *h_first)
         mids[2] = clip(2)
         lower(3, 0)
-        planes_before = {3: (1, 0), 4: (2, 1), 5: (3, 0, slice(0, P))}
-        planes_after = {3: (1, 1), 4: (2, 0), 5: (3, 0, slice(P, 2 * P))}
+        planes_before = {3: (1, 0), 4: (2, 1)}
+        planes_after = {3: (1, 1), 4: (2, 0)}
         for i in range(1, len(BATCHES)):
             if i in planes_before:
                 quantise_y(*planes_before[i])
+            if i == 5:
+                y_bf[3, 1] = late.tile([P, 2 * P, 4], BF16, name="y_bf3_1", offset=6 * KB, align_bytes=64)[:]
+                interleave(nc.vector.tensor_copy, y_bf[3, 1][:, 0:P, :], ys[3, 1][:, :, 0:P])
             h_bf = median(i, mids[i])
+            if i == 5:
+                interleave(nc.vector.tensor_copy, y_bf[3, 1][:, P : 2 * P, :], ys[3, 1][:, :, P : 2 * P])
             if i == 1:
                 quantise_we(1, 0)
                 quantise_we(1, 1)
@@ -472,21 +477,19 @@ def tile_list_triplex_median_vote_kernel(
             estimate(i, 0, *h_mx)
             if 2 <= i < len(BATCHES) - 1:
                 mids[i + 1] = late_batch(i + 1)
-            if i == 4:
-                spare = bank_tile(A_BANKS[-1])
-                product(spare[:], lambda a: wb_p[a][:, 0, :].bitcast(FP8X4), lambda a: planes[:, a, S : S + P], 0, HALF)
             if i == 5:
-                for g in range(2):
-                    round_y(nc.vector.tensor_copy, 4, g)
-                for g in range(2):
-                    quantise_y(4, g)
-                quantise_y(3, 1)
+                for n in (3, 4):
+                    for g in range(2):
+                        quantise_y(n, g)
             estimate(i, 1, *h_mx)
             if i == 2:
                 y_bf[1, 1] = keep.tile([P, 2 * P, 4], BF16, name="y_bf_second", align_bytes=64)[:]
                 interleave(nc.scalar.copy, y_bf[1, 1], joint[1][:])
-            if i in (2, 4):
-                round_y(nc.scalar.copy, i - i // 4, 1)
+            if i == 2:
+                round_y(nc.scalar.copy, i, 1)
+            if i == 4:
+                for g in range(2):
+                    round_y(nc.scalar.copy, i, g)
         for g in range(2):
             round_y(nc.vector.tensor_copy, 5, g)
         for g in range(2):

@@ -21,6 +21,7 @@ IDENT = mybir.ActivationFunctionType.Identity
 
 P = 128
 HALF = 512
+WORDS = [(0, 256), (256, 512), (512, 768), (768, 896), (896, 1024)]
 FIRST_BANK = 6
 BATCHES = [128, 128, 256, 256, 128, 128]
 B_BANKS = [0, 1, 1, 2]
@@ -347,11 +348,11 @@ def tile_list_triplex_median_vote_kernel(
         y_s = keep.tile([P, 2, S], U8, name="y_s", align_bytes=64)
         y_rows = out_0.rearrange("(g p t) j -> g p t j", p=P, t=4)
         y_words = out_1.rearrange("g p m t -> p g (m t)").bitcast(I32)
-        joint = [keep.tile([P, 4, 2 * P], F32, name="y_first%d" % g) for g in range(2)]
+        joint = keep.tile([P, 4, 4 * P], F32, name="y_first")
         ys = {}
         for i, w in enumerate(BATCHES):
             for g in range(2):
-                ys[i, g] = joint[g][:, :, i * P : (i + 1) * P] if i < 2 else keep.tile([P, 4, w], F32, name="y%d_%d" % (i, g))[:]
+                ys[i, g] = joint[:, :, (2 * g + i) * P : (2 * g + i + 1) * P] if i < 2 else keep.tile([P, 4, w], F32, name="y%d_%d" % (i, g))[:]
         y_bf = {}
 
         def interleave(copy, dst, src):
@@ -368,12 +369,15 @@ def tile_list_triplex_median_vote_kernel(
 
         def round_y(copy, i, g):
             w = BATCHES[i]
-            y_bf[i, g] = keep.tile([P, w, 4], BF16, name="y_bf%d_%d" % (i, g), align_bytes=64)[:]
+            pool, at = (rnd, 16 * KB) if i == 2 else (keep, None)
+            y_bf[i, g] = pool.tile([P, w, 4], BF16, name="y_bf%d_%d" % (i, g), offset=at, align_bytes=64)[:]
             interleave(copy, y_bf[i, g], ys[i, g])
 
         def round_first_two(at):
-            y_bf[1, 0] = rnd.tile([P, 2 * P, 4], BF16, name="y_bf_first", offset=at, align_bytes=64)[:]
-            gpsimd_round(y_bf[1, 0], joint[0][:])
+            middle = rnd.tile([P, 2 * P, 4], BF16, name="y_bf_first", offset=at, align_bytes=64)
+            gpsimd_round(middle[:], joint[:, :, P : 3 * P])
+            y_bf[1, 0] = middle[:, 0:P, :]
+            y_bf[0, 1] = middle[:, P : 2 * P, :]
 
         def round_y_gpsimd(i, g, at):
             y_bf[i, g] = rnd.tile([P, BATCHES[i], 4], BF16, name="y_bfg%d" % i, offset=at, align_bytes=64)[:]
@@ -407,17 +411,18 @@ def tile_list_triplex_median_vote_kernel(
         left = {}
 
         def quantise_y(i, g, part=slice(None)):
-            j0, w = (0, 2 * P) if i == 1 else (starts[i], BATCHES[i])
-            if i not in y_q:
-                y_q[i] = keep.tile([P, 2, w], U32, name="y_q%d" % i, align_bytes=64)
-                left[i] = 2 * w
-            codes = y_q[i][:, g, part]
+            j0, w = starts[i], BATCHES[i]
+            first, end = [span for span in WORDS if span[0] <= j0 < span[1]][0]
+            if first not in y_q:
+                y_q[first] = keep.tile([P, 2, end - first], U32, name="y_q%d" % first, align_bytes=64)
+                left[first] = 2 * (end - first)
+            codes = y_q[first][:, g, j0 - first : j0 - first + w][:, part]
             nc.vector.quantize_mx(
                 codes.bitcast(FP8X4), y_s[:, g, j0 : j0 + w][:, part], y_bf[i, g][:, part, :].rearrange("p j t -> p (j t)")
             )
-            left[i] = left[i] - codes.shape[1]
-            if left[i] == 0:
-                nc.sync.dma_start(y_words[:, :, j0 : j0 + w], y_q[i][:].bitcast(I32))
+            left[first] = left[first] - codes.shape[1]
+            if left[first] == 0:
+                nc.sync.dma_start(y_words[:, :, first:end], y_q[first][:].bitcast(I32))
 
         for n in range(2):
             product_copied(n, (0,))
@@ -445,15 +450,16 @@ def tile_list_triplex_median_vote_kernel(
         quantise_we(0, 0)
         quantise_we(0, 1)
         h_first = quantise_h(0, h_bf)
-        round_we_gpsimd(1, rnd, H_AT[0])
+        round_we_gpsimd(1, late, WA_BF_AT + RAW // 2)
         estimate(0, 0, *h_first)
+        round_y(nc.scalar.copy, 0, 0)
         mids[2] = clip(2)
         lower(3, 0)
-        planes_before = {3: (1, 0), 4: (2, 1)}
-        planes_after = {3: (1, 1), 4: (2, 0)}
+        planes_before = {3: [(0, 0), (1, 0)], 4: [(2, 0)]}
+        planes_after = {3: [(0, 1), (1, 1)], 4: [(2, 1)]}
         for i in range(1, len(BATCHES)):
-            if i in planes_before:
-                quantise_y(*planes_before[i])
+            for piece in planes_before.get(i, []):
+                quantise_y(*piece)
             if i == 5:
                 y_bf[3, 1] = late.tile([P, 2 * P, 4], BF16, name="y_bf3_1", offset=6 * KB, align_bytes=64)[:]
                 interleave(nc.vector.tensor_copy, y_bf[3, 1][:, 0:P, :], ys[3, 1][:, :, 0:P])
@@ -463,28 +469,28 @@ def tile_list_triplex_median_vote_kernel(
             if i == 1:
                 quantise_we(1, 0)
                 quantise_we(1, 1)
-            if i in planes_after:
-                quantise_y(*planes_after[i])
+            for piece in planes_after.get(i, []):
+                quantise_y(*piece)
             h_mx = quantise_h(i, h_bf)
             if i == 1:
                 estimate(0, 1, *h_first)
             if i == 2:
                 round_first_two(2 * KB)
             if i == 3:
-                round_y_gpsimd(2, 0, 6 * KB)
+                round_y_gpsimd(2, 0, 14 * KB)
             if i == 4:
-                round_y_gpsimd(3, 0, 8 * KB)
-            estimate(i, 0, *h_mx)
-            if 2 <= i < len(BATCHES) - 1:
-                mids[i + 1] = late_batch(i + 1)
+                round_y_gpsimd(3, 0, 16 * KB)
             if i == 5:
                 for n in (3, 4):
                     for g in range(2):
                         quantise_y(n, g)
+            estimate(i, 0, *h_mx)
+            if 2 <= i < len(BATCHES) - 1:
+                mids[i + 1] = late_batch(i + 1)
             estimate(i, 1, *h_mx)
             if i == 2:
-                y_bf[1, 1] = keep.tile([P, 2 * P, 4], BF16, name="y_bf_second", align_bytes=64)[:]
-                interleave(nc.scalar.copy, y_bf[1, 1], joint[1][:])
+                y_bf[1, 1] = rnd.tile([P, P, 4], BF16, name="y_bf_second", offset=14 * KB, align_bytes=64)[:]
+                interleave(nc.scalar.copy, y_bf[1, 1], ys[1, 1])
             if i == 2:
                 round_y(nc.scalar.copy, i, 1)
             if i == 4:

@@ -23,7 +23,7 @@ P = 128
 HALF = 512
 WORDS = [(0, 256), (256, 512), (512, 768), (768, 896), (896, 1024)]
 FIRST_BANK = 6
-BATCHES = [128, 128, 256, 256, 128, 128]
+BATCHES = [256, 256, 256, 128, 128]
 B_BANKS = [0, 1, 1, 2]
 LATE_BANKS = [2, 3, 2, 3]
 C_BANKS = [2, 3, 6, 3]
@@ -32,9 +32,9 @@ Y_BANKS = [4, 5, 2, 3]
 RAW = 4 * 512 * 4
 KB = 1024
 WA_BF_AT = 4 * RAW + 64 + 4 * KB
-HI_AT = [18 * KB, 10 * KB, 20 * KB, 5 * KB]
-LO_AT = {3: 20 * KB, 4: 6 * KB, 5: 7 * KB}
-H_AT = [12 * KB, 1 * KB, 3 * KB, 6 * KB, 8 * KB, 10 * KB]
+HI_AT = [18 * KB, 10 * KB, 18 * KB, 10 * KB]
+LO_AT = {2: 20 * KB, 3: 6 * KB, 4: 7 * KB}
+H_AT = [0, 2 * KB, 4 * KB, 8 * KB, 9 * KB]
 
 
 def tile_list_triplex_median_vote_kernel(
@@ -56,6 +56,9 @@ def tile_list_triplex_median_vote_kernel(
         nc.sync.dma_start(tsc[0:32, :].bitcast(I32), tab_scales.rearrange("a i t -> i a t").bitcast(I32))
         nc.vector.memset(tsc[32:64, :].bitcast(I32), 0)
         nc.vector.memset(tsc[64:128, :].bitcast(I32), 0)
+        tabw = [keep.tile([P, T], U32, name="tabw%d" % a, tag="tabw%d" % a, align_bytes=64) for a in range(2)]
+        tab_rows = tab_words.rearrange("a p t i -> a p (t i)").bitcast(I32)
+        nc.sync.dma_start(tabw[0][:].bitcast(I32), tab_rows[0])
         wsr = []
         for name, scales in (("wbs_raw", wb_scales), ("wcs_raw", wc_scales)):
             raw = keep.tile([32, H], U8, name=name, align_bytes=64)
@@ -64,12 +67,9 @@ def tile_list_triplex_median_vote_kernel(
         planes = keep.tile([P, 2, S + 2 * H], U8, name="planes", align_bytes=64)
         nc.gpsimd.memset(planes[:].bitcast(I32), 0)
 
-        tabw = [keep.tile([P, T], U32, name="tabw%d" % a, tag="tabw%d" % a, align_bytes=64) for a in range(2)]
-        tab_rows = tab_words.rearrange("a p t i -> a p (t i)").bitcast(I32)
-        nc.sync.dma_start(tabw[0][:].bitcast(I32), tab_rows[0])
+        nc.sync.dma_start(tabw[1][:].bitcast(I32), tab_rows[1])
         wc_raw = keep.tile([P, 2, H // 2], I32, name="wc_raw", tag="wc_raw", align_bytes=64)
         nc.sync.dma_start(wc_raw[:], wc_words.rearrange("a p b -> p a b").bitcast(I32))
-        nc.sync.dma_start(tabw[1][:].bitcast(I32), tab_rows[1])
 
         vsc = late.tile([P, 4 * RAW + 128], U8, name="vsc", offset=0, align_bytes=64)
         nc.vector.tensor_copy(vsc[:, 0:S], tsc[:].indirect(offsets[:]))
@@ -297,45 +297,30 @@ def tile_list_triplex_median_vote_kernel(
                     stop=(n == len(order) - 1),
                 )
 
-        def clip(i):
-            j0, w = starts[i], BATCHES[i]
-            per_bank = 512 // w
-            mid = ring.tile([P, 4, w], F32, name="mid", tag="mid", bufs=3)
-            for t0 in range(0, 4, per_bank):
-                bank = next_bank("a", A_BANKS)[:].rearrange("p (u j) -> p u j", u=per_bank)
-                order = [(a, u) for a in range(2) for u in range(per_bank)]
-                if i >= 2:
-                    order = [(a, u) for u in range(per_bank) for a in range(2)]
-                channel_a(bank, order, t0, j0, w)
-                nc.vector.tensor_tensor(mid[:, t0 : t0 + per_bank, :], span(hi, i)[:, t0 : t0 + per_bank, :], bank, MIN)
-            return mid
+        mids = {}
 
-        def late_batch(i):
-            j0, w = starts[i], BATCHES[i]
-            units = range((j0 - HALF) // P, (j0 - HALF + w) // P)
-            for u in units:
-                if u not in b_ps:
-                    upper(u)
-            for u in units:
-                if u > 0:
-                    lower(i, u)
-            mid = ring.tile([P, 4, w], F32, name="mid", tag="mid", bufs=3)
-            for u in units:
-                bank = next_bank("a", A_BANKS)[:].rearrange("p (t j) -> p t j", t=4)
-                channel_a(bank, [(a, t) for t in range(4) for a in range(2)], 0, HALF + u * P, P)
-                c0 = HALF + u * P - j0
-                nc.vector.tensor_tensor(mid[:, :, c0 : c0 + P], hi_late[u][:], bank, MIN)
-            return mid
+        def clip(i, t0, count, c0, w, bound_tile, pass_major):
+            if i not in mids:
+                mids[i] = ring.tile([P, 4, BATCHES[i]], F32, name="mid", tag="mid", bufs=3)
+            bank = next_bank("a", A_BANKS)[:].rearrange("p (u j) -> p u j", u=count)
+            order = [(a, u) for a in range(2) for u in range(count)] if pass_major else [(a, u) for u in range(count) for a in range(2)]
+            channel_a(bank, order, t0, starts[i] + c0, w)
+            nc.vector.tensor_tensor(mids[i][:, t0 : t0 + count, c0 : c0 + w], bound_tile, bank, MIN)
 
-        def median(i, mid):
+        def clip_late(i, u):
+            clip(i, 0, 4, HALF + u * P - starts[i], P, hi_late[u][:], False)
+
+        def median(i, mid, parts=1):
             w = BATCHES[i]
             h_bf = rnd.tile([P, w, 4], BF16, name="h_bf%d" % i, offset=H_AT[i], align_bytes=64)
-            nc.vector.tensor_tensor(
-                h_bf[:].rearrange("p (u e) t -> p u t e", e=2),
-                span(lo, i).rearrange("p t (u e) -> p u t e", e=2),
-                mid[:].rearrange("p t (u e) -> p u t e", e=2),
-                MAX,
-            )
+            for c0 in range(0, w, w // parts):
+                cols = slice(c0, c0 + w // parts)
+                nc.vector.tensor_tensor(
+                    h_bf[:, cols, :].rearrange("p (u e) t -> p u t e", e=2),
+                    span(lo, i)[:, :, cols].rearrange("p t (u e) -> p u t e", e=2),
+                    mid[:, :, cols].rearrange("p t (u e) -> p u t e", e=2),
+                    MAX,
+                )
             return h_bf
 
         def quantise_h(i, h_bf):
@@ -348,11 +333,10 @@ def tile_list_triplex_median_vote_kernel(
         y_s = keep.tile([P, 2, S], U8, name="y_s", align_bytes=64)
         y_rows = out_0.rearrange("(g p t) j -> g p t j", p=P, t=4)
         y_words = out_1.rearrange("g p m t -> p g (m t)").bitcast(I32)
-        joint = keep.tile([P, 4, 4 * P], F32, name="y_first")
         ys = {}
         for i, w in enumerate(BATCHES):
             for g in range(2):
-                ys[i, g] = joint[:, :, (2 * g + i) * P : (2 * g + i + 1) * P] if i < 2 else keep.tile([P, 4, w], F32, name="y%d_%d" % (i, g))[:]
+                ys[i, g] = keep.tile([P, 4, w], F32, name="y%d_%d" % (i, g))[:]
         y_bf = {}
 
         def interleave(copy, dst, src):
@@ -368,19 +352,11 @@ def tile_list_triplex_median_vote_kernel(
             nc.gpsimd.tensor_scalar(pairs_out(dst), pairs_in(src), 1.0, 1.0, MULT, MULT)
 
         def round_y(copy, i, g):
-            w = BATCHES[i]
-            pool, at = (rnd, 16 * KB) if i == 2 else (keep, None)
-            y_bf[i, g] = pool.tile([P, w, 4], BF16, name="y_bf%d_%d" % (i, g), offset=at, align_bytes=64)[:]
+            y_bf[i, g] = keep.tile([P, BATCHES[i], 4], BF16, name="y_bf%d_%d" % (i, g), align_bytes=64)[:]
             interleave(copy, y_bf[i, g], ys[i, g])
 
-        def round_first_two(at):
-            middle = rnd.tile([P, 2 * P, 4], BF16, name="y_bf_first", offset=at, align_bytes=64)
-            gpsimd_round(middle[:], joint[:, :, P : 3 * P])
-            y_bf[1, 0] = middle[:, 0:P, :]
-            y_bf[0, 1] = middle[:, P : 2 * P, :]
-
         def round_y_gpsimd(i, g, at):
-            y_bf[i, g] = rnd.tile([P, BATCHES[i], 4], BF16, name="y_bfg%d" % i, offset=at, align_bytes=64)[:]
+            y_bf[i, g] = rnd.tile([P, BATCHES[i], 4], BF16, name="y_bfg%d_%d" % (i, g), offset=at, align_bytes=64)[:]
             gpsimd_round(y_bf[i, g], ys[i, g])
 
         def estimate(i, g, h_q, h_s):
@@ -399,7 +375,7 @@ def tile_list_triplex_median_vote_kernel(
                         start=True,
                         stop=True,
                     )
-                if (i, g) == (5, 1):
+                if (i, g) == (len(BATCHES) - 1, 1):
                     nc.vector.tensor_tensor(y, bank, bias[:, g, :].unsqueeze(2).broadcast_to([P, 4, w]), ADD)
                     continue
                 for u in range(per_bank):
@@ -442,64 +418,70 @@ def tile_list_triplex_median_vote_kernel(
         upper(0)
         round_we(nc.scalar.copy, 0, 0, RAW)
         round_we_gpsimd(0, late, WA_BF_AT + RAW // 2)
-        mids = {0: clip(0), 1: clip(1)}
+        for c0 in (0, P):
+            clip(0, 0, 4, c0, P, hi[0][:, :, c0 : c0 + P], True)
         round_we(nc.scalar.copy, 1, 0, RAW + 2 * KB)
         for u in range(1, 4):
             copy_c_late(u, 2 * KB * u)
-        h_bf = median(0, mids[0])
+        h_mx = {}
         quantise_we(0, 0)
+        h_bf = median(0, mids[0])
         quantise_we(0, 1)
-        h_first = quantise_h(0, h_bf)
+        h_mx[0] = quantise_h(0, h_bf)
         round_we_gpsimd(1, late, WA_BF_AT + RAW // 2)
-        estimate(0, 0, *h_first)
+        estimate(0, 0, *h_mx[0])
         round_y(nc.scalar.copy, 0, 0)
-        mids[2] = clip(2)
-        lower(3, 0)
-        planes_before = {3: [(0, 0), (1, 0)], 4: [(2, 0)]}
-        planes_after = {3: [(0, 1), (1, 1)], 4: [(2, 1)]}
-        for i in range(1, len(BATCHES)):
-            for piece in planes_before.get(i, []):
-                quantise_y(*piece)
-            if i == 5:
-                y_bf[3, 1] = late.tile([P, 2 * P, 4], BF16, name="y_bf3_1", offset=6 * KB, align_bytes=64)[:]
-                interleave(nc.vector.tensor_copy, y_bf[3, 1][:, 0:P, :], ys[3, 1][:, :, 0:P])
-            h_bf = median(i, mids[i])
-            if i == 5:
-                interleave(nc.vector.tensor_copy, y_bf[3, 1][:, P : 2 * P, :], ys[3, 1][:, :, P : 2 * P])
-            if i == 1:
-                quantise_we(1, 0)
-                quantise_we(1, 1)
-            for piece in planes_after.get(i, []):
-                quantise_y(*piece)
-            h_mx = quantise_h(i, h_bf)
-            if i == 1:
-                estimate(0, 1, *h_first)
-            if i == 2:
-                round_first_two(2 * KB)
-            if i == 3:
-                round_y_gpsimd(2, 0, 14 * KB)
-            if i == 4:
-                round_y_gpsimd(3, 0, 16 * KB)
-            if i == 5:
-                for n in (3, 4):
-                    for g in range(2):
-                        quantise_y(n, g)
-            estimate(i, 0, *h_mx)
-            if 2 <= i < len(BATCHES) - 1:
-                mids[i + 1] = late_batch(i + 1)
-            estimate(i, 1, *h_mx)
-            if i == 2:
-                y_bf[1, 1] = rnd.tile([P, P, 4], BF16, name="y_bf_second", offset=14 * KB, align_bytes=64)[:]
-                interleave(nc.scalar.copy, y_bf[1, 1], ys[1, 1])
-            if i == 2:
-                round_y(nc.scalar.copy, i, 1)
-            if i == 4:
-                for g in range(2):
-                    round_y(nc.scalar.copy, i, g)
+        for t0 in (0, 2):
+            clip(1, t0, 2, 0, 2 * P, hi[0][:, t0 : t0 + 2, 2 * P : 4 * P], False)
+        lower(2, 0)
+        quantise_we(1, 0)
+        quantise_we(1, 1)
+        estimate(0, 1, *h_mx[0])
+        h_bf = median(1, mids[1])
+        quantise_y(0, 0)
+        h_mx[1] = quantise_h(1, h_bf)
+        round_y_gpsimd(0, 1, H_AT[1])
+        estimate(1, 0, *h_mx[1])
+        estimate(1, 1, *h_mx[1])
+        upper(1)
+        lower(2, 1)
+        clip_late(2, 0)
+        clip_late(2, 1)
+        round_y(nc.scalar.copy, 1, 1)
+        h_bf = median(2, mids[2], parts=2)
+        quantise_y(0, 1)
+        h_mx[2] = quantise_h(2, h_bf)
+        round_y_gpsimd(1, 0, H_AT[2])
+        estimate(2, 0, *h_mx[2])
+        estimate(2, 1, *h_mx[2])
+        round_y(nc.scalar.copy, 2, 1)
+        upper(2)
+        lower(3, 2)
+        clip_late(3, 2)
+        quantise_y(1, 1)
+        h_bf = median(3, mids[3])
+        quantise_y(1, 0)
+        round_y_gpsimd(2, 0, H_AT[2])
+        h_mx[3] = quantise_h(3, h_bf)
+        estimate(3, 0, *h_mx[3])
+        estimate(3, 1, *h_mx[3])
+        upper(3)
+        lower(4, 3)
+        clip_late(4, 3)
+        quantise_y(2, 0)
+        h_bf = median(4, mids[4])
+        quantise_y(2, 1)
+        h_mx[4] = quantise_h(4, h_bf)
         for g in range(2):
-            round_y(nc.vector.tensor_copy, 5, g)
+            round_y(nc.vector.tensor_copy, 3, g)
         for g in range(2):
-            quantise_y(5, g)
+            quantise_y(3, g)
+        estimate(4, 0, *h_mx[4])
+        estimate(4, 1, *h_mx[4])
+        for g in range(2):
+            round_y(nc.vector.tensor_copy, 4, g)
+        for g in range(2):
+            quantise_y(4, g)
         for q in range(4):
             (nc.scalar if q // 2 else nc.sync).dma_start(
                 out_2[:, 4 * q : 4 * q + 4, :].rearrange("g r m -> r g m").bitcast(I32),

@@ -83,8 +83,9 @@ def tile_list_triplex_median_vote_kernel(
         for q in (0, 2, 1, 3):
             nc.sync.dma_start(planes[32 * q : 32 * q + 4, :, :].bitcast(I32), staged[8 * q : 8 * q + 8, :].bitcast(I32))
 
-        wb_raw = late.tile([P, 2, H], I32, name="wb_raw", offset=4 * RAW + 64, align_bytes=64)
-        nc.sync.dma_start(wb_raw[:], wb_words.rearrange("a p e i -> p a (e i)").bitcast(I32))
+        wb_raw = [late.tile([P, H], I32, name="wb_raw%d" % a, offset=4 * RAW + 64 + 2 * KB * a, align_bytes=64) for a in range(2)]
+        for a in range(2):
+            nc.sync.dma_start(wb_raw[a][:], wb_words.rearrange("a p e i -> a p (e i)").bitcast(I32)[a])
         wa_raw = [late.tile([P, 4, 512], F32, name="wa_raw%d" % a, offset=a * RAW, align_bytes=64) for a in range(2)]
         we_raw = [late.tile([P, 4, 512], F32, name="we_raw%d" % g, offset=(2 + g) * RAW, align_bytes=64) for g in range(2)]
         for a in range(2):
@@ -110,10 +111,11 @@ def tile_list_triplex_median_vote_kernel(
         nc.vector.tensor_copy(third[:], tabw[1][:].indirect(offsets[:, HALF // 16 : 3 * HALF // 32]))
         wb_p = [keep.tile([P, 4, P], I32, name="wb_p%d" % a, align_bytes=64) for a in range(2)]
         for a in range(2):
-            nc.vector.tensor_copy(
-                wb_p[a][:].rearrange("p t (q i) -> p q t i", i=8), wb_raw[:, a].rearrange("p (q t i) -> p q t i", t=4, i=8)
+            (nc.scalar.copy, nc.vector.tensor_copy)[a](
+                wb_p[a][:].bitcast((U32, I32)[a]).rearrange("p t (q i) -> p q t i", i=8),
+                wb_raw[a][:].bitcast((U32, I32)[a]).rearrange("p (q t i) -> p q t i", t=4, i=8),
             )
-        fourth = late.tile([P, HALF // 2], U32, name="vw1_3", offset=4 * RAW + 64, align_bytes=64)
+        fourth = late.tile([P, HALF // 2], U32, name="vw1_3", offset=4 * RAW + 64 + 2 * KB, align_bytes=64)
         nc.vector.tensor_copy(fourth[:], tabw[1][:].indirect(offsets[:, 3 * HALF // 32 : S // 16]))
 
         def picked(a, j, w):

from contextlib import ExitStack

import concourse.mybir as mybir

K, H, N, T, S = 1024, 512, 1024, 2048, 1024
FLOPS = 2 * S * (3 * K * H + H * N)

F32 = mybir.dt.float32
BF16 = mybir.dt.bfloat16
I32 = mybir.dt.int32
U32 = mybir.dt.uint32
U16 = mybir.dt.uint16
U8 = mybir.dt.uint8
FP8X4 = mybir.dt.float8_e4m3fn_x4
FP4X4 = mybir.dt.float4_e2m1fn_x4
MIN = mybir.AluOpType.min
MAX = mybir.AluOpType.max
MULT = mybir.AluOpType.mult
ADD = mybir.AluOpType.add
IDENT = mybir.ActivationFunctionType.Identity

P = 128
HALF = 512
WORDS = [(0, 256), (256, 512), (512, 768), (768, 896), (896, 1024)]
FIRST_BANK = 6
BATCHES = [256, 256, 256, 128, 128]
B_BANKS = [0, 1, 1, 2]
LATE_BANKS = [2, 3, 2, 3]
C_BANKS = [2, 3, 6, 3]
A_BANKS = [1, 0, 6, 7, 0, 6, 7, 0, 1, 6, 7, 0]
Y_BANKS = [4, 5, 2, 3]
RAW = 4 * 512 * 4
KB = 1024
WA_BF_AT = 4 * RAW + 64 + 4 * KB
HI_AT = [18 * KB, 10 * KB, 18 * KB, 10 * KB]
LO_AT = {2: 20 * KB, 3: 6 * KB, 4: 7 * KB}
H_AT = [0, 2 * KB, 4 * KB, 8 * KB, 9 * KB]


def tile_list_triplex_median_vote_kernel(
    tc, tab_words, tab_scales, offs, wa, wb_words, wb_scales, wc_words, wc_scales, we, be, out_0, out_1, out_2
):
    nc = tc.nc
    with ExitStack() as ctx:
        keep = ctx.enter_context(tc.tile_pool(name="keep", bufs=1))
        late = ctx.enter_context(tc.tile_pool(name="late", bufs=1))
        ring = ctx.enter_context(tc.tile_pool(name="ring", bufs=2))
        bnd = ctx.enter_context(tc.tile_pool(name="bnd", bufs=1))
        rnd = ctx.enter_context(tc.tile_pool(name="rnd", bufs=1))
        psum = ctx.enter_context(tc.psum_pool(name="psum", bufs=1))

        offsets = keep.tile([P, S // 16], U16, name="offsets")
        nc.sync.dma_start(offsets[:], offs)

        tsc = keep.tile([P, T], U8, name="tsc", align_bytes=64)
        nc.sync.dma_start(tsc[0:32, :].bitcast(I32), tab_scales.rearrange("a i t -> i a t").bitcast(I32))
        nc.vector.memset(tsc[32:64, :].bitcast(I32), 0)
        nc.vector.memset(tsc[64:128, :].bitcast(I32), 0)
        tabw = [keep.tile([P, T], U32, name="tabw%d" % a, tag="tabw%d" % a, align_bytes=64) for a in range(2)]
        tab_rows = tab_words.rearrange("a p t i -> a p (t i)").bitcast(I32)
        nc.sync.dma_start(tabw[0][:].bitcast(I32), tab_rows[0])
        wsr = []
        for name, scales in (("wbs_raw", wb_scales), ("wcs_raw", wc_scales)):
            raw = keep.tile([32, H], U8, name=name, align_bytes=64)
            nc.sync.dma_start(raw[:].bitcast(I32), scales.rearrange("a i e -> i a e").bitcast(I32))
            wsr.append(raw)
        planes = keep.tile([P, 2, S + 2 * H], U8, name="planes", align_bytes=64)
        nc.gpsimd.memset(planes[:].bitcast(I32), 0)

        nc.sync.dma_start(tabw[1][:].bitcast(I32), tab_rows[1])
        wc_raw = keep.tile([P, 2, H // 2], I32, name="wc_raw", tag="wc_raw", align_bytes=64)
        nc.sync.dma_start(wc_raw[:], wc_words.rearrange("a p b -> p a b").bitcast(I32))

        vsc = late.tile([P, 4 * RAW + 128], U8, name="vsc", offset=0, align_bytes=64)
        nc.vector.tensor_copy(vsc[:, 0:S], tsc[:].indirect(offsets[:]))
        staged = keep.tile([32, S + 2 * H], U8, name="staged", align_bytes=64)
        for n, raw in enumerate(wsr):
            nc.gpsimd.tensor_copy(
                staged[:, S + n * H : S + (n + 1) * H].bitcast(I32).rearrange("p (t q i) -> p q t i", t=4, i=2),
                raw[:].bitcast(I32).rearrange("p (q t i) -> p q t i", t=4, i=2),
            )
        nc.vector.tensor_copy(staged[:, 0:S].bitcast(I32), vsc[0:32, 0:S].bitcast(I32))
        for q in (0, 2, 1, 3):
            nc.sync.dma_start(planes[32 * q : 32 * q + 4, :, :].bitcast(I32), staged[8 * q : 8 * q + 8, :].bitcast(I32))

        wb_raw = [late.tile([P, H], I32, name="wb_raw%d" % a, offset=4 * RAW + 64 + 2 * KB * a, align_bytes=64) for a in range(2)]
        for a in range(2):
            nc.sync.dma_start(wb_raw[a][:], wb_words.rearrange("a p e i -> a p (e i)").bitcast(I32)[a])
        wa_raw = [late.tile([P, 4, 512], F32, name="wa_raw%d" % a, offset=a * RAW, align_bytes=64) for a in range(2)]
        we_raw = [late.tile([P, 4, 512], F32, name="we_raw%d" % g, offset=(2 + g) * RAW, align_bytes=64) for g in range(2)]
        for a in range(2):
            nc.sync.dma_start(wa_raw[a][:], wa[512 * a : 512 * (a + 1), :].rearrange("(p j) r -> p j r", j=4))
        we_rows = we.rearrange("(q s i) (g n) -> g s q i n", s=4, i=8, g=2)
        for g in range(2):
            for s in range(4):
                nc.sync.dma_start(we_raw[g][:, s, :], we_rows[g, s])
        bias = late.tile([P, 2, 4], F32, name="bias", offset=4 * RAW, align_bytes=64)
        nc.sync.dma_start(bias[:], be.rearrange("(g p t) -> p g t", p=P, t=4))

        wc_p = keep.tile([P, 2, 4, 2 * P], U8, name="wc_p", align_bytes=64)
        nc.gpsimd.tensor_copy(
            wc_p[:].bitcast(I32).rearrange("p a t (q i) -> p a q t i", i=4),
            wc_raw[:].rearrange("p a (q t i) -> p a q t i", t=4, i=4),
        )
        vw_first = keep.tile([P, S], U32, name="vw_first", align_bytes=64)
        nc.vector.tensor_copy(vw_first[:], tabw[0][:].indirect(offsets[:]))
        vw = {(0, h): vw_first[:, h * HALF : (h + 1) * HALF] for h in range(2)}
        vw[1, 0] = keep.tile([P, HALF], U32, name="vw1_0", align_bytes=64)[:]
        nc.vector.tensor_copy(vw[1, 0], tabw[1][:].indirect(offsets[:, 0 : HALF // 16]))
        third = keep.tile([P, HALF // 2], U32, name="vw1_2", align_bytes=64)
        nc.vector.tensor_copy(third[:], tabw[1][:].indirect(offsets[:, HALF // 16 : 3 * HALF // 32]))
        wb_p = [keep.tile([P, 4, P], I32, name="wb_p%d" % a, align_bytes=64) for a in range(2)]
        for a in range(2):
            (nc.scalar.copy, nc.vector.tensor_copy)[a](
                wb_p[a][:].bitcast((U32, I32)[a]).rearrange("p t (q i) -> p q t i", i=8),
                wb_raw[a][:].bitcast((U32, I32)[a]).rearrange("p (q t i) -> p q t i", t=4, i=8),
            )
        fourth = late.tile([P, HALF // 2], U32, name="vw1_3", offset=4 * RAW + 64 + 2 * KB, align_bytes=64)
        nc.vector.tensor_copy(fourth[:], tabw[1][:].indirect(offsets[:, 3 * HALF // 32 : S // 16]))

        def picked(a, j, w):
            h, c0 = divmod(j, HALF)
            if (a, h) == (1, 1):
                quarter, c0 = divmod(c0, HALF // 2)
                return (third, fourth)[quarter][:, c0 : c0 + w]
            return vw[a, h][:, c0 : c0 + w]

        def bank_tile(n):
            return psum.tile([P, 512], F32, name="bank%d" % n, tag="bank%d" % n)

        used = {"a": 0, "y": 0}

        def next_bank(kind, banks):
            used[kind] = used[kind] + 1
            return bank_tile(banks[(used[kind] - 1) % len(banks)])

        def product(out, codes, scales, j, w, passes=(0, 1)):
            for a in passes:
                nc.tensor.matmul_mx(
                    out,
                    lhsT=codes(a),
                    lhsT_scale=scales(a),
                    rhs=picked(a, j, w).bitcast(FP8X4),
                    rhs_scale=planes[:, a, j : j + w],
                    start=(a == 0),
                    stop=(a == 1),
                )

        b_sb = {}
        c_ps = {}
        lo = {0: bnd.tile([P, 4, HALF], F32, name="lo_first", offset=0)}
        hi = {0: bnd.tile([P, 4, HALF], F32, name="hi_first", offset=10 * KB)}
        c_late = {}

        copied_ps = {}

        def product_copied(n, passes):
            h, t = divmod(n, 4)
            if n not in copied_ps:
                copied_ps[n] = bank_tile(B_BANKS[n])
            product(
                copied_ps[n][:],
                lambda a: wc_p[:, a, t, :].bitcast(FP4X4),
                lambda a: planes[:, a, S + H + P * t : S + H + P * (t + 1)],
                h * HALF,
                HALF,
                passes,
            )

        def channel_b(n):
            h, t = divmod(n, 4)
            product_copied(n, (1,) if n < 2 else (0, 1))
            bank = copied_ps[n]
            b_sb[n] = keep.tile([P, HALF], F32, name="b_sb%d" % n)[:]
            nc.scalar.activation(b_sb[n], bank[:], IDENT)

        def copy_c_late(u, at):
            bank = bank_tile(LATE_BANKS[u])
            for t in range(4):
                product(
                    bank[:, t * P : (t + 1) * P],
                    lambda a: wc_p[:, a, t, :].bitcast(FP4X4),
                    lambda a: planes[:, a, S + H + P * t : S + H + P * (t + 1)],
                    HALF + u * P,
                    P,
                )
            c_late[u] = late.tile([P, 4, P], F32, name="c_late%d" % u, offset=at, align_bytes=64)
            nc.scalar.activation(c_late[u][:].rearrange("p t j -> p (t j)"), bank[:], IDENT)

        def channel_c(n):
            h, t = divmod(n, 4)
            c_ps[n] = bank_tile(C_BANKS[n % len(C_BANKS)])
            product(
                c_ps[n][:],
                lambda a: wb_p[a][:, t, :].bitcast(FP8X4),
                lambda a: planes[:, a, S + P * t : S + P * (t + 1)],
                h * HALF,
                HALF,
            )

        def bound(n, dst, op):
            h, t = divmod(n, 4)
            nc.vector.tensor_tensor(dst[h][:, t, :], b_sb[n], c_ps[n][:], op)

        def first_pair():
            w = HALF // 2
            for part, n in enumerate((C_BANKS[0], FIRST_BANK)):
                bank = bank_tile(n)[:, 0:w]
                product(
                    bank, lambda a: wb_p[a][:, 0, :].bitcast(FP8X4), lambda a: planes[:, a, S : S + P], part * w, w
                )
                cols = slice(part * w, (part + 1) * w)
                for dst, op in ((lo, MIN), (hi, MAX)):
                    nc.vector.tensor_tensor(dst[0][:, 0, cols], b_sb[0][:, cols], bank, op)

        wa_q = keep.tile([P, 2, 4, P], U32, name="wa_q", align_bytes=64)
        wa_s = keep.tile([P, 2, 4, P], U8, name="wa_s", align_bytes=64)
        wa_bf = {}

        def round_wa(a):
            wa_bf[a] = late.tile([P, 4, P, 4], BF16, name="wa_bf%d" % a, offset=WA_BF_AT + a * RAW // 2, align_bytes=64)
            for t in range(4):
                dst = wa_bf[a][:, t, :, :].rearrange("p (q i) j -> p q i j", i=8)
                src = wa_raw[a][:].rearrange("p j (q t i) -> p t q i j", t=4, i=8)[:, t]
                if t >= 2:
                    nc.gpsimd.tensor_scalar(dst.rearrange("p q i j -> p q j i"), src.rearrange("p q i j -> p q j i"), 1.0, 1.0, MULT, MULT)
                else:
                    nc.scalar.copy(
                        dst.rearrange("p q (u e) j -> p q u j e", e=2), src.rearrange("p q (u e) j -> p q u j e", e=2)
                    )

        def quantise_wa(a):
            nc.vector.quantize_mx(
                wa_q[:, a].rearrange("p t m -> p (t m)").bitcast(FP8X4),
                wa_s[:, a].rearrange("p t m -> p (t m)"),
                wa_bf[a][:].rearrange("p t m j -> p (t m j)"),
            )

        we_q = keep.tile([P, 2, 4, P], U32, name="we_q", align_bytes=64)
        we_s = keep.tile([P, 2, 4, P], U8, name="we_s", align_bytes=64)

        we_bf = {}

        def round_we(copy, g, half, at):
            we_bf[g, half] = late.tile([P, 2, P, 4], BF16, name="we_bf%d_%d" % (g, half), offset=at, align_bytes=64)
            src = we_raw[g][:].rearrange("p s (m t) -> p m s t", t=4)[:, :, :, 2 * half : 2 * half + 2]
            copy(we_bf[g, half][:].rearrange("p t m s -> p m s t"), src)

        def round_we_gpsimd(g, pool, at):
            we_bf[g, 1] = pool.tile([P, 2, P, 4], BF16, name="we_bf%d_1" % g, offset=at, align_bytes=64)
            dst = we_bf[g, 1][:].rearrange("p t m s -> p m s t")
            src = we_raw[g][:].rearrange("p s (m t) -> p m s t", t=4)[:, :, :, 2:4]
            nc.gpsimd.tensor_scalar(dst, src, 1.0, 1.0, MULT, MULT)

        def quantise_we(g, half):
            nc.vector.quantize_mx(
                we_q[:, g, 2 * half : 2 * half + 2].rearrange("p t m -> p (t m)").bitcast(FP8X4),
                we_s[:, g, 2 * half : 2 * half + 2].rearrange("p t m -> p (t m)"),
                we_bf[g, half][:].rearrange("p t m j -> p (t m j)"),
            )

        starts = [sum(BATCHES[:i]) for i in range(len(BATCHES))]
        def span(tiles, i):
            if starts[i] < HALF:
                return tiles[0][:, :, starts[i] : starts[i] + BATCHES[i]]
            return tiles[i][:]

        b_ps = {}
        hi_late = {}

        def upper(u):
            b_ps[u] = next_bank("a", A_BANKS)[:].rearrange("p (t j) -> p t j", t=4)
            for t in range(4):
                product(
                    b_ps[u][:, t, :],
                    lambda a: wb_p[a][:, t, :].bitcast(FP8X4),
                    lambda a: planes[:, a, S + P * t : S + P * (t + 1)],
                    HALF + u * P,
                    P,
                )
            hi_late[u] = bnd.tile([P, 4, P], F32, name="hi_late%d" % u, offset=HI_AT[u])
            nc.vector.tensor_tensor(hi_late[u][:], c_late[u][:], b_ps[u], MAX)

        def lower(i, u):
            c0 = HALF + u * P - starts[i]
            if c0 == 0:
                lo[i] = bnd.tile([P, 4, BATCHES[i]], F32, name="lo%d" % i, offset=LO_AT[i])
            nc.vector.tensor_tensor(lo[i][:, :, c0 : c0 + P], c_late[u][:], b_ps[u], MIN)

        def channel_a(bank, order, t0, j0, w):
            for n, (a, u) in enumerate(order):
                nc.tensor.matmul_mx(
                    bank[:, u, :],
                    lhsT=wa_q[:, a, t0 + u, :].bitcast(FP8X4),
                    lhsT_scale=wa_s[:, a, t0 + u, :],
                    rhs=picked(a, j0, w).bitcast(FP8X4),
                    rhs_scale=planes[:, a, j0 : j0 + w],
                    start=(n == 0),
                    stop=(n == len(order) - 1),
                )

        mids = {}

        def clip(i, t0, count, c0, w, bound_tile, pass_major):
            if i not in mids:
                mids[i] = ring.tile([P, 4, BATCHES[i]], F32, name="mid", tag="mid", bufs=3)
            bank = next_bank("a", A_BANKS)[:].rearrange("p (u j) -> p u j", u=count)
            order = [(a, u) for a in range(2) for u in range(count)] if pass_major else [(a, u) for u in range(count) for a in range(2)]
            channel_a(bank, order, t0, starts[i] + c0, w)
            nc.vector.tensor_tensor(mids[i][:, t0 : t0 + count, c0 : c0 + w], bound_tile, bank, MIN)

        def clip_late(i, u):
            clip(i, 0, 4, HALF + u * P - starts[i], P, hi_late[u][:], False)

        def median(i, mid, parts=1):
            w = BATCHES[i]
            h_bf = rnd.tile([P, w, 4], BF16, name="h_bf%d" % i, offset=H_AT[i], align_bytes=64)
            for c0 in range(0, w, w // parts):
                cols = slice(c0, c0 + w // parts)
                nc.vector.tensor_tensor(
                    h_bf[:, cols, :].rearrange("p (u e) t -> p u t e", e=2),
                    span(lo, i)[:, :, cols].rearrange("p t (u e) -> p u t e", e=2),
                    mid[:, :, cols].rearrange("p t (u e) -> p u t e", e=2),
                    MAX,
                )
            return h_bf

        def quantise_h(i, h_bf):
            w = BATCHES[i]
            h_q = ring.tile([P, w], U32, name="h_q", tag="h_q", align_bytes=64, bufs=3)
            h_s = ring.tile([P, w], U8, name="h_s", tag="h_s", align_bytes=64, bufs=3)
            nc.vector.quantize_mx(h_q[:].bitcast(FP8X4), h_s[:], h_bf[:].rearrange("p j t -> p (j t)"))
            return h_q, h_s

        y_s = keep.tile([P, 2, S], U8, name="y_s", align_bytes=64)
        y_rows = out_0.rearrange("(g p t) j -> g p t j", p=P, t=4)
        y_words = out_1.rearrange("g p m t -> p g (m t)").bitcast(I32)
        ys = {}
        for i, w in enumerate(BATCHES):
            for g in range(2):
                ys[i, g] = keep.tile([P, 4, w], F32, name="y%d_%d" % (i, g))[:]
        y_bf = {}

        def interleave(copy, dst, src):
            copy(dst.rearrange("p (u e) t -> p u t e", e=2), src.rearrange("p t (u e) -> p u t e", e=2))

        def pairs_out(ap):
            return ap.rearrange("p (u e) t -> p u t e", e=2)

        def pairs_in(ap):
            return ap.rearrange("p t (u e) -> p u t e", e=2)

        def gpsimd_round(dst, src):
            nc.gpsimd.tensor_scalar(pairs_out(dst), pairs_in(src), 1.0, 1.0, MULT, MULT)

        def round_y(copy, i, g):
            y_bf[i, g] = keep.tile([P, BATCHES[i], 4], BF16, name="y_bf%d_%d" % (i, g), align_bytes=64)[:]
            interleave(copy, y_bf[i, g], ys[i, g])

        def round_y_gpsimd(i, g, at):
            y_bf[i, g] = rnd.tile([P, BATCHES[i], 4], BF16, name="y_bfg%d_%d" % (i, g), offset=at, align_bytes=64)[:]
            gpsimd_round(y_bf[i, g], ys[i, g])

        def estimate(i, g, h_q, h_s):
            j0, w = starts[i], BATCHES[i]
            per_bank = 512 // w
            y = ys[i, g]
            for t0 in range(0, 4, per_bank):
                bank = next_bank("y", Y_BANKS)[:].rearrange("p (u j) -> p u j", u=per_bank)
                for u in range(per_bank):
                    nc.tensor.matmul_mx(
                        bank[:, u, :],
                        lhsT=we_q[:, g, t0 + u, :].bitcast(FP8X4),
                        lhsT_scale=we_s[:, g, t0 + u, :],
                        rhs=h_q[:].bitcast(FP8X4),
                        rhs_scale=h_s[:],
                        start=True,
                        stop=True,
                    )
                if (i, g) == (len(BATCHES) - 1, 1):
                    nc.vector.tensor_tensor(y, bank, bias[:, g, :].unsqueeze(2).broadcast_to([P, 4, w]), ADD)
                    continue
                for u in range(per_bank):
                    nc.scalar.activation(y[:, t0 + u, :], bank[:, u, :], IDENT, bias=bias[:, g, t0 + u : t0 + u + 1])
            nc.sync.dma_start(y_rows[g][:, :, j0 : j0 + w], y)

        y_q = {}

        left = {}

        def quantise_y(i, g, part=slice(None)):
            j0, w = starts[i], BATCHES[i]
            first, end = [span for span in WORDS if span[0] <= j0 < span[1]][0]
            if first not in y_q:
                y_q[first] = keep.tile([P, 2, end - first], U32, name="y_q%d" % first, align_bytes=64)
                left[first] = 2 * (end - first)
            codes = y_q[first][:, g, j0 - first : j0 - first + w][:, part]
            nc.vector.quantize_mx(
                codes.bitcast(FP8X4), y_s[:, g, j0 : j0 + w][:, part], y_bf[i, g][:, part, :].rearrange("p j t -> p (j t)")
            )
            left[first] = left[first] - codes.shape[1]
            if left[first] == 0:
                nc.sync.dma_start(y_words[:, :, first:end], y_q[first][:].bitcast(I32))

        for n in range(2):
            product_copied(n, (0,))
        for n in range(4):
            channel_b(n)
            if n == 0:
                first_pair()
            else:
                channel_c(n)
                bound(n, lo, MIN)
                bound(n, hi, MAX)
            if n in (0, 2):
                round_wa(n // 2)
        quantise_wa(0)
        quantise_wa(1)
        copy_c_late(0, 0)
        upper(0)
        round_we(nc.scalar.copy, 0, 0, RAW)
        round_we_gpsimd(0, late, WA_BF_AT + RAW // 2)
        for c0 in (0, P):
            clip(0, 0, 4, c0, P, hi[0][:, :, c0 : c0 + P], True)
        round_we(nc.scalar.copy, 1, 0, RAW + 2 * KB)
        for u in range(1, 4):
            copy_c_late(u, 2 * KB * u)
        h_mx = {}
        quantise_we(0, 0)
        h_bf = median(0, mids[0])
        quantise_we(0, 1)
        h_mx[0] = quantise_h(0, h_bf)
        round_we_gpsimd(1, late, WA_BF_AT + RAW // 2)
        estimate(0, 0, *h_mx[0])
        round_y(nc.scalar.copy, 0, 0)
        for t0 in (0, 2):
            clip(1, t0, 2, 0, 2 * P, hi[0][:, t0 : t0 + 2, 2 * P : 4 * P], False)
        lower(2, 0)
        quantise_we(1, 0)
        quantise_we(1, 1)
        estimate(0, 1, *h_mx[0])
        h_bf = median(1, mids[1])
        quantise_y(0, 0)
        h_mx[1] = quantise_h(1, h_bf)
        round_y_gpsimd(0, 1, H_AT[1])
        estimate(1, 0, *h_mx[1])
        estimate(1, 1, *h_mx[1])
        upper(1)
        lower(2, 1)
        clip_late(2, 0)
        clip_late(2, 1)
        round_y(nc.scalar.copy, 1, 1)
        h_bf = median(2, mids[2], parts=2)
        quantise_y(0, 1)
        h_mx[2] = quantise_h(2, h_bf)
        round_y_gpsimd(1, 0, H_AT[2])
        estimate(2, 0, *h_mx[2])
        estimate(2, 1, *h_mx[2])
        round_y(nc.scalar.copy, 2, 1)
        upper(2)
        lower(3, 2)
        clip_late(3, 2)
        quantise_y(1, 1)
        h_bf = median(3, mids[3])
        quantise_y(1, 0)
        round_y_gpsimd(2, 0, H_AT[2])
        h_mx[3] = quantise_h(3, h_bf)
        estimate(3, 0, *h_mx[3])
        estimate(3, 1, *h_mx[3])
        upper(3)
        lower(4, 3)
        clip_late(4, 3)
        quantise_y(2, 0)
        h_bf = median(4, mids[4])
        quantise_y(2, 1)
        h_mx[4] = quantise_h(4, h_bf)
        for g in range(2):
            round_y(nc.vector.tensor_copy, 3, g)
        for g in range(2):
            quantise_y(3, g)
        estimate(4, 0, *h_mx[4])
        estimate(4, 1, *h_mx[4])
        for g in range(2):
            round_y(nc.vector.tensor_copy, 4, g)
        for g in range(2):
            quantise_y(4, g)
        for q in range(4):
            (nc.scalar if q // 2 else nc.sync).dma_start(
                out_2[:, 4 * q : 4 * q + 4, :].rearrange("g r m -> r g m").bitcast(I32),
                y_s[32 * q : 32 * q + 4, :, :].bitcast(I32),
            )
